import numpy as np
import ml_dtypes


def mxq(x, axis, fmt="e4m3"):
    dtype, down = {"e4m3": (ml_dtypes.float8_e4m3fn, 7), "e5m2": (ml_dtypes.float8_e5m2, 14)}[fmt]
    v = np.moveaxis(np.asarray(x, np.float32).astype(ml_dtypes.bfloat16).astype(np.float64), axis, -1)
    blocks = v.reshape(v.shape[:-1] + (-1, 32))
    amax = np.abs(blocks).max(-1, keepdims=True)
    byte = np.maximum(np.where(amax > 0, np.frexp(amax)[1] - 1 + 127, 0) - down, 1)
    scale = np.exp2(byte - 127.0)
    codes = (blocks / scale).astype(np.float32).astype(dtype).astype(np.float64)
    return np.moveaxis((codes * scale).reshape(v.shape), -1, axis)


WIDE = False


def mx_kscale(k):
    if not WIDE:
        return np.ones(k)
    levels = np.array([10, -10, 5, -5, 0])
    if k % 512:
        return np.exp2(np.random.permutation(np.resize(levels, k // 32))).repeat(32)
    a = np.empty((k // 512, 16))
    for p in range(k // 512):
        a[p, :8] = np.random.permutation(np.resize(levels, 8))
        for g in range(8):
            far = levels[np.abs(levels - a[p, g]) >= 10]
            a[p, g + 8] = far[np.random.randint(len(far))]
    return np.exp2(a.ravel()).repeat(32)


BF16 = ml_dtypes.bfloat16


def bf(x):
    return np.asarray(x, np.float32).astype(BF16)


def f64(x):
    return np.asarray(x).astype(np.float64)


N, D, F, E = 4096, 1024, 512, 128


def modrelu_scale(zr, zi, b):
    m = np.sqrt(zr * zr + zi * zi + 1e-6)
    return np.maximum(m + b[None, :], 0.0) / m


def draw0():
    s, t = mx_kscale(D), mx_kscale(F)
    return {"x": bf(np.random.standard_normal((N, D)) * s),
            "wr": bf(np.random.standard_normal((D, F)) / np.sqrt(D) / s[:, None]),
            "wi": bf(np.random.standard_normal((D, F)) / np.sqrt(D) / s[:, None]),
            "b": bf(-0.5 + 0.3 * np.random.standard_normal(F)),
            "g": bf((1.0 + 0.1 * np.random.standard_normal(F)) * t),
            "vr": bf(np.random.standard_normal((F, E)) / np.sqrt(F) / t[:, None]),
            "vi": bf(np.random.standard_normal((F, E)) / np.sqrt(F) / t[:, None])}


def core(x, wr, wi, b, g, vr, vi):
    xq = mxq(f64(x), 1, "e4m3")
    zr = xq @ mxq(f64(wr), 0, "e4m3")
    zi = xq @ mxq(f64(wi), 0, "e4m3")
    sc = modrelu_scale(zr, zi, f64(b))
    gain = f64(g)[None, :]
    hr = mxq((sc * zr) * gain, 1, "e4m3")
    hi = mxq((sc * zi) * gain, 1, "e4m3")
    vrq = mxq(f64(vr), 0, "e4m3")
    viq = mxq(f64(vi), 0, "e4m3")
    yr = (hr @ vrq) - (hi @ viq)
    yi = (hr @ viq) + (hi @ vrq)
    return yr, yi


def e4m3fn_bytes(y):
    return np.clip(np.asarray(y, np.float64), -448.0, 448.0).astype(np.float32).astype(ml_dtypes.float8_e4m3fn).view(np.uint8)


def e4m3fn_values(b):
    return np.asarray(b, np.uint8).view(ml_dtypes.float8_e4m3fn).astype(np.float64)


def setup_inputs():
    d = draw0()
    x0 = np.asarray(d['x']).astype(np.float64)
    s = (np.max(np.abs(x0), axis=(0,), keepdims=True) / 448.0).astype(np.float32)
    out = {}
    for k, v in d.items():
        if k == 'x':
            out['x_bytes'] = e4m3fn_bytes(x0 / s.astype(np.float64))
            out['x_scale'] = s
        else:
            out[k] = v
    return out


def reference(x_bytes, x_scale, wr, wi, b, g, vr, vi):
    return core(e4m3fn_values(x_bytes) * x_scale.astype(np.float64), wr, wi, b, g, vr, vi)

@@ -1,0 +1,328 @@
+from contextlib import ExitStack
+
+import concourse.mybir as mybir
+from concourse.masks import make_identity
+
+N, D, F, E = 4096, 1024, 512, 128
+FLOPS = 2 * N * D * F * 2 + 2 * N * F * E * 4
+
+F32 = mybir.dt.float32
+BF16 = mybir.dt.bfloat16
+U32 = mybir.dt.uint32
+U8 = mybir.dt.uint8
+FP8 = mybir.dt.float8_e4m3fn
+FP8X4 = mybir.dt.float8_e4m3fn_x4
+ALU = mybir.AluOpType
+ACT = mybir.ActivationFunctionType
+
+P = 128
+TILES = N // P
+PAIRS = TILES // 2
+G = D // 512
+EPS = 1e-6
+
+
+def tile_complexdensemodrelupair_t_kernel(tc, x_bytes, x_scale, wr, wi, b, g, vr, vi, out_r, out_i):
+    nc = tc.nc
+    x_rows = x_bytes.rearrange("(p i) k -> p (i k)", p=P)
+    y_rows = [out_r.rearrange("(p i) e -> p i e", p=P), out_i.rearrange("(p i) e -> p i e", p=P)]
+
+    with ExitStack() as ctx:
+        keep = ctx.enter_context(tc.tile_pool(name="keep", bufs=1))
+        xin = ctx.enter_context(tc.tile_pool(name="xin", bufs=3))
+        xw = ctx.enter_context(tc.tile_pool(name="xw", bufs=3))
+        hid = ctx.enter_context(tc.tile_pool(name="hid", bufs=3))
+        outp = ctx.enter_context(tc.tile_pool(name="outp", bufs=3))
+        mix_ps = ctx.enter_context(tc.psum_pool(name="mix_ps", bufs=2))
+        z_ps = ctx.enter_context(tc.psum_pool(name="z_ps", bufs=6))
+
+        x8 = {}
+
+        def load_x(first, count):
+            name = "x8_" + str(first)
+            x8_part = keep.tile([P, count * D], U8, name=name)
+            nc.sync.dma_start(out=x8_part[:], in_=x_rows[:, first * D:(first + count) * D])
+            for i in range(count):
+                x8[first + i] = x8_part[:, i * D:(i + 1) * D]
+
+        w_raw = {}
+
+        def load_w(which, src, gg):
+            name = "w_raw_" + which + str(gg)
+            w_part = keep.tile([P, 4, F], BF16, name=name)
+            nc.sync.dma_start(out=w_part[:], in_=src[gg * 512:(gg + 1) * 512, :].rearrange("(p j) c -> p j c", j=4))
+            w_raw[which, gg] = w_part
+
+        load_x(0, 2)
+        xs = keep.tile([P, G, 4], F32)
+        nc.sync.dma_start(out=xs[:], in_=x_scale.rearrange("o (q p t) -> p (o q) t", p=P, t=4))
+        load_w("r", wr, 0)
+        load_w("r", wr, 1)
+        load_x(2, 2)
+        load_w("i", wi, 0)
+        load_w("i", wi, 1)
+        b_bf = keep.tile([P, 4], BF16)
+        nc.sync.dma_start(out=b_bf[:], in_=b.rearrange("(p t) -> p t", t=4))
+        g_bf = keep.tile([P, 4], BF16)
+        nc.sync.dma_start(out=g_bf[:], in_=g.rearrange("(p t) -> p t", t=4))
+        vr_raw = keep.tile([P, 4, E], BF16)
+        nc.sync.dma_start(out=vr_raw[:], in_=vr.rearrange("(p j) e -> p j e", j=4))
+        vi_raw = keep.tile([P, 4, E], BF16)
+        nc.sync.dma_start(out=vi_raw[:], in_=vi.rearrange("(p j) e -> p j e", j=4))
+        for first in range(4, TILES, 4):
+            load_x(first, 4)
+
+        warm = keep.tile([P, 1], F32)
+        nc.vector.memset(warm[:], 1.0)
+        nc.scalar.activation(out=warm[:], in_=warm[:], func=ACT.Abs_reciprocal_sqrt)
+        ident = keep.tile([P, P], F32)
+        make_identity(nc, ident[:])
+
+        xb = {}
+
+        def cast_x(i):
+            if i % 2 == 0:
+                xb_pair = xin.tile([P, 2 * D], BF16)
+                xb[i // 2] = xb_pair
+            nc.scalar.copy(out=xb[i // 2][:, (i % 2) * D:(i % 2 + 1) * D], in_=x8[i].bitcast(FP8))
+
+        xt = {}
+
+        def turn_x(q, gg):
+            words = xb[q][:].bitcast(F32)
+            bank = mix_ps.tile([P, 2, 256], F32, tag="mix")
+            for h in range(2):
+                for u in range(2):
+                    first = h * 512 + 256 * gg
+                    nc.tensor.transpose(bank[:, u, h * P:(h + 1) * P], words[:, first + u:first + 256:2], ident[:])
+            xt[q, gg] = bank
+
+        xg = {}
+
+        def scale_x(q, gg):
+            if gg == 0:
+                xg_pair = xw.tile([P, G, 256, 4], BF16, align_bytes=64)
+                xg[q] = xg_pair
+            nc.vector.tensor_tensor(
+                out=xg[q][:, gg, :, :].rearrange("p n (u e) -> p n u e", u=2),
+                in0=xt[q, gg][:].bitcast(BF16).rearrange("p u (n e) -> p n u e", e=2),
+                in1=xs[:, gg:gg + 1, :].to_broadcast([P, 256, 4]).rearrange("p n (u e) -> p n u e", u=2),
+                op=ALU.mult,
+            )
+
+        xc = {}
+
+        def quant_x(q):
+            x_codes = xw.tile([P, G, 256], U32, align_bytes=64)
+            x_sc = xw.tile([P, G, 256], U8, align_bytes=64)
+            nc.vector.quantize_mx(
+                out=x_codes[:].rearrange("p q n -> p (q n)").bitcast(FP8X4),
+                scales=x_sc[:].rearrange("p q n -> p (q n)"),
+                in_=xg[q][:].rearrange("p q n t -> p (q n t)"),
+            )
+            xc[q] = (x_codes, x_sc)
+
+        w_grp = {}
+        wc = {}
+
+        def group_w(which, gg, how):
+            name = "w_grp_" + which + str(gg)
+            w_grouped = keep.tile([P, 4 * F], BF16, align_bytes=64, name=name)
+            dst = w_grouped[:].rearrange("p (t m j) -> p t m j", t=4, j=4)
+            src = w_raw[which, gg][:].rearrange("p j (m t) -> p t m j", t=4)
+            for t in range(4):
+                if how == "v":
+                    nc.vector.tensor_copy(out=dst[:, t], in_=src[:, t])
+                elif how == "s":
+                    nc.scalar.copy(out=dst[:, t], in_=src[:, t])
+                else:
+                    nc.gpsimd.tensor_scalar(out=dst[:, t], in0=src[:, t], scalar1=1.0, scalar2=0.0, op0=ALU.mult, op1=ALU.add)
+            w_grp[which, gg] = w_grouped
+
+        def quant_w(which, gg):
+            w_codes = keep.tile([P, F], U32, align_bytes=64, name="w_codes_" + which + str(gg))
+            w_sc = keep.tile([P, F], U8, align_bytes=64, name="w_sc_" + which + str(gg))
+            nc.vector.quantize_mx(out=w_codes[:].bitcast(FP8X4), scales=w_sc[:], in_=w_grp[which, gg][:])
+            wc[which, gg] = (w_codes, w_sc)
+
+        z = {}
+
+        def dense_1(i, which):
+            bank = z_ps.tile([P, 4, P], F32)
+            x_codes, x_sc = xc[i // 2]
+            cols = slice((i % 2) * P, (i % 2 + 1) * P)
+            for t in range(4):
+                for gg in range(G):
+                    w_codes, w_sc = wc[which, gg]
+                    rows = slice(t * P, (t + 1) * P)
+                    nc.tensor.matmul_mx(
+                        out=bank[:, t, :],
+                        lhsT=w_codes[:, rows].bitcast(FP8X4),
+                        lhsT_scale=w_sc[:, rows],
+                        rhs=x_codes[:, gg, cols].bitcast(FP8X4),
+                        rhs_scale=x_sc[:, gg, cols],
+                        start=(gg == 0),
+                        stop=(gg == G - 1),
+                    )
+            z[i, which] = bank
+
+        sq = {}
+
+        def squares(i):
+            sq_pair = hid.tile([P, 2, 512], F32)
+            nc.scalar.activation(out=sq_pair[:, 0, :], in_=z[i, "r"][:].rearrange("p t n -> p (t n)"), func=ACT.Square)
+            nc.scalar.activation(out=sq_pair[:, 1, :], in_=z[i, "i"][:].rearrange("p t n -> p (t n)"), func=ACT.Square)
+            sq[i] = sq_pair
+
+        m2 = {}
+
+        def add_squares(i):
+            m2_tile = hid.tile([P, 512], F32)
+            nc.gpsimd.tensor_tensor(out=m2_tile[:], in0=sq[i][:, 0, :], in1=sq[i][:, 1, :], op=ALU.add)
+            m2[i] = m2_tile
+
+        rs = {}
+
+        def rsqrt(i):
+            r_tile = hid.tile([P, 4, P], F32)
+            nc.scalar.activation(out=r_tile[:].rearrange("p t n -> p (t n)"), in_=m2[i][:], func=ACT.Abs_reciprocal_sqrt, bias=EPS)
+            rs[i] = r_tile
+
+        gain = {}
+
+        def affine(i):
+            gain_tile = hid.tile([P, 4, P], F32)
+            for t in range(4):
+                nc.scalar.activation(
+                    out=gain_tile[:, t, :], in_=rs[i][:, t, :], func=ACT.Relu, scale=beta[:, t:t + 1], bias=absg[:, t:t + 1],
+                )
+            gain[i] = gain_tile
+
+        h = {}
+
+        def hidden(i):
+            h_tile = hid.tile([P, 2, P, 4], BF16, align_bytes=64)
+            for o, which in ((0, "r"), (1, "i")):
+                nc.vector.tensor_tensor(
+                    out=h_tile[:, o, :, :].rearrange("p (c k) t -> p c t k", k=4),
+                    in0=z[i, which][:].rearrange("p t (c k) -> p c t k", k=4),
+                    in1=gain[i][:].rearrange("p t (c k) -> p c t k", k=4),
+                    op=ALU.mult,
+                )
+            h[i] = h_tile
+
+        hc = {}
+
+        def quant_h(i):
+            h_codes = hid.tile([P, 2 * P], U32, align_bytes=64)
+            h_sc = hid.tile([P, 2 * P], U8, align_bytes=64)
+            nc.vector.quantize_mx(out=h_codes[:].bitcast(FP8X4), scales=h_sc[:], in_=h[i][:].rearrange("p o n t -> p (o n t)"))
+            hc[i] = (h_codes, h_sc)
+
+        y = {}
+
+        def dense_2(i):
+            if i % 2 == 0:
+                y_bank = mix_ps.tile([P, 2, 2 * E], F32, tag="mix")
+                y[i // 2] = y_bank
+            h_codes, h_sc = hc[i]
+            for o in range(2):
+                rows = slice(o * P, (o + 1) * P)
+                cols = slice((1 - o) * E, (3 - o) * E)
+                nc.tensor.matmul_mx(
+                    out=y[i // 2][:, i % 2, :],
+                    lhsT=h_codes[:, rows].bitcast(FP8X4),
+                    lhsT_scale=h_sc[:, rows],
+                    rhs=v_codes[:, cols].bitcast(FP8X4),
+                    rhs_scale=v_sc[:, cols],
+                    start=(o == 0),
+                    stop=(o == 1),
+                )
+
+        ysb = {}
+
+        def emit_y(q):
+            if q % 2 == 0:
+                y_tile = outp.tile([P, 2, 4, E], F32)
+                ysb[q // 2] = y_tile
+            half = (q % 2) * 2
+            nc.scalar.copy(
+                out=ysb[q // 2][:, :, half:half + 2, :],
+                in_=y[q][:].rearrange("p j (o e) -> p o j e", o=2),
+            )
+            if q % 2 == 1:
+                for o in range(2):
+                    nc.sync.dma_start(out=y_rows[o][:, 2 * q - 2:2 * q + 2, :], in_=ysb[q // 2][:, o, :, :])
+
+        sgn = keep.tile([P, 4], F32)
+        nsgn = keep.tile([P, 4], F32)
+        absg = keep.tile([P, 4], F32)
+        beta = keep.tile([P, 4], F32)
+        v_grp = keep.tile([P, 3, E, 4], BF16, align_bytes=64)
+        v_codes = keep.tile([P, 3 * E], U32, align_bytes=64)
+        v_sc = keep.tile([P, 3 * E], U8, align_bytes=64)
+
+        def prep_v():
+            step_g = keep.tile([P, 4], F32)
+            nc.gpsimd.tensor_scalar(out=step_g[:], in0=g_bf[:], scalar1=0.0, scalar2=2.0, op0=ALU.is_ge, op1=ALU.mult)
+            nc.gpsimd.tensor_scalar(out=sgn[:], in0=step_g[:], scalar1=1.0, scalar2=-1.0, op0=ALU.mult, op1=ALU.add)
+            nc.gpsimd.tensor_scalar(out=nsgn[:], in0=step_g[:], scalar1=-1.0, scalar2=1.0, op0=ALU.mult, op1=ALU.add)
+            nc.gpsimd.tensor_tensor(out=absg[:], in0=g_bf[:], in1=sgn[:], op=ALU.mult)
+            nc.gpsimd.tensor_tensor(out=beta[:], in0=absg[:], in1=b_bf[:], op=ALU.mult)
+            for o, raw, s in ((0, vi_raw, nsgn), (1, vr_raw, sgn), (2, vi_raw, sgn)):
+                nc.gpsimd.tensor_tensor(
+                    out=v_grp[:, o, :, :], in0=raw[:].rearrange("p j e -> p e j"),
+                    in1=s[:].unsqueeze(1).to_broadcast([P, E, 4]), op=ALU.mult,
+                )
+
+        def quant_v():
+            for o in range(3):
+                cols = slice(o * E, (o + 1) * E)
+                nc.vector.quantize_mx(
+                    out=v_codes[:, cols].bitcast(FP8X4), scales=v_sc[:, cols],
+                    in_=v_grp[:, o, :, :].rearrange("p e j -> p (e j)"),
+                )
+
+        for s in range(-6, TILES + 4):
+            if s == -4:
+                group_w("r", 0, "v")
+                quant_w("r", 0)
+                group_w("r", 1, "g")
+            if s == -2:
+                quant_w("r", 1)
+                group_w("i", 0, "g")
+                group_w("i", 1, "v")
+                prep_v()
+            if s == 0:
+                quant_w("i", 1)
+                quant_w("i", 0)
+            if s == 1:
+                quant_v()
+            if 0 <= (s + 4) // 2 < PAIRS and s % 2 == 0:
+                turn_x((s + 4) // 2, 0)
+            if 0 <= (s + 3) // 2 < PAIRS and s % 2 == 1:
+                turn_x((s + 3) // 2, 1)
+            if s % 2 == 1 and 0 <= (s + 3) // 2 < PAIRS:
+                scale_x((s + 3) // 2, 0)
+            if s % 2 == 0 and 0 <= (s + 2) // 2 < PAIRS:
+                scale_x((s + 2) // 2, 1)
+            if 0 <= s - 2 < TILES:
+                hidden(s - 2)
+            if 0 <= s - 3 < TILES:
+                quant_h(s - 3)
+            if s % 2 == 0 and 0 <= (s + 2) // 2 < PAIRS:
+                quant_x((s + 2) // 2)
+            if 0 <= s < TILES:
+                dense_1(s, "r")
+                dense_1(s, "i")
+                squares(s)
+                add_squares(s)
+            if 0 <= s - 1 < TILES:
+                rsqrt(s - 1)
+                affine(s - 1)
+            if 0 <= s + 6 < TILES:
+                cast_x(s + 6)
+            if s % 2 == 1 and 0 <= (s - 5) // 2 < PAIRS:
+                dense_2(s - 5)
+                dense_2(s - 4)
+                emit_y((s - 5) // 2)

@@ -20,6 +20,7 @@ TILES = N // P
 PAIRS = TILES // 2
 G = D // 512
 EPS = 1e-6
+WHICH = ("r", "i")
 
 
 def tile_complexdensemodrelupair_t_kernel(tc, x_bytes, x_scale, wr, wi, b, g, vr, vi, out_r, out_i):
@@ -29,12 +30,15 @@ def tile_complexdensemodrelupair_t_kernel(tc, x_bytes, x_scale, wr, wi, b, g, vr
 
     with ExitStack() as ctx:
         keep = ctx.enter_context(tc.tile_pool(name="keep", bufs=1))
-        xin = ctx.enter_context(tc.tile_pool(name="xin", bufs=3))
+        xin = ctx.enter_context(tc.tile_pool(name="xin", bufs=5))
         xw = ctx.enter_context(tc.tile_pool(name="xw", bufs=3))
+        xq = ctx.enter_context(tc.tile_pool(name="xq", bufs=10))
+        mh = ctx.enter_context(tc.tile_pool(name="mh", bufs=2))
         hid = ctx.enter_context(tc.tile_pool(name="hid", bufs=3))
         outp = ctx.enter_context(tc.tile_pool(name="outp", bufs=3))
-        mix_ps = ctx.enter_context(tc.psum_pool(name="mix_ps", bufs=2))
+        side_ps = ctx.enter_context(tc.psum_pool(name="side_ps", bufs=1))
         z_ps = ctx.enter_context(tc.psum_pool(name="z_ps", bufs=6))
+        ctx.enter_context(tc.manual_schedule())
 
         x8 = {}
 
@@ -61,6 +65,7 @@ def tile_complexdensemodrelupair_t_kernel(tc, x_bytes, x_scale, wr, wi, b, g, vr
         load_x(2, 2)
         load_w("i", wi, 0)
         load_w("i", wi, 1)
+        load_x(4, 4)
         b_bf = keep.tile([P, 4], BF16)
         nc.sync.dma_start(out=b_bf[:], in_=b.rearrange("(p t) -> p t", t=4))
         g_bf = keep.tile([P, 4], BF16)
@@ -69,7 +74,7 @@ def tile_complexdensemodrelupair_t_kernel(tc, x_bytes, x_scale, wr, wi, b, g, vr
         nc.sync.dma_start(out=vr_raw[:], in_=vr.rearrange("(p j) e -> p j e", j=4))
         vi_raw = keep.tile([P, 4, E], BF16)
         nc.sync.dma_start(out=vi_raw[:], in_=vi.rearrange("(p j) e -> p j e", j=4))
-        for first in range(4, TILES, 4):
+        for first in range(8, TILES, 4):
             load_x(first, 4)
 
         warm = keep.tile([P, 1], F32)
@@ -80,47 +85,48 @@ def tile_complexdensemodrelupair_t_kernel(tc, x_bytes, x_scale, wr, wi, b, g, vr
 
         xb = {}
 
-        def cast_x(i):
+        def cast_x(i, on_vector=False):
             if i % 2 == 0:
                 xb_pair = xin.tile([P, 2 * D], BF16)
                 xb[i // 2] = xb_pair
-            nc.scalar.copy(out=xb[i // 2][:, (i % 2) * D:(i % 2 + 1) * D], in_=x8[i].bitcast(FP8))
+            dst = xb[i // 2][:, (i % 2) * D:(i % 2 + 1) * D]
+            if on_vector:
+                nc.vector.tensor_copy(out=dst, in_=x8[i].bitcast(FP8))
+            else:
+                nc.scalar.copy(out=dst, in_=x8[i].bitcast(FP8))
 
         xt = {}
 
-        def turn_x(q, gg):
+        def turn_x(v, tag="xt"):
+            q, gg = divmod(v, G)
             words = xb[q][:].bitcast(F32)
-            bank = mix_ps.tile([P, 2, 256], F32, tag="mix")
+            bank = side_ps.tile([P, 2, 256], F32, tag=tag, name="xt_bank")
             for h in range(2):
                 for u in range(2):
                     first = h * 512 + 256 * gg
                     nc.tensor.transpose(bank[:, u, h * P:(h + 1) * P], words[:, first + u:first + 256:2], ident[:])
-            xt[q, gg] = bank
+            xt[v] = bank
 
         xg = {}
 
-        def scale_x(q, gg):
-            if gg == 0:
-                xg_pair = xw.tile([P, G, 256, 4], BF16, align_bytes=64)
-                xg[q] = xg_pair
+        def scale_x(v):
+            gg = v % G
+            xg_pass = xw.tile([P, 256, 4], BF16, align_bytes=64)
             nc.vector.tensor_tensor(
-                out=xg[q][:, gg, :, :].rearrange("p n (u e) -> p n u e", u=2),
-                in0=xt[q, gg][:].bitcast(BF16).rearrange("p u (n e) -> p n u e", e=2),
+                out=xg_pass[:].rearrange("p n (u e) -> p n u e", u=2),
+                in0=xt[v][:].bitcast(BF16).rearrange("p u (n e) -> p n u e", e=2),
                 in1=xs[:, gg:gg + 1, :].to_broadcast([P, 256, 4]).rearrange("p n (u e) -> p n u e", u=2),
                 op=ALU.mult,
             )
+            xg[v] = xg_pass
 
         xc = {}
 
-        def quant_x(q):
-            x_codes = xw.tile([P, G, 256], U32, align_bytes=64)
-            x_sc = xw.tile([P, G, 256], U8, align_bytes=64)
-            nc.vector.quantize_mx(
-                out=x_codes[:].rearrange("p q n -> p (q n)").bitcast(FP8X4),
-                scales=x_sc[:].rearrange("p q n -> p (q n)"),
-                in_=xg[q][:].rearrange("p q n t -> p (q n t)"),
-            )
-            xc[q] = (x_codes, x_sc)
+        def quant_x(v):
+            x_codes = xq.tile([P, 256], U32, align_bytes=64)
+            x_sc = xq.tile([P, 256], U8, align_bytes=64)
+            nc.vector.quantize_mx(out=x_codes[:].bitcast(FP8X4), scales=x_sc[:], in_=xg[v][:].rearrange("p n t -> p (n t)"))
+            xc[v] = (x_codes, x_sc)
 
         w_grp = {}
         wc = {}
@@ -149,18 +155,18 @@ def tile_complexdensemodrelupair_t_kernel(tc, x_bytes, x_scale, wr, wi, b, g, vr
 
         def dense_1(i, which):
             bank = z_ps.tile([P, 4, P], F32)
-            x_codes, x_sc = xc[i // 2]
             cols = slice((i % 2) * P, (i % 2 + 1) * P)
             for t in range(4):
                 for gg in range(G):
                     w_codes, w_sc = wc[which, gg]
+                    x_codes, x_sc = xc[G * (i // 2) + gg]
                     rows = slice(t * P, (t + 1) * P)
                     nc.tensor.matmul_mx(
                         out=bank[:, t, :],
                         lhsT=w_codes[:, rows].bitcast(FP8X4),
                         lhsT_scale=w_sc[:, rows],
-                        rhs=x_codes[:, gg, cols].bitcast(FP8X4),
-                        rhs_scale=x_sc[:, gg, cols],
+                        rhs=x_codes[:, cols].bitcast(FP8X4),
+                        rhs_scale=x_sc[:, cols],
                         start=(gg == 0),
                         stop=(gg == G - 1),
                     )
@@ -168,18 +174,19 @@ def tile_complexdensemodrelupair_t_kernel(tc, x_bytes, x_scale, wr, wi, b, g, vr
 
         sq = {}
 
-        def squares(i):
-            sq_pair = hid.tile([P, 2, 512], F32)
-            nc.scalar.activation(out=sq_pair[:, 0, :], in_=z[i, "r"][:].rearrange("p t n -> p (t n)"), func=ACT.Square)
-            nc.scalar.activation(out=sq_pair[:, 1, :], in_=z[i, "i"][:].rearrange("p t n -> p (t n)"), func=ACT.Square)
-            sq[i] = sq_pair
+        def square(i, o):
+            if o == 0:
+                sq_pair = hid.tile([P, 2, 512], F32)
+                sq[i] = sq_pair
+            nc.scalar.activation(out=sq[i][:, o, :], in_=z[i, WHICH[o]][:].rearrange("p t n -> p (t n)"), func=ACT.Square)
 
         m2 = {}
 
-        def add_squares(i):
-            m2_tile = hid.tile([P, 512], F32)
-            nc.gpsimd.tensor_tensor(out=m2_tile[:], in0=sq[i][:, 0, :], in1=sq[i][:, 1, :], op=ALU.add)
-            m2[i] = m2_tile
+        def add_squares(i, on_vector=False):
+            m2_then_h = mh.tile([P, 512], F32, align_bytes=64)
+            engine = nc.vector if on_vector else nc.gpsimd
+            engine.tensor_tensor(out=m2_then_h[:], in0=sq[i][:, 0, :], in1=sq[i][:, 1, :], op=ALU.add)
+            m2[i] = m2_then_h
 
         rs = {}
 
@@ -201,7 +208,7 @@ def tile_complexdensemodrelupair_t_kernel(tc, x_bytes, x_scale, wr, wi, b, g, vr
         h = {}
 
         def hidden(i):
-            h_tile = hid.tile([P, 2, P, 4], BF16, align_bytes=64)
+            h_tile = m2[i][:].bitcast(BF16).rearrange("p (o n t) -> p o n t", o=2, t=4)
             for o, which in ((0, "r"), (1, "i")):
                 nc.vector.tensor_tensor(
                     out=h_tile[:, o, :, :].rearrange("p (c k) t -> p c t k", k=4),
@@ -216,21 +223,19 @@ def tile_complexdensemodrelupair_t_kernel(tc, x_bytes, x_scale, wr, wi, b, g, vr
         def quant_h(i):
             h_codes = hid.tile([P, 2 * P], U32, align_bytes=64)
             h_sc = hid.tile([P, 2 * P], U8, align_bytes=64)
-            nc.vector.quantize_mx(out=h_codes[:].bitcast(FP8X4), scales=h_sc[:], in_=h[i][:].rearrange("p o n t -> p (o n t)"))
+            nc.vector.quantize_mx(out=h_codes[:].bitcast(FP8X4), scales=h_sc[:], in_=h[i].rearrange("p o n t -> p (o n t)"))
             hc[i] = (h_codes, h_sc)
 
         y = {}
 
         def dense_2(i):
-            if i % 2 == 0:
-                y_bank = mix_ps.tile([P, 2, 2 * E], F32, tag="mix")
-                y[i // 2] = y_bank
+            y_bank = side_ps.tile([P, 2, E], F32, tag="y")
             h_codes, h_sc = hc[i]
             for o in range(2):
                 rows = slice(o * P, (o + 1) * P)
                 cols = slice((1 - o) * E, (3 - o) * E)
                 nc.tensor.matmul_mx(
-                    out=y[i // 2][:, i % 2, :],
+                    out=y_bank[:].rearrange("p o e -> p (o e)"),
                     lhsT=h_codes[:, rows].bitcast(FP8X4),
                     lhsT_scale=h_sc[:, rows],
                     rhs=v_codes[:, cols].bitcast(FP8X4),
@@ -238,91 +243,126 @@ def tile_complexdensemodrelupair_t_kernel(tc, x_bytes, x_scale, wr, wi, b, g, vr
                     start=(o == 0),
                     stop=(o == 1),
                 )
+            y[i] = y_bank
 
         ysb = {}
 
-        def emit_y(q):
-            if q % 2 == 0:
+        def emit_y(i, on_vector):
+            if i % 4 == 0:
                 y_tile = outp.tile([P, 2, 4, E], F32)
-                ysb[q // 2] = y_tile
-            half = (q % 2) * 2
-            nc.scalar.copy(
-                out=ysb[q // 2][:, :, half:half + 2, :],
-                in_=y[q][:].rearrange("p j (o e) -> p o j e", o=2),
-            )
-            if q % 2 == 1:
+                ysb[i // 4] = y_tile
+            dst = ysb[i // 4][:, :, i % 4, :]
+            if on_vector:
+                nc.vector.tensor_copy(out=dst, in_=y[i][:])
+            else:
+                nc.scalar.copy(out=dst, in_=y[i][:])
+            if i == TILES - 1:
+                first = i
+            else:
+                first = i - i % 4
+            if i % 4 == 3 or i == TILES - 2:
                 for o in range(2):
-                    nc.sync.dma_start(out=y_rows[o][:, 2 * q - 2:2 * q + 2, :], in_=ysb[q // 2][:, o, :, :])
+                    nc.sync.dma_start(out=y_rows[o][:, first:i + 1, :], in_=ysb[i // 4][:, o, first % 4:i % 4 + 1, :])
 
         sgn = keep.tile([P, 4], F32)
-        nsgn = keep.tile([P, 4], F32)
         absg = keep.tile([P, 4], F32)
         beta = keep.tile([P, 4], F32)
         v_grp = keep.tile([P, 3, E, 4], BF16, align_bytes=64)
         v_codes = keep.tile([P, 3 * E], U32, align_bytes=64)
         v_sc = keep.tile([P, 3 * E], U8, align_bytes=64)
 
-        def prep_v():
+        def prep_gain():
             step_g = keep.tile([P, 4], F32)
             nc.gpsimd.tensor_scalar(out=step_g[:], in0=g_bf[:], scalar1=0.0, scalar2=2.0, op0=ALU.is_ge, op1=ALU.mult)
             nc.gpsimd.tensor_scalar(out=sgn[:], in0=step_g[:], scalar1=1.0, scalar2=-1.0, op0=ALU.mult, op1=ALU.add)
-            nc.gpsimd.tensor_scalar(out=nsgn[:], in0=step_g[:], scalar1=-1.0, scalar2=1.0, op0=ALU.mult, op1=ALU.add)
             nc.gpsimd.tensor_tensor(out=absg[:], in0=g_bf[:], in1=sgn[:], op=ALU.mult)
             nc.gpsimd.tensor_tensor(out=beta[:], in0=absg[:], in1=b_bf[:], op=ALU.mult)
-            for o, raw, s in ((0, vi_raw, nsgn), (1, vr_raw, sgn), (2, vi_raw, sgn)):
-                nc.gpsimd.tensor_tensor(
-                    out=v_grp[:, o, :, :], in0=raw[:].rearrange("p j e -> p e j"),
-                    in1=s[:].unsqueeze(1).to_broadcast([P, E, 4]), op=ALU.mult,
-                )
+
+        def sign_v(o, raw):
+            nc.gpsimd.tensor_tensor(
+                out=v_grp[:, o, :, :], in0=raw[:].rearrange("p j e -> p e j"),
+                in1=sgn[:].unsqueeze(1).to_broadcast([P, E, 4]), op=ALU.mult,
+            )
+
+        def negate_vi():
+            nc.vector.tensor_scalar(out=v_grp[:, 0, :, :], in0=v_grp[:, 2, :, :], scalar1=-1.0, scalar2=None, op0=ALU.mult)
 
         def quant_v():
-            for o in range(3):
-                cols = slice(o * E, (o + 1) * E)
+            for lo, hi in ((1, 3), (0, 1)):
+                cols = slice(lo * E, hi * E)
                 nc.vector.quantize_mx(
                     out=v_codes[:, cols].bitcast(FP8X4), scales=v_sc[:, cols],
-                    in_=v_grp[:, o, :, :].rearrange("p e j -> p (e j)"),
+                    in_=v_grp[:, lo:hi, :, :].rearrange("p o e j -> p (o e j)"),
                 )
 
-        for s in range(-6, TILES + 4):
-            if s == -4:
-                group_w("r", 0, "v")
-                quant_w("r", 0)
-                group_w("r", 1, "g")
-            if s == -2:
-                quant_w("r", 1)
-                group_w("i", 0, "g")
-                group_w("i", 1, "v")
-                prep_v()
-            if s == 0:
-                quant_w("i", 1)
-                quant_w("i", 0)
-            if s == 1:
-                quant_v()
-            if 0 <= (s + 4) // 2 < PAIRS and s % 2 == 0:
-                turn_x((s + 4) // 2, 0)
-            if 0 <= (s + 3) // 2 < PAIRS and s % 2 == 1:
-                turn_x((s + 3) // 2, 1)
-            if s % 2 == 1 and 0 <= (s + 3) // 2 < PAIRS:
-                scale_x((s + 3) // 2, 0)
-            if s % 2 == 0 and 0 <= (s + 2) // 2 < PAIRS:
-                scale_x((s + 2) // 2, 1)
-            if 0 <= s - 2 < TILES:
-                hidden(s - 2)
-            if 0 <= s - 3 < TILES:
-                quant_h(s - 3)
-            if s % 2 == 0 and 0 <= (s + 2) // 2 < PAIRS:
-                quant_x((s + 2) // 2)
-            if 0 <= s < TILES:
-                dense_1(s, "r")
-                dense_1(s, "i")
-                squares(s)
-                add_squares(s)
-            if 0 <= s - 1 < TILES:
+        def live(i):
+            return 0 <= i < TILES
+
+        cast_x(0)
+        cast_x(1, True)
+        turn_x(0)
+        turn_x(1, "y")
+        group_w("r", 0, "v")
+        group_w("r", 1, "s")
+        scale_x(0)
+        quant_w("r", 0)
+        scale_x(1)
+        cast_x(2)
+        cast_x(3)
+        turn_x(2)
+        turn_x(3, "y")
+        quant_x(0)
+        quant_w("r", 1)
+        quant_x(1)
+        group_w("i", 1, "s")
+        dense_1(0, "r")
+        group_w("i", 0, "v")
+        scale_x(2)
+        prep_gain()
+        quant_w("i", 0)
+        quant_w("i", 1)
+        cast_x(4)
+        cast_x(5)
+        turn_x(4)
+        dense_1(0, "i")
+        scale_x(3)
+        sign_v(1, vr_raw)
+        quant_x(2)
+        cast_x(6)
+        for s in range(0, TILES + 3):
+            if live(s + 1):
+                dense_1(s + 1, "r")
+            if live(s - 3) and (s % 2 == 0 or s > TILES - 3):
+                emit_y(s - 3, True)
+            if live(s + 3):
+                quant_x(s + 3)
+            if live(s - 2):
+                quant_h(s - 2)
+            if live(s):
+                square(s, 0)
+            if live(s - 1):
                 rsqrt(s - 1)
+            if live(s):
+                square(s, 1)
+                add_squares(s, s >= TILES - 3)
+            if live(s - 1):
                 affine(s - 1)
-            if 0 <= s + 6 < TILES:
-                cast_x(s + 6)
-            if s % 2 == 1 and 0 <= (s - 5) // 2 < PAIRS:
-                dense_2(s - 5)
-                dense_2(s - 4)
-                emit_y((s - 5) // 2)
+            if live(s - 2):
+                dense_2(s - 2)
+            if live(s + 1):
+                dense_1(s + 1, "i")
+            if live(s + 4):
+                scale_x(s + 4)
+            if s == 0:
+                sign_v(2, vi_raw)
+            if s == 1:
+                negate_vi()
+                quant_v()
+            if live(s + 5):
+                turn_x(s + 5)
+            if live(s + 7):
+                cast_x(s + 7)
+            if live(s - 2) and s % 2 == 0 and s < TILES - 3:
+                emit_y(s - 2, False)
+            if live(s - 1):
+                hidden(s - 1)

@@ -30,14 +30,15 @@ def tile_complexdensemodrelupair_t_kernel(tc, x_bytes, x_scale, wr, wi, b, g, vr
 
     with ExitStack() as ctx:
         keep = ctx.enter_context(tc.tile_pool(name="keep", bufs=1))
-        xin = ctx.enter_context(tc.tile_pool(name="xin", bufs=5))
+        xin = ctx.enter_context(tc.tile_pool(name="xin", bufs=6))
         xw = ctx.enter_context(tc.tile_pool(name="xw", bufs=3))
-        xq = ctx.enter_context(tc.tile_pool(name="xq", bufs=10))
+        xq = ctx.enter_context(tc.tile_pool(name="xq", bufs=4))
+        wgp = ctx.enter_context(tc.tile_pool(name="wgp", bufs=2))
         mh = ctx.enter_context(tc.tile_pool(name="mh", bufs=2))
         hid = ctx.enter_context(tc.tile_pool(name="hid", bufs=3))
         outp = ctx.enter_context(tc.tile_pool(name="outp", bufs=3))
         side_ps = ctx.enter_context(tc.psum_pool(name="side_ps", bufs=1))
-        z_ps = ctx.enter_context(tc.psum_pool(name="z_ps", bufs=6))
+        z_ps = ctx.enter_context(tc.psum_pool(name="z_ps", bufs=3))
         ctx.enter_context(tc.manual_schedule())
 
         x8 = {}
@@ -65,7 +66,6 @@ def tile_complexdensemodrelupair_t_kernel(tc, x_bytes, x_scale, wr, wi, b, g, vr
         load_x(2, 2)
         load_w("i", wi, 0)
         load_w("i", wi, 1)
-        load_x(4, 4)
         b_bf = keep.tile([P, 4], BF16)
         nc.sync.dma_start(out=b_bf[:], in_=b.rearrange("(p t) -> p t", t=4))
         g_bf = keep.tile([P, 4], BF16)
@@ -74,7 +74,7 @@ def tile_complexdensemodrelupair_t_kernel(tc, x_bytes, x_scale, wr, wi, b, g, vr
         nc.sync.dma_start(out=vr_raw[:], in_=vr.rearrange("(p j) e -> p j e", j=4))
         vi_raw = keep.tile([P, 4, E], BF16)
         nc.sync.dma_start(out=vi_raw[:], in_=vi.rearrange("(p j) e -> p j e", j=4))
-        for first in range(8, TILES, 4):
+        for first in range(4, TILES, 4):
             load_x(first, 4)
 
         warm = keep.tile([P, 1], F32)
@@ -85,15 +85,15 @@ def tile_complexdensemodrelupair_t_kernel(tc, x_bytes, x_scale, wr, wi, b, g, vr
 
         xb = {}
 
-        def cast_x(i, on_vector=False):
+        def cast_x(i, engine):
             if i % 2 == 0:
                 xb_pair = xin.tile([P, 2 * D], BF16)
                 xb[i // 2] = xb_pair
             dst = xb[i // 2][:, (i % 2) * D:(i % 2 + 1) * D]
-            if on_vector:
-                nc.vector.tensor_copy(out=dst, in_=x8[i].bitcast(FP8))
-            else:
+            if engine is nc.scalar:
                 nc.scalar.copy(out=dst, in_=x8[i].bitcast(FP8))
+            else:
+                engine.tensor_copy(out=dst, in_=x8[i].bitcast(FP8))
 
         xt = {}
 
@@ -110,40 +110,44 @@ def tile_complexdensemodrelupair_t_kernel(tc, x_bytes, x_scale, wr, wi, b, g, vr
         xg = {}
 
         def scale_x(v):
-            gg = v % G
-            xg_pass = xw.tile([P, 256, 4], BF16, align_bytes=64)
+            q, gg = divmod(v, G)
+            if gg == 0:
+                xg_pair = xw.tile([P, G, 256, 4], BF16, align_bytes=64)
+                xg[q] = xg_pair
             nc.vector.tensor_tensor(
-                out=xg_pass[:].rearrange("p n (u e) -> p n u e", u=2),
+                out=xg[q][:, gg, :, :].rearrange("p n (u e) -> p n u e", u=2),
                 in0=xt[v][:].bitcast(BF16).rearrange("p u (n e) -> p n u e", e=2),
                 in1=xs[:, gg:gg + 1, :].to_broadcast([P, 256, 4]).rearrange("p n (u e) -> p n u e", u=2),
                 op=ALU.mult,
             )
-            xg[v] = xg_pass
 
         xc = {}
 
-        def quant_x(v):
-            x_codes = xq.tile([P, 256], U32, align_bytes=64)
-            x_sc = xq.tile([P, 256], U8, align_bytes=64)
-            nc.vector.quantize_mx(out=x_codes[:].bitcast(FP8X4), scales=x_sc[:], in_=xg[v][:].rearrange("p n t -> p (n t)"))
-            xc[v] = (x_codes, x_sc)
+        def quant_x(q):
+            x_codes = xq.tile([P, G, 256], U32, align_bytes=64)
+            x_sc = xq.tile([P, G, 256], U8, align_bytes=64)
+            nc.vector.quantize_mx(
+                out=x_codes[:].rearrange("p q n -> p (q n)").bitcast(FP8X4),
+                scales=x_sc[:].rearrange("p q n -> p (q n)"),
+                in_=xg[q][:].rearrange("p q n t -> p (q n t)"),
+            )
+            xc[q] = (x_codes, x_sc)
 
         w_grp = {}
         wc = {}
 
-        def group_w(which, gg, how):
-            name = "w_grp_" + which + str(gg)
-            w_grouped = keep.tile([P, 4 * F], BF16, align_bytes=64, name=name)
-            dst = w_grouped[:].rearrange("p (t m j) -> p t m j", t=4, j=4)
-            src = w_raw[which, gg][:].rearrange("p j (m t) -> p t m j", t=4)
-            for t in range(4):
-                if how == "v":
-                    nc.vector.tensor_copy(out=dst[:, t], in_=src[:, t])
-                elif how == "s":
-                    nc.scalar.copy(out=dst[:, t], in_=src[:, t])
-                else:
-                    nc.gpsimd.tensor_scalar(out=dst[:, t], in0=src[:, t], scalar1=1.0, scalar2=0.0, op0=ALU.mult, op1=ALU.add)
-            w_grp[which, gg] = w_grouped
+        def group_w(which, gg, lo, hi, engine):
+            if (which, gg) not in w_grp:
+                w_grouped = wgp.tile([P, 4 * F], BF16, align_bytes=64)
+                w_grp[which, gg] = w_grouped
+            dst = w_grp[which, gg][:].rearrange("p (t m j) -> p t m j", t=4, j=4)[:, lo:hi]
+            src = w_raw[which, gg][:].rearrange("p j (m t) -> p t m j", t=4)[:, lo:hi]
+            if engine is nc.vector:
+                nc.vector.tensor_copy(out=dst, in_=src)
+            elif engine is nc.scalar:
+                nc.scalar.copy(out=dst, in_=src)
+            else:
+                nc.gpsimd.tensor_scalar(out=dst, in0=src, scalar1=1.0, scalar2=0.0, op0=ALU.mult, op1=ALU.add)
 
         def quant_w(which, gg):
             w_codes = keep.tile([P, F], U32, align_bytes=64, name="w_codes_" + which + str(gg))
@@ -154,19 +158,19 @@ def tile_complexdensemodrelupair_t_kernel(tc, x_bytes, x_scale, wr, wi, b, g, vr
         z = {}
 
         def dense_1(i, which):
-            bank = z_ps.tile([P, 4, P], F32)
+            bank = z_ps.tile([P, 4, P], F32, tag=which)
             cols = slice((i % 2) * P, (i % 2 + 1) * P)
             for t in range(4):
                 for gg in range(G):
                     w_codes, w_sc = wc[which, gg]
-                    x_codes, x_sc = xc[G * (i // 2) + gg]
+                    x_codes, x_sc = xc[i // 2]
                     rows = slice(t * P, (t + 1) * P)
                     nc.tensor.matmul_mx(
                         out=bank[:, t, :],
                         lhsT=w_codes[:, rows].bitcast(FP8X4),
                         lhsT_scale=w_sc[:, rows],
-                        rhs=x_codes[:, cols].bitcast(FP8X4),
-                        rhs_scale=x_sc[:, cols],
+                        rhs=x_codes[:, gg, cols].bitcast(FP8X4),
+                        rhs_scale=x_sc[:, gg, cols],
                         start=(gg == 0),
                         stop=(gg == G - 1),
                     )
@@ -181,18 +185,23 @@ def tile_complexdensemodrelupair_t_kernel(tc, x_bytes, x_scale, wr, wi, b, g, vr
             nc.scalar.activation(out=sq[i][:, o, :], in_=z[i, WHICH[o]][:].rearrange("p t n -> p (t n)"), func=ACT.Square)
 
         m2 = {}
+        h = {}
 
-        def add_squares(i, on_vector=False):
-            m2_then_h = mh.tile([P, 512], F32, align_bytes=64)
-            engine = nc.vector if on_vector else nc.gpsimd
-            engine.tensor_tensor(out=m2_then_h[:], in0=sq[i][:, 0, :], in1=sq[i][:, 1, :], op=ALU.add)
-            m2[i] = m2_then_h
+        def add_squares(i, engine):
+            if i % 2 == 0:
+                m2_then_h = mh.tile([P, 2, 512], F32, align_bytes=64)
+                h[i // 2] = m2_then_h[:].bitcast(BF16)
+                m2[i] = m2_then_h[:, 0, :]
+            else:
+                m2_odd = hid.tile([P, 512], F32)
+                m2[i] = m2_odd[:]
+            engine.tensor_tensor(out=m2[i], in0=sq[i][:, 0, :], in1=sq[i][:, 1, :], op=ALU.add)
 
         rs = {}
 
         def rsqrt(i):
             r_tile = hid.tile([P, 4, P], F32)
-            nc.scalar.activation(out=r_tile[:].rearrange("p t n -> p (t n)"), in_=m2[i][:], func=ACT.Abs_reciprocal_sqrt, bias=EPS)
+            nc.scalar.activation(out=r_tile[:].rearrange("p t n -> p (t n)"), in_=m2[i], func=ACT.Abs_reciprocal_sqrt, bias=EPS)
             rs[i] = r_tile
 
         gain = {}
@@ -205,64 +214,64 @@ def tile_complexdensemodrelupair_t_kernel(tc, x_bytes, x_scale, wr, wi, b, g, vr
                 )
             gain[i] = gain_tile
 
-        h = {}
-
         def hidden(i):
-            h_tile = m2[i][:].bitcast(BF16).rearrange("p (o n t) -> p o n t", o=2, t=4)
-            for o, which in ((0, "r"), (1, "i")):
+            h_tile = h[i // 2][:, i % 2, :].rearrange("p (o n t) -> p o n t", o=2, t=4)
+            for o in range(2):
                 nc.vector.tensor_tensor(
                     out=h_tile[:, o, :, :].rearrange("p (c k) t -> p c t k", k=4),
-                    in0=z[i, which][:].rearrange("p t (c k) -> p c t k", k=4),
+                    in0=z[i, WHICH[o]][:].rearrange("p t (c k) -> p c t k", k=4),
                     in1=gain[i][:].rearrange("p t (c k) -> p c t k", k=4),
                     op=ALU.mult,
                 )
-            h[i] = h_tile
 
         hc = {}
 
-        def quant_h(i):
-            h_codes = hid.tile([P, 2 * P], U32, align_bytes=64)
-            h_sc = hid.tile([P, 2 * P], U8, align_bytes=64)
-            nc.vector.quantize_mx(out=h_codes[:].bitcast(FP8X4), scales=h_sc[:], in_=h[i].rearrange("p o n t -> p (o n t)"))
-            hc[i] = (h_codes, h_sc)
+        def quant_h(first, count):
+            h_codes = hid.tile([P, 4 * P], U32, align_bytes=64)
+            h_sc = hid.tile([P, 4 * P], U8, align_bytes=64)
+            lo, hi = first % 2, first % 2 + count
+            nc.vector.quantize_mx(
+                out=h_codes[:, 0:count * 2 * P].bitcast(FP8X4), scales=h_sc[:, 0:count * 2 * P],
+                in_=h[first // 2][:, lo:hi, :].rearrange("p j c -> p (j c)"),
+            )
+            for j in range(count):
+                hc[first + j] = (h_codes[:, j * 2 * P:(j + 1) * 2 * P], h_sc[:, j * 2 * P:(j + 1) * 2 * P])
 
         y = {}
 
-        def dense_2(i):
-            y_bank = side_ps.tile([P, 2, E], F32, tag="y")
-            h_codes, h_sc = hc[i]
-            for o in range(2):
-                rows = slice(o * P, (o + 1) * P)
-                cols = slice((1 - o) * E, (3 - o) * E)
-                nc.tensor.matmul_mx(
-                    out=y_bank[:].rearrange("p o e -> p (o e)"),
-                    lhsT=h_codes[:, rows].bitcast(FP8X4),
-                    lhsT_scale=h_sc[:, rows],
-                    rhs=v_codes[:, cols].bitcast(FP8X4),
-                    rhs_scale=v_sc[:, cols],
-                    start=(o == 0),
-                    stop=(o == 1),
-                )
-            y[i] = y_bank
+        def dense_2(first, count, tag="y"):
+            y_bank = side_ps.tile([P, 2, 2 * E], F32, tag=tag)
+            for j in range(count):
+                h_codes, h_sc = hc[first + j]
+                for o in range(2):
+                    rows = slice(o * P, (o + 1) * P)
+                    cols = slice((1 - o) * E, (3 - o) * E)
+                    nc.tensor.matmul_mx(
+                        out=y_bank[:, j, :],
+                        lhsT=h_codes[:, rows].bitcast(FP8X4),
+                        lhsT_scale=h_sc[:, rows],
+                        rhs=v_codes[:, cols].bitcast(FP8X4),
+                        rhs_scale=v_sc[:, cols],
+                        start=(o == 0),
+                        stop=(o == 1),
+                    )
+                y[first + j] = y_bank[:, j, :].rearrange("p (o e) -> p o e", o=2)
 
         ysb = {}
 
-        def emit_y(i, on_vector):
-            if i % 4 == 0:
+        def emit_y(i, engine):
+            if i // 4 not in ysb:
                 y_tile = outp.tile([P, 2, 4, E], F32)
                 ysb[i // 4] = y_tile
             dst = ysb[i // 4][:, :, i % 4, :]
-            if on_vector:
-                nc.vector.tensor_copy(out=dst, in_=y[i][:])
+            if engine is nc.scalar:
+                nc.scalar.copy(out=dst, in_=y[i])
             else:
-                nc.scalar.copy(out=dst, in_=y[i][:])
-            if i == TILES - 1:
-                first = i
-            else:
-                first = i - i % 4
-            if i % 4 == 3 or i == TILES - 2:
-                for o in range(2):
-                    nc.sync.dma_start(out=y_rows[o][:, first:i + 1, :], in_=ysb[i // 4][:, o, first % 4:i % 4 + 1, :])
+                nc.vector.tensor_copy(out=dst, in_=y[i])
+
+        def store_y(first, count):
+            for o in range(2):
+                nc.sync.dma_start(out=y_rows[o][:, first:first + count, :], in_=ysb[first // 4][:, o, first % 4:first % 4 + count, :])
 
         sgn = keep.tile([P, 4], F32)
         absg = keep.tile([P, 4], F32)
@@ -272,14 +281,12 @@ def tile_complexdensemodrelupair_t_kernel(tc, x_bytes, x_scale, wr, wi, b, g, vr
         v_sc = keep.tile([P, 3 * E], U8, align_bytes=64)
 
         def prep_gain():
-            step_g = keep.tile([P, 4], F32)
-            nc.gpsimd.tensor_scalar(out=step_g[:], in0=g_bf[:], scalar1=0.0, scalar2=2.0, op0=ALU.is_ge, op1=ALU.mult)
-            nc.gpsimd.tensor_scalar(out=sgn[:], in0=step_g[:], scalar1=1.0, scalar2=-1.0, op0=ALU.mult, op1=ALU.add)
-            nc.gpsimd.tensor_tensor(out=absg[:], in0=g_bf[:], in1=sgn[:], op=ALU.mult)
-            nc.gpsimd.tensor_tensor(out=beta[:], in0=absg[:], in1=b_bf[:], op=ALU.mult)
+            nc.scalar.activation(out=sgn[:], in_=g_bf[:], func=ACT.Sign)
+            nc.scalar.activation(out=absg[:], in_=g_bf[:], func=ACT.Abs)
+            nc.vector.tensor_tensor(out=beta[:], in0=absg[:], in1=b_bf[:], op=ALU.mult)
 
-        def sign_v(o, raw):
-            nc.gpsimd.tensor_tensor(
+        def sign_v(o, raw, engine):
+            engine.tensor_tensor(
                 out=v_grp[:, o, :, :], in0=raw[:].rearrange("p j e -> p e j"),
                 in1=sgn[:].unsqueeze(1).to_broadcast([P, E, 4]), op=ALU.mult,
             )
@@ -298,71 +305,143 @@ def tile_complexdensemodrelupair_t_kernel(tc, x_bytes, x_scale, wr, wi, b, g, vr
         def live(i):
             return 0 <= i < TILES
 
-        cast_x(0)
-        cast_x(1, True)
+        cast_x(0, nc.scalar)
+        cast_x(1, nc.vector)
         turn_x(0)
         turn_x(1, "y")
-        group_w("r", 0, "v")
-        group_w("r", 1, "s")
+        group_w("r", 0, 0, 2, nc.scalar)
+        group_w("r", 0, 2, 4, nc.vector)
         scale_x(0)
-        quant_w("r", 0)
         scale_x(1)
-        cast_x(2)
-        cast_x(3)
+        group_w("r", 1, 0, 2, nc.scalar)
+        group_w("r", 1, 2, 4, nc.gpsimd)
+        cast_x(2, nc.scalar)
+        cast_x(3, nc.scalar)
         turn_x(2)
         turn_x(3, "y")
+        quant_w("r", 0)
         quant_x(0)
         quant_w("r", 1)
-        quant_x(1)
-        group_w("i", 1, "s")
+        group_w("i", 0, 0, 4, nc.scalar)
+        group_w("i", 1, 0, 2, nc.gpsimd)
+        group_w("i", 1, 2, 4, nc.scalar)
         dense_1(0, "r")
-        group_w("i", 0, "v")
+        dense_1(1, "r")
         scale_x(2)
-        prep_gain()
+        scale_x(3)
         quant_w("i", 0)
         quant_w("i", 1)
-        cast_x(4)
-        cast_x(5)
-        turn_x(4)
+        prep_gain()
+        quant_x(1)
+        cast_x(4, nc.scalar)
+        cast_x(5, nc.scalar)
         dense_1(0, "i")
-        scale_x(3)
-        sign_v(1, vr_raw)
+        turn_x(4)
+        dense_1(1, "i")
+        turn_x(5, "y")
+        square(0, 0)
+        square(0, 1)
+        square(1, 0)
+        square(1, 1)
+        sign_v(1, vr_raw, nc.vector)
+        sign_v(2, vi_raw, nc.vector)
+        add_squares(0, nc.vector)
+        scale_x(4)
+        add_squares(1, nc.gpsimd)
+        dense_1(2, "r")
+        dense_1(2, "i")
+        rsqrt(0)
+        cast_x(6, nc.scalar)
+        affine(0)
+        cast_x(7, nc.scalar)
+        scale_x(5)
+        turn_x(6)
+        negate_vi()
         quant_x(2)
-        cast_x(6)
-        for s in range(0, TILES + 3):
-            if live(s + 1):
-                dense_1(s + 1, "r")
-            if live(s - 3) and (s % 2 == 0 or s > TILES - 3):
-                emit_y(s - 3, True)
-            if live(s + 3):
-                quant_x(s + 3)
-            if live(s - 2):
-                quant_h(s - 2)
+        quant_v()
+        for q in range(1, PAIRS - 2):
+            a, c = 2 * q, 2 * q + 1
+            if live(a):
+                square(a, 0)
+                square(a, 1)
+                add_squares(a, nc.gpsimd)
+            if live(a - 2):
+                hidden(a - 2)
+            if live(a - 1):
+                rsqrt(a - 1)
+            if live(a - 4):
+                dense_2(a - 4, 2)
+            if live(a + 6):
+                cast_x(a + 6, nc.scalar)
+                cast_x(a + 7, nc.gpsimd)
+            elif live(a - 4):
+                emit_y(a - 4, nc.scalar)
+            if live(c):
+                dense_1(c, "r")
+                dense_1(c, "i")
+            if live(a + 4):
+                scale_x(a + 4)
+                turn_x(a + 5)
+            if live(a - 1):
+                affine(a - 1)
+            if live(a - 4):
+                if live(a + 6):
+                    emit_y(a - 4, nc.vector)
+            if live(c):
+                square(c, 0)
+                square(c, 1)
+                add_squares(c, nc.gpsimd)
+            if live(a - 1):
+                hidden(a - 1)
+            if live(a):
+                rsqrt(a)
+            if live(a - 3):
+                emit_y(a - 3, nc.scalar)
+                if q % 2 == 1:
+                    store_y(a - 6, 4)
+            if live(a + 2):
+                dense_1(a + 2, "r")
+                dense_1(a + 2, "i")
+            if live(a):
+                affine(a)
+            if live(a + 5):
+                scale_x(a + 5)
+            if live(a + 6):
+                turn_x(a + 6)
+            if live(a - 2):
+                quant_h(a - 2, 2)
+            if live(a + 4):
+                quant_x(q + 2)
+        first = TILES - 4
+        hidden(first - 2)
+        dense_2(first - 4, 2)
+        quant_h(first - 2, 1)
+        for s in range(first, TILES + 2):
             if live(s):
                 square(s, 0)
             if live(s - 1):
                 rsqrt(s - 1)
             if live(s):
                 square(s, 1)
-                add_squares(s, s >= TILES - 3)
-            if live(s - 1):
-                affine(s - 1)
-            if live(s - 2):
-                dense_2(s - 2)
+            if live(s + 1):
+                dense_1(s + 1, "r")
+            dense_2(s - 2, 1, ("xt", "y")[s % 2])
             if live(s + 1):
                 dense_1(s + 1, "i")
-            if live(s + 4):
-                scale_x(s + 4)
-            if s == 0:
-                sign_v(2, vi_raw)
-            if s == 1:
-                negate_vi()
-                quant_v()
-            if live(s + 5):
-                turn_x(s + 5)
-            if live(s + 7):
-                cast_x(s + 7)
-            if live(s - 2) and s % 2 == 0 and s < TILES - 3:
-                emit_y(s - 2, False)
+            if s == first:
+                emit_y(s - 4, nc.vector)
+            if live(s):
+                add_squares(s, nc.vector)
             if live(s - 1):
+                affine(s - 1)
                 hidden(s - 1)
+            if s == first:
+                emit_y(s - 3, nc.vector)
+            emit_y(s - 2, nc.vector)
+            if live(s - 1):
+                quant_h(s - 1, 1)
+            if s == first + 1:
+                store_y(first - 4, 4)
+            if s == TILES:
+                store_y(first, 3)
+        store_y(TILES - 1, 1)

@@ -218,9 +218,9 @@ def tile_complexdensemodrelupair_t_kernel(tc, x_bytes, x_scale, wr, wi, b, g, vr
             h_tile = h[i // 2][:, i % 2, :].rearrange("p (o n t) -> p o n t", o=2, t=4)
             for o in range(2):
                 nc.vector.tensor_tensor(
-                    out=h_tile[:, o, :, :].rearrange("p (c k) t -> p c t k", k=4),
-                    in0=z[i, WHICH[o]][:].rearrange("p t (c k) -> p c t k", k=4),
-                    in1=gain[i][:].rearrange("p t (c k) -> p c t k", k=4),
+                    out=h_tile[:, o, :, :].rearrange("p (c k) t -> p c t k", k=2),
+                    in0=z[i, WHICH[o]][:].rearrange("p t (c k) -> p c t k", k=2),
+                    in1=gain[i][:].rearrange("p t (c k) -> p c t k", k=2),
                     op=ALU.mult,
                 )
 

@@ -33,7 +33,7 @@ def tile_complexdensemodrelupair_t_kernel(tc, x_bytes, x_scale, wr, wi, b, g, vr
         xin = ctx.enter_context(tc.tile_pool(name="xin", bufs=6))
         xw = ctx.enter_context(tc.tile_pool(name="xw", bufs=3))
         xq = ctx.enter_context(tc.tile_pool(name="xq", bufs=4))
-        wgp = ctx.enter_context(tc.tile_pool(name="wgp", bufs=2))
+        wgp = ctx.enter_context(tc.tile_pool(name="wgp", bufs=3))
         mh = ctx.enter_context(tc.tile_pool(name="mh", bufs=2))
         hid = ctx.enter_context(tc.tile_pool(name="hid", bufs=3))
         outp = ctx.enter_context(tc.tile_pool(name="outp", bufs=3))
@@ -85,15 +85,19 @@ def tile_complexdensemodrelupair_t_kernel(tc, x_bytes, x_scale, wr, wi, b, g, vr
 
         xb = {}
 
-        def cast_x(i, engine):
-            if i % 2 == 0:
+        def cast_x(i, engine, lo=0, hi=D):
+            if i // 2 not in xb:
                 xb_pair = xin.tile([P, 2 * D], BF16)
                 xb[i // 2] = xb_pair
-            dst = xb[i // 2][:, (i % 2) * D:(i % 2 + 1) * D]
+            dst = xb[i // 2][:, (i % 2) * D + lo:(i % 2) * D + hi]
             if engine is nc.scalar:
-                nc.scalar.copy(out=dst, in_=x8[i].bitcast(FP8))
+                nc.scalar.copy(out=dst, in_=x8[i][:, lo:hi].bitcast(FP8))
             else:
-                engine.tensor_copy(out=dst, in_=x8[i].bitcast(FP8))
+                engine.tensor_copy(out=dst, in_=x8[i][:, lo:hi].bitcast(FP8))
+
+        def cast_unit(v, side, engine):
+            q, gg = divmod(v, G)
+            cast_x(2 * q + side, engine, gg * 512, (gg + 1) * 512)
 
         xt = {}
 
@@ -157,8 +161,11 @@ def tile_complexdensemodrelupair_t_kernel(tc, x_bytes, x_scale, wr, wi, b, g, vr
 
         z = {}
 
-        def dense_1(i, which):
-            bank = z_ps.tile([P, 4, P], F32, tag=which)
+        def dense_1(i, which, tag=None):
+            if tag == "xt":
+                bank = side_ps.tile([P, 4, P], F32, tag=tag, name="z_bank")
+            else:
+                bank = z_ps.tile([P, 4, P], F32, tag=tag or which)
             cols = slice((i % 2) * P, (i % 2 + 1) * P)
             for t in range(4):
                 for gg in range(G):
@@ -188,90 +195,90 @@ def tile_complexdensemodrelupair_t_kernel(tc, x_bytes, x_scale, wr, wi, b, g, vr
         h = {}
 
         def add_squares(i, engine):
-            if i % 2 == 0:
-                m2_then_h = mh.tile([P, 2, 512], F32, align_bytes=64)
-                h[i // 2] = m2_then_h[:].bitcast(BF16)
-                m2[i] = m2_then_h[:, 0, :]
-            else:
-                m2_odd = hid.tile([P, 512], F32)
-                m2[i] = m2_odd[:]
-            engine.tensor_tensor(out=m2[i], in0=sq[i][:, 0, :], in1=sq[i][:, 1, :], op=ALU.add)
+            m2_then_gain = mh.tile([P, 4, P], F32, tag="last" if i == TILES - 1 else "m2")
+            m2[i] = m2_then_gain
+            engine.tensor_tensor(out=m2[i][:].rearrange("p t n -> p (t n)"), in0=sq[i][:, 0, :], in1=sq[i][:, 1, :], op=ALU.add)
 
         rs = {}
 
         def rsqrt(i):
             r_tile = hid.tile([P, 4, P], F32)
-            nc.scalar.activation(out=r_tile[:].rearrange("p t n -> p (t n)"), in_=m2[i], func=ACT.Abs_reciprocal_sqrt, bias=EPS)
+            nc.scalar.activation(out=r_tile[:].rearrange("p t n -> p (t n)"), in_=m2[i][:].rearrange("p t n -> p (t n)"), func=ACT.Abs_reciprocal_sqrt, bias=EPS)
             rs[i] = r_tile
 
         gain = {}
 
         def affine(i):
-            gain_tile = hid.tile([P, 4, P], F32)
+            gain_tile = m2[i]
             for t in range(4):
                 nc.scalar.activation(
                     out=gain_tile[:, t, :], in_=rs[i][:, t, :], func=ACT.Relu, scale=beta[:, t:t + 1], bias=absg[:, t:t + 1],
                 )
             gain[i] = gain_tile
 
-        def hidden(i):
-            h_tile = h[i // 2][:, i % 2, :].rearrange("p (o n t) -> p o n t", o=2, t=4)
-            for o in range(2):
-                nc.vector.tensor_tensor(
-                    out=h_tile[:, o, :, :].rearrange("p (c k) t -> p c t k", k=2),
-                    in0=z[i, WHICH[o]][:].rearrange("p t (c k) -> p c t k", k=2),
-                    in1=gain[i][:].rearrange("p t (c k) -> p c t k", k=2),
-                    op=ALU.mult,
-                )
+        def hidden(i, o):
+            j, side = divmod(i + 1, 2)
+            if j not in h:
+                h_pair = hid.tile([P, 2, 8 * P], BF16, align_bytes=64)
+                h[j] = h_pair
+            h_part = h[j][:, side, o * 512:(o + 1) * 512]
+            nc.vector.tensor_tensor(
+                out=h_part.rearrange("p (c k t) -> p c t k", k=2, t=4),
+                in0=z[i, WHICH[o]][:].rearrange("p t (c k) -> p c t k", k=2),
+                in1=gain[i][:].rearrange("p t (c k) -> p c t k", k=2),
+                op=ALU.mult,
+            )
 
         hc = {}
 
         def quant_h(first, count):
             h_codes = hid.tile([P, 4 * P], U32, align_bytes=64)
             h_sc = hid.tile([P, 4 * P], U8, align_bytes=64)
-            lo, hi = first % 2, first % 2 + count
+            j, side = divmod(first + 1, 2)
             nc.vector.quantize_mx(
                 out=h_codes[:, 0:count * 2 * P].bitcast(FP8X4), scales=h_sc[:, 0:count * 2 * P],
-                in_=h[first // 2][:, lo:hi, :].rearrange("p j c -> p (j c)"),
+                in_=h[j][:, side:side + count, :].rearrange("p j c -> p (j c)"),
             )
-            for j in range(count):
-                hc[first + j] = (h_codes[:, j * 2 * P:(j + 1) * 2 * P], h_sc[:, j * 2 * P:(j + 1) * 2 * P])
+            for n in range(count):
+                hc[first + n] = (h_codes[:, n * 2 * P:(n + 1) * 2 * P], h_sc[:, n * 2 * P:(n + 1) * 2 * P])
 
         y = {}
 
-        def dense_2(first, count, tag="y"):
-            y_bank = side_ps.tile([P, 2, 2 * E], F32, tag=tag)
-            for j in range(count):
-                h_codes, h_sc = hc[first + j]
-                for o in range(2):
-                    rows = slice(o * P, (o + 1) * P)
-                    cols = slice((1 - o) * E, (3 - o) * E)
-                    nc.tensor.matmul_mx(
-                        out=y_bank[:, j, :],
-                        lhsT=h_codes[:, rows].bitcast(FP8X4),
-                        lhsT_scale=h_sc[:, rows],
-                        rhs=v_codes[:, cols].bitcast(FP8X4),
-                        rhs_scale=v_sc[:, cols],
-                        start=(o == 0),
-                        stop=(o == 1),
-                    )
-                y[first + j] = y_bank[:, j, :].rearrange("p (o e) -> p o e", o=2)
+        def dense_2(i, o, tag="y"):
+            if o == 0:
+                pool = z_ps if tag in WHICH else side_ps
+                y_bank = pool.tile([P, 2, E], F32, tag=tag)
+                y[i] = y_bank
+            h_codes, h_sc = hc[i]
+            rows = slice(o * P, (o + 1) * P)
+            cols = slice((1 - o) * E, (3 - o) * E)
+            nc.tensor.matmul_mx(
+                out=y[i][:].rearrange("p o e -> p (o e)"),
+                lhsT=h_codes[:, rows].bitcast(FP8X4),
+                lhsT_scale=h_sc[:, rows],
+                rhs=v_codes[:, cols].bitcast(FP8X4),
+                rhs_scale=v_sc[:, cols],
+                start=(o == 0),
+                stop=(o == 1),
+            )
 
         ysb = {}
 
         def emit_y(i, engine):
-            if i // 4 not in ysb:
+            group, place = divmod(i, 4)
+            if place == 0:
                 y_tile = outp.tile([P, 2, 4, E], F32)
-                ysb[i // 4] = y_tile
-            dst = ysb[i // 4][:, :, i % 4, :]
+                ysb[group] = y_tile
+            dst = ysb[group][:, :, place, :]
             if engine is nc.scalar:
-                nc.scalar.copy(out=dst, in_=y[i])
+                nc.scalar.copy(out=dst, in_=y[i][:])
             else:
-                nc.vector.tensor_copy(out=dst, in_=y[i])
+                nc.vector.tensor_copy(out=dst, in_=y[i][:])
 
         def store_y(first, count):
+            group, place = divmod(first, 4)
             for o in range(2):
-                nc.sync.dma_start(out=y_rows[o][:, first:first + count, :], in_=ysb[first // 4][:, o, first % 4:first % 4 + count, :])
+                nc.sync.dma_start(out=y_rows[o][:, first:first + count, :], in_=ysb[group][:, o, place:place + count, :])
 
         sgn = keep.tile([P, 4], F32)
         absg = keep.tile([P, 4], F32)
@@ -319,129 +326,156 @@ def tile_complexdensemodrelupair_t_kernel(tc, x_bytes, x_scale, wr, wi, b, g, vr
         cast_x(3, nc.scalar)
         turn_x(2)
         turn_x(3, "y")
-        quant_w("r", 0)
+        group_w("i", 0, 0, 4, nc.scalar)
         quant_x(0)
         quant_w("r", 1)
-        group_w("i", 0, 0, 4, nc.scalar)
+        quant_w("r", 0)
         group_w("i", 1, 0, 2, nc.gpsimd)
         group_w("i", 1, 2, 4, nc.scalar)
         dense_1(0, "r")
-        dense_1(1, "r")
         scale_x(2)
         scale_x(3)
         quant_w("i", 0)
         quant_w("i", 1)
         prep_gain()
-        quant_x(1)
         cast_x(4, nc.scalar)
-        cast_x(5, nc.scalar)
+        dense_1(1, "r")
         dense_1(0, "i")
-        turn_x(4)
         dense_1(1, "i")
+        cast_x(5, nc.scalar)
+        turn_x(4)
         turn_x(5, "y")
         square(0, 0)
+        cast_unit(6, 0, nc.scalar)
+        quant_x(1)
+        sign_v(2, vi_raw, nc.vector)
+        sign_v(1, vr_raw, nc.vector)
+        dense_1(2, "r")
         square(0, 1)
+        add_squares(0, nc.gpsimd)
+        scale_x(4)
         square(1, 0)
         square(1, 1)
-        sign_v(1, vr_raw, nc.vector)
-        sign_v(2, vi_raw, nc.vector)
-        add_squares(0, nc.vector)
-        scale_x(4)
         add_squares(1, nc.gpsimd)
-        dense_1(2, "r")
-        dense_1(2, "i")
-        rsqrt(0)
-        cast_x(6, nc.scalar)
-        affine(0)
-        cast_x(7, nc.scalar)
-        scale_x(5)
+        cast_unit(6, 1, nc.scalar)
+        cast_unit(7, 0, nc.scalar)
         turn_x(6)
+        dense_1(2, "i")
+        scale_x(5)
+        rsqrt(0)
+        cast_unit(7, 1, nc.scalar)
+        affine(0)
         negate_vi()
         quant_x(2)
         quant_v()
-        for q in range(1, PAIRS - 2):
-            a, c = 2 * q, 2 * q + 1
-            if live(a):
-                square(a, 0)
-                square(a, 1)
-                add_squares(a, nc.gpsimd)
-            if live(a - 2):
-                hidden(a - 2)
-            if live(a - 1):
-                rsqrt(a - 1)
-            if live(a - 4):
-                dense_2(a - 4, 2)
-            if live(a + 6):
-                cast_x(a + 6, nc.scalar)
-                cast_x(a + 7, nc.gpsimd)
-            elif live(a - 4):
-                emit_y(a - 4, nc.scalar)
-            if live(c):
-                dense_1(c, "r")
-                dense_1(c, "i")
-            if live(a + 4):
-                scale_x(a + 4)
-                turn_x(a + 5)
-            if live(a - 1):
-                affine(a - 1)
-            if live(a - 4):
-                if live(a + 6):
-                    emit_y(a - 4, nc.vector)
-            if live(c):
-                square(c, 0)
-                square(c, 1)
-                add_squares(c, nc.gpsimd)
-            if live(a - 1):
-                hidden(a - 1)
-            if live(a):
-                rsqrt(a)
-            if live(a - 3):
-                emit_y(a - 3, nc.scalar)
-                if q % 2 == 1:
-                    store_y(a - 6, 4)
-            if live(a + 2):
-                dense_1(a + 2, "r")
-                dense_1(a + 2, "i")
-            if live(a):
-                affine(a)
-            if live(a + 5):
-                scale_x(a + 5)
-            if live(a + 6):
-                turn_x(a + 6)
-            if live(a - 2):
-                quant_h(a - 2, 2)
-            if live(a + 4):
-                quant_x(q + 2)
-        first = TILES - 4
-        hidden(first - 2)
-        dense_2(first - 4, 2)
-        quant_h(first - 2, 1)
-        for s in range(first, TILES + 2):
+        hidden(0, 0)
+        hidden(0, 1)
+        for s in range(2, TILES - 4):
             if live(s):
                 square(s, 0)
+                square(s, 1)
+                if s < TILES - 1:
+                    add_squares(s, nc.gpsimd)
+            if live(s + 6):
+                cast_unit(s + 6, 1, nc.gpsimd)
             if live(s - 1):
                 rsqrt(s - 1)
-            if live(s):
-                square(s, 1)
+            if live(s - 5):
+                dense_2(s - 5, 1)
             if live(s + 1):
                 dense_1(s + 1, "r")
-            dense_2(s - 2, 1, ("xt", "y")[s % 2])
-            if live(s + 1):
                 dense_1(s + 1, "i")
-            if s == first:
-                emit_y(s - 4, nc.vector)
-            if live(s):
+            if live(s + 4):
+                scale_x(s + 4)
+            if s == TILES - 1:
                 add_squares(s, nc.vector)
+            if live(s + 6):
+                cast_unit(s + 6, 0, nc.scalar)
+            if live(s - 5):
+                emit_y(s - 5, nc.scalar)
+                if s % 4 == 0:
+                    store_y(s - 8, 4)
+            if live(s - 4):
+                dense_2(s - 4, 0)
+            if live(s + 5):
+                turn_x(s + 5)
             if live(s - 1):
                 affine(s - 1)
-                hidden(s - 1)
-            if s == first:
-                emit_y(s - 3, nc.vector)
-            emit_y(s - 2, nc.vector)
-            if live(s - 1):
-                quant_h(s - 1, 1)
-            if s == first + 1:
-                store_y(first - 4, 4)
-            if s == TILES:
-                store_y(first, 3)
-        store_y(TILES - 1, 1)
+                hidden(s - 1, 0)
+                hidden(s - 1, 1)
+            if s % 2 == 1 and live(s + 3):
+                quant_x((s + 3) // 2)
+            elif s == 2:
+                quant_h(0, 1)
+            elif s % 2 == 0:
+                quant_h(s - 3, 2)
+        ta, tb, te, td = TILES - 4, TILES - 3, TILES - 2, TILES - 1
+
+        def finish(i, tag="y"):
+            dense_2(i, 0, tag)
+            dense_2(i, 1, tag)
+
+        def both_hidden(i):
+            hidden(i, 0)
+            hidden(i, 1)
+
+        dense_2(ta - 5, 1)
+        dense_1(tb, "r", "xt")
+        square(ta, 0)
+        square(ta, 1)
+        add_squares(ta, nc.vector)
+        rsqrt(ta - 1)
+        dense_1(tb, "i")
+        dense_1(te, "r")
+        square(tb, 0)
+        quant_h(ta - 3, 2)
+        affine(ta - 1)
+        both_hidden(ta - 1)
+        emit_y(ta - 5, nc.vector)
+        store_y(ta - 8, 4)
+        dense_1(te, "i", "r")
+        dense_1(td, "r", "i")
+        finish(ta - 4)
+        square(tb, 1)
+        add_squares(tb, nc.vector)
+        rsqrt(ta)
+        square(te, 0)
+        affine(ta)
+        both_hidden(ta)
+        emit_y(ta - 4, nc.vector)
+        dense_1(td, "i", "r")
+        finish(ta - 3)
+        finish(ta - 2, "i")
+        square(te, 1)
+        add_squares(te, nc.vector)
+        rsqrt(tb)
+        square(td, 0)
+        affine(tb)
+        square(td, 1)
+        both_hidden(tb)
+        add_squares(td, nc.vector)
+        quant_h(ta - 1, 2)
+        rsqrt(te)
+        emit_y(ta - 3, nc.scalar)
+        finish(ta - 1, "xt")
+        finish(ta, "i")
+        affine(te)
+        rsqrt(td)
+        emit_y(ta - 2, nc.scalar)
+        affine(td)
+        both_hidden(te)
+        quant_h(tb, 1)
+        finish(tb)
+        emit_y(ta - 1, nc.scalar)
+        store_y(ta - 4, 4)
+        emit_y(ta, nc.scalar)
+        both_hidden(td)
+        quant_h(te, 1)
+        finish(te, "r")
+        quant_h(td, 1)
+        finish(td, "r")
+        emit_y(tb, nc.scalar)
+        store_y(ta, 2)
+        emit_y(te, nc.scalar)
+        emit_y(td, nc.vector)
+        store_y(te, 2)

@@ -20,6 +20,7 @@ TILES = N // P
 PAIRS = TILES // 2
 G = D // 512
 EPS = 1e-6
+S_COLS = 384
 WHICH = ("r", "i")
 
 
@@ -320,8 +321,8 @@ def tile_complexdensemodrelupair_t_kernel(tc, x_bytes, x_scale, wr, wi, b, g, vr
         group_w("r", 0, 2, 4, nc.vector)
         scale_x(0)
         scale_x(1)
-        group_w("r", 1, 0, 2, nc.scalar)
-        group_w("r", 1, 2, 4, nc.gpsimd)
+        group_w("r", 1, 0, 1, nc.scalar)
+        group_w("r", 1, 1, 4, nc.gpsimd)
         cast_x(2, nc.scalar)
         cast_x(3, nc.scalar)
         turn_x(2)
@@ -330,8 +331,8 @@ def tile_complexdensemodrelupair_t_kernel(tc, x_bytes, x_scale, wr, wi, b, g, vr
         quant_x(0)
         quant_w("r", 1)
         quant_w("r", 0)
-        group_w("i", 1, 0, 2, nc.gpsimd)
-        group_w("i", 1, 2, 4, nc.scalar)
+        group_w("i", 1, 0, 3, nc.gpsimd)
+        group_w("i", 1, 3, 4, nc.scalar)
         dense_1(0, "r")
         scale_x(2)
         scale_x(3)
@@ -346,7 +347,8 @@ def tile_complexdensemodrelupair_t_kernel(tc, x_bytes, x_scale, wr, wi, b, g, vr
         turn_x(4)
         turn_x(5, "y")
         square(0, 0)
-        cast_unit(6, 0, nc.scalar)
+        cast_x(6, nc.scalar)
+        cast_x(7, nc.scalar)
         quant_x(1)
         sign_v(2, vi_raw, nc.vector)
         sign_v(1, vr_raw, nc.vector)
@@ -357,13 +359,12 @@ def tile_complexdensemodrelupair_t_kernel(tc, x_bytes, x_scale, wr, wi, b, g, vr
         square(1, 0)
         square(1, 1)
         add_squares(1, nc.gpsimd)
-        cast_unit(6, 1, nc.scalar)
-        cast_unit(7, 0, nc.scalar)
+        cast_x(8, nc.scalar, 0, D // 2)
         turn_x(6)
         dense_1(2, "i")
         scale_x(5)
         rsqrt(0)
-        cast_unit(7, 1, nc.scalar)
+        cast_x(8, nc.scalar, D // 2, D)
         affine(0)
         negate_vi()
         quant_x(2)
@@ -376,12 +377,10 @@ def tile_complexdensemodrelupair_t_kernel(tc, x_bytes, x_scale, wr, wi, b, g, vr
                 square(s, 1)
                 if s < TILES - 1:
                     add_squares(s, nc.gpsimd)
-            if live(s + 6):
-                cast_unit(s + 6, 1, nc.gpsimd)
+            if live(s + 7):
+                cast_x(s + 7, nc.gpsimd, S_COLS, D)
             if live(s - 1):
                 rsqrt(s - 1)
-            if live(s - 5):
-                dense_2(s - 5, 1)
             if live(s + 1):
                 dense_1(s + 1, "r")
                 dense_1(s + 1, "i")
@@ -389,14 +388,15 @@ def tile_complexdensemodrelupair_t_kernel(tc, x_bytes, x_scale, wr, wi, b, g, vr
                 scale_x(s + 4)
             if s == TILES - 1:
                 add_squares(s, nc.vector)
-            if live(s + 6):
-                cast_unit(s + 6, 0, nc.scalar)
+            if live(s + 7):
+                cast_x(s + 7, nc.scalar, 0, S_COLS)
             if live(s - 5):
                 emit_y(s - 5, nc.scalar)
                 if s % 4 == 0:
                     store_y(s - 8, 4)
             if live(s - 4):
                 dense_2(s - 4, 0)
+                dense_2(s - 4, 1)
             if live(s + 5):
                 turn_x(s + 5)
             if live(s - 1):
@@ -419,7 +419,6 @@ def tile_complexdensemodrelupair_t_kernel(tc, x_bytes, x_scale, wr, wi, b, g, vr
             hidden(i, 0)
             hidden(i, 1)
 
-        dense_2(ta - 5, 1)
         dense_1(tb, "r", "xt")
         square(ta, 0)
         square(ta, 1)

@@ -43,6 +43,7 @@ def tile_complexdensemodrelupair_t_kernel(tc, x_bytes, x_scale, wr, wi, b, g, vr
         ctx.enter_context(tc.manual_schedule())
 
         x8 = {}
+        x8_first = []
 
         def load_x(first, count):
             name = "x8_" + str(first)
@@ -59,7 +60,11 @@ def tile_complexdensemodrelupair_t_kernel(tc, x_bytes, x_scale, wr, wi, b, g, vr
             nc.sync.dma_start(out=w_part[:], in_=src[gg * 512:(gg + 1) * 512, :].rearrange("(p j) c -> p j c", j=4))
             w_raw[which, gg] = w_part
 
-        load_x(0, 2)
+        first_pair = x_rows[:, 0:2 * D].rearrange("p (h c) -> p h c", h=2)
+        for gg in range(G):
+            x8_half = keep.tile([P, 2, 512], U8, name="x8_first_" + str(gg))
+            nc.sync.dma_start(out=x8_half[:], in_=first_pair[:, :, gg * 512:(gg + 1) * 512])
+            x8_first.append(x8_half)
         xs = keep.tile([P, G, 4], F32)
         nc.sync.dma_start(out=xs[:], in_=x_scale.rearrange("o (q p t) -> p (o q) t", p=P, t=4))
         load_w("r", wr, 0)
@@ -99,6 +104,13 @@ def tile_complexdensemodrelupair_t_kernel(tc, x_bytes, x_scale, wr, wi, b, g, vr
         def cast_unit(v, side, engine):
             q, gg = divmod(v, G)
             cast_x(2 * q + side, engine, gg * 512, (gg + 1) * 512)
+
+        def cast_first(gg):
+            if gg == 0:
+                xb_pair = xin.tile([P, 2 * D], BF16)
+                xb[0] = xb_pair
+            nc.scalar.copy(out=xb[0][:, gg * 512:(gg + 1) * 512], in_=x8_first[gg][:, 0, :].bitcast(FP8))
+            nc.vector.tensor_copy(out=xb[0][:, D + gg * 512:D + (gg + 1) * 512], in_=x8_first[gg][:, 1, :].bitcast(FP8))
 
         xt = {}
 
@@ -145,8 +157,8 @@ def tile_complexdensemodrelupair_t_kernel(tc, x_bytes, x_scale, wr, wi, b, g, vr
             if (which, gg) not in w_grp:
                 w_grouped = wgp.tile([P, 4 * F], BF16, align_bytes=64)
                 w_grp[which, gg] = w_grouped
-            dst = w_grp[which, gg][:].rearrange("p (t m j) -> p t m j", t=4, j=4)[:, lo:hi]
-            src = w_raw[which, gg][:].rearrange("p j (m t) -> p t m j", t=4)[:, lo:hi]
+            dst = w_grp[which, gg][:].rearrange("p (t m j) -> p m t j", t=4, j=4)[:, 32 * lo:32 * hi]
+            src = w_raw[which, gg][:].rearrange("p j (m t) -> p m t j", t=4)[:, 32 * lo:32 * hi]
             if engine is nc.vector:
                 nc.vector.tensor_copy(out=dst, in_=src)
             elif engine is nc.scalar:
@@ -313,9 +325,9 @@ def tile_complexdensemodrelupair_t_kernel(tc, x_bytes, x_scale, wr, wi, b, g, vr
         def live(i):
             return 0 <= i < TILES
 
-        cast_x(0, nc.scalar)
-        cast_x(1, nc.vector)
+        cast_first(0)
         turn_x(0)
+        cast_first(1)
         turn_x(1, "y")
         group_w("r", 0, 0, 2, nc.scalar)
         group_w("r", 0, 2, 4, nc.vector)

@@ -20,7 +20,7 @@ TILES = N // P
 PAIRS = TILES // 2
 G = D // 512
 EPS = 1e-6
-S_COLS = 384
+S_COLS = 352
 WHICH = ("r", "i")
 
 
@@ -34,7 +34,7 @@ def tile_complexdensemodrelupair_t_kernel(tc, x_bytes, x_scale, wr, wi, b, g, vr
         xin = ctx.enter_context(tc.tile_pool(name="xin", bufs=6))
         xw = ctx.enter_context(tc.tile_pool(name="xw", bufs=3))
         xq = ctx.enter_context(tc.tile_pool(name="xq", bufs=4))
-        wgp = ctx.enter_context(tc.tile_pool(name="wgp", bufs=3))
+        wgp = ctx.enter_context(tc.tile_pool(name="wgp", bufs=1))
         mh = ctx.enter_context(tc.tile_pool(name="mh", bufs=2))
         hid = ctx.enter_context(tc.tile_pool(name="hid", bufs=3))
         outp = ctx.enter_context(tc.tile_pool(name="outp", bufs=3))
@@ -155,10 +155,10 @@ def tile_complexdensemodrelupair_t_kernel(tc, x_bytes, x_scale, wr, wi, b, g, vr
 
         def group_w(which, gg, lo, hi, engine):
             if (which, gg) not in w_grp:
-                w_grouped = wgp.tile([P, 4 * F], BF16, align_bytes=64)
+                w_grouped = wgp.tile([P, 4 * F], BF16, align_bytes=64, tag="second" if gg == 1 else which)
                 w_grp[which, gg] = w_grouped
-            dst = w_grp[which, gg][:].rearrange("p (t m j) -> p m t j", t=4, j=4)[:, 32 * lo:32 * hi]
-            src = w_raw[which, gg][:].rearrange("p j (m t) -> p m t j", t=4)[:, 32 * lo:32 * hi]
+            dst = w_grp[which, gg][:].rearrange("p (t m j) -> p m t j", t=4, j=4)[:, lo:hi]
+            src = w_raw[which, gg][:].rearrange("p j (m t) -> p m t j", t=4)[:, lo:hi]
             if engine is nc.vector:
                 nc.vector.tensor_copy(out=dst, in_=src)
             elif engine is nc.scalar:
@@ -329,22 +329,22 @@ def tile_complexdensemodrelupair_t_kernel(tc, x_bytes, x_scale, wr, wi, b, g, vr
         turn_x(0)
         cast_first(1)
         turn_x(1, "y")
-        group_w("r", 0, 0, 2, nc.scalar)
-        group_w("r", 0, 2, 4, nc.vector)
+        group_w("r", 0, 0, 64, nc.scalar)
+        group_w("r", 0, 64, 128, nc.vector)
         scale_x(0)
         scale_x(1)
-        group_w("r", 1, 0, 1, nc.scalar)
-        group_w("r", 1, 1, 4, nc.gpsimd)
+        group_w("r", 1, 0, 32, nc.scalar)
+        group_w("r", 1, 32, 128, nc.gpsimd)
         cast_x(2, nc.scalar)
         cast_x(3, nc.scalar)
         turn_x(2)
         turn_x(3, "y")
-        group_w("i", 0, 0, 4, nc.scalar)
+        group_w("i", 0, 0, 128, nc.scalar)
+        quant_w("r", 0)
         quant_x(0)
         quant_w("r", 1)
-        quant_w("r", 0)
-        group_w("i", 1, 0, 3, nc.gpsimd)
-        group_w("i", 1, 3, 4, nc.scalar)
+        group_w("i", 1, 0, 80, nc.gpsimd)
+        group_w("i", 1, 80, 128, nc.scalar)
         dense_1(0, "r")
         scale_x(2)
         scale_x(3)
@@ -354,9 +354,9 @@ def tile_complexdensemodrelupair_t_kernel(tc, x_bytes, x_scale, wr, wi, b, g, vr
         cast_x(4, nc.scalar)
         dense_1(1, "r")
         dense_1(0, "i")
-        dense_1(1, "i")
         cast_x(5, nc.scalar)
         turn_x(4)
+        dense_1(1, "i")
         turn_x(5, "y")
         square(0, 0)
         cast_x(6, nc.scalar)
@@ -379,18 +379,19 @@ def tile_complexdensemodrelupair_t_kernel(tc, x_bytes, x_scale, wr, wi, b, g, vr
         cast_x(8, nc.scalar, D // 2, D)
         affine(0)
         negate_vi()
-        quant_x(2)
         quant_v()
         hidden(0, 0)
         hidden(0, 1)
+        quant_x(2)
         for s in range(2, TILES - 4):
+            s_cols = S_COLS if live(s - 5) else D // 2
             if live(s):
                 square(s, 0)
                 square(s, 1)
                 if s < TILES - 1:
                     add_squares(s, nc.gpsimd)
             if live(s + 7):
-                cast_x(s + 7, nc.gpsimd, S_COLS, D)
+                cast_x(s + 7, nc.gpsimd, s_cols, D)
             if live(s - 1):
                 rsqrt(s - 1)
             if live(s + 1):
@@ -401,7 +402,7 @@ def tile_complexdensemodrelupair_t_kernel(tc, x_bytes, x_scale, wr, wi, b, g, vr
             if s == TILES - 1:
                 add_squares(s, nc.vector)
             if live(s + 7):
-                cast_x(s + 7, nc.scalar, 0, S_COLS)
+                cast_x(s + 7, nc.scalar, 0, s_cols)
             if live(s - 5):
                 emit_y(s - 5, nc.scalar)
                 if s % 4 == 0:

@@ -20,7 +20,7 @@ TILES = N // P
 PAIRS = TILES // 2
 G = D // 512
 EPS = 1e-6
-S_COLS = 352
+S_COLS = 320
 WHICH = ("r", "i")
 
 

@@ -16,12 +16,15 @@ ALU = mybir.AluOpType
 ACT = mybir.ActivationFunctionType
 
 P = 128
+K_PASS = 4 * P
+PASSES = D // K_PASS
 TILES = N // P
-PAIRS = TILES // 2
-G = D // 512
+GROUPS = F // 4
 EPS = 1e-6
-S_COLS = 320
-WHICH = ("r", "i")
+SIGN_OF_ZERO = 1e-38
+PARTS = ("r", "i")
+SCALAR_COLS = 320
+GPSIMD_GROUPS = {"r": 96, "i": 80}
 
 
 def tile_complexdensemodrelupair_t_kernel(tc, x_bytes, x_scale, wr, wi, b, g, vr, vi, out_r, out_i):
@@ -54,18 +57,18 @@ def tile_complexdensemodrelupair_t_kernel(tc, x_bytes, x_scale, wr, wi, b, g, vr
 
         w_raw = {}
 
-        def load_w(which, src, gg):
-            name = "w_raw_" + which + str(gg)
-            w_part = keep.tile([P, 4, F], BF16, name=name)
-            nc.sync.dma_start(out=w_part[:], in_=src[gg * 512:(gg + 1) * 512, :].rearrange("(p j) c -> p j c", j=4))
-            w_raw[which, gg] = w_part
+        def load_w(part, src, kp):
+            name = "w_raw_" + part + str(kp)
+            w_rows = keep.tile([P, 4, F], BF16, name=name)
+            nc.sync.dma_start(out=w_rows[:], in_=src[kp * K_PASS:(kp + 1) * K_PASS, :].rearrange("(p j) c -> p j c", j=4))
+            w_raw[part, kp] = w_rows
 
         first_pair = x_rows[:, 0:2 * D].rearrange("p (h c) -> p h c", h=2)
-        for gg in range(G):
-            x8_half = keep.tile([P, 2, 512], U8, name="x8_first_" + str(gg))
-            nc.sync.dma_start(out=x8_half[:], in_=first_pair[:, :, gg * 512:(gg + 1) * 512])
+        for kp in range(PASSES):
+            x8_half = keep.tile([P, 2, K_PASS], U8, name="x8_first_" + str(kp))
+            nc.sync.dma_start(out=x8_half[:], in_=first_pair[:, :, kp * K_PASS:(kp + 1) * K_PASS])
             x8_first.append(x8_half)
-        xs = keep.tile([P, G, 4], F32)
+        xs = keep.tile([P, PASSES, 4], F32)
         nc.sync.dma_start(out=xs[:], in_=x_scale.rearrange("o (q p t) -> p (o q) t", p=P, t=4))
         load_w("r", wr, 0)
         load_w("r", wr, 1)
@@ -91,7 +94,7 @@ def tile_complexdensemodrelupair_t_kernel(tc, x_bytes, x_scale, wr, wi, b, g, vr
 
         xb = {}
 
-        def cast_x(i, engine, lo=0, hi=D):
+        def widen_x(i, engine, lo=0, hi=D):
             if i // 2 not in xb:
                 xb_pair = xin.tile([P, 2 * D], BF16)
                 xb[i // 2] = xb_pair
@@ -99,66 +102,65 @@ def tile_complexdensemodrelupair_t_kernel(tc, x_bytes, x_scale, wr, wi, b, g, vr
             if engine is nc.scalar:
                 nc.scalar.copy(out=dst, in_=x8[i][:, lo:hi].bitcast(FP8))
             else:
-                engine.tensor_copy(out=dst, in_=x8[i][:, lo:hi].bitcast(FP8))
+                nc.gpsimd.tensor_copy(out=dst, in_=x8[i][:, lo:hi].bitcast(FP8))
 
-        def cast_unit(v, side, engine):
-            q, gg = divmod(v, G)
-            cast_x(2 * q + side, engine, gg * 512, (gg + 1) * 512)
-
-        def cast_first(gg):
-            if gg == 0:
+        def widen_first_pair(kp):
+            if kp == 0:
                 xb_pair = xin.tile([P, 2 * D], BF16)
                 xb[0] = xb_pair
-            nc.scalar.copy(out=xb[0][:, gg * 512:(gg + 1) * 512], in_=x8_first[gg][:, 0, :].bitcast(FP8))
-            nc.vector.tensor_copy(out=xb[0][:, D + gg * 512:D + (gg + 1) * 512], in_=x8_first[gg][:, 1, :].bitcast(FP8))
+            lo, hi = kp * K_PASS, (kp + 1) * K_PASS
+            nc.scalar.copy(out=xb[0][:, lo:hi], in_=x8_first[kp][:, 0, :].bitcast(FP8))
+            nc.vector.tensor_copy(out=xb[0][:, D + lo:D + hi], in_=x8_first[kp][:, 1, :].bitcast(FP8))
 
         xt = {}
 
         def turn_x(v, tag="xt"):
-            q, gg = divmod(v, G)
-            words = xb[q][:].bitcast(F32)
-            bank = side_ps.tile([P, 2, 256], F32, tag=tag, name="xt_bank")
-            for h in range(2):
+            pair, kp = divmod(v, PASSES)
+            words = xb[pair][:].bitcast(F32)
+            bank = side_ps.tile([P, 2, 2 * P], F32, tag=tag, name="xt_bank")
+            for side in range(2):
                 for u in range(2):
-                    first = h * 512 + 256 * gg
-                    nc.tensor.transpose(bank[:, u, h * P:(h + 1) * P], words[:, first + u:first + 256:2], ident[:])
+                    first = (side * D + kp * K_PASS) // 2
+                    nc.tensor.transpose(
+                        bank[:, u, side * P:(side + 1) * P], words[:, first + u:first + K_PASS // 2:2], ident[:],
+                    )
             xt[v] = bank
 
         xg = {}
 
         def scale_x(v):
-            q, gg = divmod(v, G)
-            if gg == 0:
-                xg_pair = xw.tile([P, G, 256, 4], BF16, align_bytes=64)
-                xg[q] = xg_pair
+            pair, kp = divmod(v, PASSES)
+            if kp == 0:
+                xg_pair = xw.tile([P, PASSES, 2 * P, 4], BF16, align_bytes=64)
+                xg[pair] = xg_pair
             nc.vector.tensor_tensor(
-                out=xg[q][:, gg, :, :].rearrange("p n (u e) -> p n u e", u=2),
+                out=xg[pair][:, kp, :, :].rearrange("p n (u e) -> p n u e", u=2),
                 in0=xt[v][:].bitcast(BF16).rearrange("p u (n e) -> p n u e", e=2),
-                in1=xs[:, gg:gg + 1, :].to_broadcast([P, 256, 4]).rearrange("p n (u e) -> p n u e", u=2),
+                in1=xs[:, kp:kp + 1, :].to_broadcast([P, 2 * P, 4]).rearrange("p n (u e) -> p n u e", u=2),
                 op=ALU.mult,
             )
 
         xc = {}
 
-        def quant_x(q):
-            x_codes = xq.tile([P, G, 256], U32, align_bytes=64)
-            x_sc = xq.tile([P, G, 256], U8, align_bytes=64)
+        def quant_x(pair):
+            x_codes = xq.tile([P, PASSES, 2 * P], U32, align_bytes=64)
+            x_sc = xq.tile([P, PASSES, 2 * P], U8, align_bytes=64)
             nc.vector.quantize_mx(
                 out=x_codes[:].rearrange("p q n -> p (q n)").bitcast(FP8X4),
                 scales=x_sc[:].rearrange("p q n -> p (q n)"),
-                in_=xg[q][:].rearrange("p q n t -> p (q n t)"),
+                in_=xg[pair][:].rearrange("p q n t -> p (q n t)"),
             )
-            xc[q] = (x_codes, x_sc)
+            xc[pair] = (x_codes, x_sc)
 
         w_grp = {}
         wc = {}
 
-        def group_w(which, gg, lo, hi, engine):
-            if (which, gg) not in w_grp:
-                w_grouped = wgp.tile([P, 4 * F], BF16, align_bytes=64, tag="second" if gg == 1 else which)
-                w_grp[which, gg] = w_grouped
-            dst = w_grp[which, gg][:].rearrange("p (t m j) -> p m t j", t=4, j=4)[:, lo:hi]
-            src = w_raw[which, gg][:].rearrange("p j (m t) -> p m t j", t=4)[:, lo:hi]
+        def group_w(part, kp, lo, hi, engine):
+            if (part, kp) not in w_grp:
+                w_grouped = wgp.tile([P, 4 * F], BF16, align_bytes=64, tag="second" if kp == 1 else part)
+                w_grp[part, kp] = w_grouped
+            dst = w_grp[part, kp][:].rearrange("p (t m j) -> p m t j", t=4, j=4)[:, lo:hi]
+            src = w_raw[part, kp][:].rearrange("p j (m t) -> p m t j", t=4)[:, lo:hi]
             if engine is nc.vector:
                 nc.vector.tensor_copy(out=dst, in_=src)
             elif engine is nc.scalar:
@@ -166,81 +168,81 @@ def tile_complexdensemodrelupair_t_kernel(tc, x_bytes, x_scale, wr, wi, b, g, vr
             else:
                 nc.gpsimd.tensor_scalar(out=dst, in0=src, scalar1=1.0, scalar2=0.0, op0=ALU.mult, op1=ALU.add)
 
-        def quant_w(which, gg):
-            w_codes = keep.tile([P, F], U32, align_bytes=64, name="w_codes_" + which + str(gg))
-            w_sc = keep.tile([P, F], U8, align_bytes=64, name="w_sc_" + which + str(gg))
-            nc.vector.quantize_mx(out=w_codes[:].bitcast(FP8X4), scales=w_sc[:], in_=w_grp[which, gg][:])
-            wc[which, gg] = (w_codes, w_sc)
+        def quant_w(part, kp):
+            w_codes = keep.tile([P, F], U32, align_bytes=64, name="w_codes_" + part + str(kp))
+            w_sc = keep.tile([P, F], U8, align_bytes=64, name="w_sc_" + part + str(kp))
+            nc.vector.quantize_mx(out=w_codes[:].bitcast(FP8X4), scales=w_sc[:], in_=w_grp[part, kp][:])
+            wc[part, kp] = (w_codes, w_sc)
 
         z = {}
 
-        def dense_1(i, which, tag=None):
+        def dense_1(i, part, tag=None):
             if tag == "xt":
                 bank = side_ps.tile([P, 4, P], F32, tag=tag, name="z_bank")
             else:
-                bank = z_ps.tile([P, 4, P], F32, tag=tag or which)
-            cols = slice((i % 2) * P, (i % 2 + 1) * P)
+                bank = z_ps.tile([P, 4, P], F32, tag=tag or part)
+            tokens = slice((i % 2) * P, (i % 2 + 1) * P)
             for t in range(4):
-                for gg in range(G):
-                    w_codes, w_sc = wc[which, gg]
+                for kp in range(PASSES):
+                    w_codes, w_sc = wc[part, kp]
                     x_codes, x_sc = xc[i // 2]
-                    rows = slice(t * P, (t + 1) * P)
+                    channels = slice(t * P, (t + 1) * P)
                     nc.tensor.matmul_mx(
                         out=bank[:, t, :],
-                        lhsT=w_codes[:, rows].bitcast(FP8X4),
-                        lhsT_scale=w_sc[:, rows],
-                        rhs=x_codes[:, gg, cols].bitcast(FP8X4),
-                        rhs_scale=x_sc[:, gg, cols],
-                        start=(gg == 0),
-                        stop=(gg == G - 1),
+                        lhsT=w_codes[:, channels].bitcast(FP8X4),
+                        lhsT_scale=w_sc[:, channels],
+                        rhs=x_codes[:, kp, tokens].bitcast(FP8X4),
+                        rhs_scale=x_sc[:, kp, tokens],
+                        start=(kp == 0),
+                        stop=(kp == PASSES - 1),
                     )
-            z[i, which] = bank
+            z[i, part] = bank
 
         sq = {}
 
         def square(i, o):
             if o == 0:
-                sq_pair = hid.tile([P, 2, 512], F32)
+                sq_pair = hid.tile([P, 2, F], F32)
                 sq[i] = sq_pair
-            nc.scalar.activation(out=sq[i][:, o, :], in_=z[i, WHICH[o]][:].rearrange("p t n -> p (t n)"), func=ACT.Square)
+            nc.scalar.activation(out=sq[i][:, o, :], in_=z[i, PARTS[o]][:].rearrange("p t n -> p (t n)"), func=ACT.Square)
 
-        m2 = {}
-        h = {}
+        mg = {}
 
         def add_squares(i, engine):
             m2_then_gain = mh.tile([P, 4, P], F32, tag="last" if i == TILES - 1 else "m2")
-            m2[i] = m2_then_gain
-            engine.tensor_tensor(out=m2[i][:].rearrange("p t n -> p (t n)"), in0=sq[i][:, 0, :], in1=sq[i][:, 1, :], op=ALU.add)
+            mg[i] = m2_then_gain
+            engine.tensor_tensor(out=mg[i][:].rearrange("p t n -> p (t n)"), in0=sq[i][:, 0, :], in1=sq[i][:, 1, :], op=ALU.add)
 
-        rs = {}
+        inv_m = {}
 
-        def rsqrt(i):
+        def inverse_root(i):
             r_tile = hid.tile([P, 4, P], F32)
-            nc.scalar.activation(out=r_tile[:].rearrange("p t n -> p (t n)"), in_=m2[i][:].rearrange("p t n -> p (t n)"), func=ACT.Abs_reciprocal_sqrt, bias=EPS)
-            rs[i] = r_tile
+            nc.scalar.activation(
+                out=r_tile[:].rearrange("p t n -> p (t n)"), in_=mg[i][:].rearrange("p t n -> p (t n)"),
+                func=ACT.Abs_reciprocal_sqrt, bias=EPS,
+            )
+            inv_m[i] = r_tile
 
-        gain = {}
-
-        def affine(i):
-            gain_tile = m2[i]
+        def gain(i):
             for t in range(4):
                 nc.scalar.activation(
-                    out=gain_tile[:, t, :], in_=rs[i][:, t, :], func=ACT.Relu, scale=beta[:, t:t + 1], bias=absg[:, t:t + 1],
+                    out=mg[i][:, t, :], in_=inv_m[i][:, t, :], func=ACT.Relu, scale=beta[:, t:t + 1], bias=absg[:, t:t + 1],
                 )
-            gain[i] = gain_tile
 
-        def hidden(i, o):
+        h = {}
+
+        def hidden(i):
             j, side = divmod(i + 1, 2)
             if j not in h:
-                h_pair = hid.tile([P, 2, 8 * P], BF16, align_bytes=64)
+                h_pair = hid.tile([P, 2, 2 * F], BF16, align_bytes=64)
                 h[j] = h_pair
-            h_part = h[j][:, side, o * 512:(o + 1) * 512]
-            nc.vector.tensor_tensor(
-                out=h_part.rearrange("p (c k t) -> p c t k", k=2, t=4),
-                in0=z[i, WHICH[o]][:].rearrange("p t (c k) -> p c t k", k=2),
-                in1=gain[i][:].rearrange("p t (c k) -> p c t k", k=2),
-                op=ALU.mult,
-            )
+            for o in range(2):
+                nc.vector.tensor_tensor(
+                    out=h[j][:, side, o * F:(o + 1) * F].rearrange("p (c k t) -> p c t k", k=2, t=4),
+                    in0=z[i, PARTS[o]][:].rearrange("p t (c k) -> p c t k", k=2),
+                    in1=mg[i][:].rearrange("p t (c k) -> p c t k", k=2),
+                    op=ALU.mult,
+                )
 
         hc = {}
 
@@ -257,23 +259,23 @@ def tile_complexdensemodrelupair_t_kernel(tc, x_bytes, x_scale, wr, wi, b, g, vr
 
         y = {}
 
-        def dense_2(i, o, tag="y"):
-            if o == 0:
-                pool = z_ps if tag in WHICH else side_ps
-                y_bank = pool.tile([P, 2, E], F32, tag=tag)
-                y[i] = y_bank
+        def dense_2(i, tag="y"):
+            pool = z_ps if tag in PARTS else side_ps
+            y_bank = pool.tile([P, 2, E], F32, tag=tag)
             h_codes, h_sc = hc[i]
-            rows = slice(o * P, (o + 1) * P)
-            cols = slice((1 - o) * E, (3 - o) * E)
-            nc.tensor.matmul_mx(
-                out=y[i][:].rearrange("p o e -> p (o e)"),
-                lhsT=h_codes[:, rows].bitcast(FP8X4),
-                lhsT_scale=h_sc[:, rows],
-                rhs=v_codes[:, cols].bitcast(FP8X4),
-                rhs_scale=v_sc[:, cols],
-                start=(o == 0),
-                stop=(o == 1),
-            )
+            for o in range(2):
+                tokens = slice(o * P, (o + 1) * P)
+                cols = slice((1 - o) * E, (3 - o) * E)
+                nc.tensor.matmul_mx(
+                    out=y_bank[:].rearrange("p o e -> p (o e)"),
+                    lhsT=h_codes[:, tokens].bitcast(FP8X4),
+                    lhsT_scale=h_sc[:, tokens],
+                    rhs=v_codes[:, cols].bitcast(FP8X4),
+                    rhs_scale=v_sc[:, cols],
+                    start=(o == 0),
+                    stop=(o == 1),
+                )
+            y[i] = y_bank
 
         ysb = {}
 
@@ -301,20 +303,18 @@ def tile_complexdensemodrelupair_t_kernel(tc, x_bytes, x_scale, wr, wi, b, g, vr
         v_sc = keep.tile([P, 3 * E], U8, align_bytes=64)
 
         def prep_gain():
-            nc.scalar.activation(out=sgn[:], in_=g_bf[:], func=ACT.Sign)
+            nc.scalar.activation(out=sgn[:], in_=g_bf[:], func=ACT.Sign, bias=SIGN_OF_ZERO)
             nc.scalar.activation(out=absg[:], in_=g_bf[:], func=ACT.Abs)
             nc.vector.tensor_tensor(out=beta[:], in0=absg[:], in1=b_bf[:], op=ALU.mult)
 
-        def sign_v(o, raw, engine):
-            engine.tensor_tensor(
-                out=v_grp[:, o, :, :], in0=raw[:].rearrange("p j e -> p e j"),
+        def sign_v(slot, raw):
+            nc.vector.tensor_tensor(
+                out=v_grp[:, slot, :, :], in0=raw[:].rearrange("p j e -> p e j"),
                 in1=sgn[:].unsqueeze(1).to_broadcast([P, E, 4]), op=ALU.mult,
             )
 
-        def negate_vi():
-            nc.vector.tensor_scalar(out=v_grp[:, 0, :, :], in0=v_grp[:, 2, :, :], scalar1=-1.0, scalar2=None, op0=ALU.mult)
-
         def quant_v():
+            nc.vector.tensor_scalar(out=v_grp[:, 0, :, :], in0=v_grp[:, 2, :, :], scalar1=-1.0, scalar2=None, op0=ALU.mult)
             for lo, hi in ((1, 3), (0, 1)):
                 cols = slice(lo * E, hi * E)
                 nc.vector.quantize_mx(
@@ -322,48 +322,45 @@ def tile_complexdensemodrelupair_t_kernel(tc, x_bytes, x_scale, wr, wi, b, g, vr
                     in_=v_grp[:, lo:hi, :, :].rearrange("p o e j -> p (o e j)"),
                 )
 
-        def live(i):
-            return 0 <= i < TILES
-
-        cast_first(0)
+        widen_first_pair(0)
         turn_x(0)
-        cast_first(1)
+        widen_first_pair(1)
         turn_x(1, "y")
-        group_w("r", 0, 0, 64, nc.scalar)
-        group_w("r", 0, 64, 128, nc.vector)
+        group_w("r", 0, 0, GROUPS // 2, nc.scalar)
+        group_w("r", 0, GROUPS // 2, GROUPS, nc.vector)
         scale_x(0)
         scale_x(1)
-        group_w("r", 1, 0, 32, nc.scalar)
-        group_w("r", 1, 32, 128, nc.gpsimd)
-        cast_x(2, nc.scalar)
-        cast_x(3, nc.scalar)
+        group_w("r", 1, 0, GROUPS - GPSIMD_GROUPS["r"], nc.scalar)
+        group_w("r", 1, GROUPS - GPSIMD_GROUPS["r"], GROUPS, nc.gpsimd)
+        widen_x(2, nc.scalar)
+        widen_x(3, nc.scalar)
         turn_x(2)
         turn_x(3, "y")
-        group_w("i", 0, 0, 128, nc.scalar)
+        group_w("i", 0, 0, GROUPS, nc.scalar)
         quant_w("r", 0)
         quant_x(0)
         quant_w("r", 1)
-        group_w("i", 1, 0, 80, nc.gpsimd)
-        group_w("i", 1, 80, 128, nc.scalar)
+        group_w("i", 1, 0, GPSIMD_GROUPS["i"], nc.gpsimd)
+        group_w("i", 1, GPSIMD_GROUPS["i"], GROUPS, nc.scalar)
         dense_1(0, "r")
         scale_x(2)
         scale_x(3)
         quant_w("i", 0)
         quant_w("i", 1)
         prep_gain()
-        cast_x(4, nc.scalar)
+        widen_x(4, nc.scalar)
         dense_1(1, "r")
         dense_1(0, "i")
-        cast_x(5, nc.scalar)
+        widen_x(5, nc.scalar)
         turn_x(4)
         dense_1(1, "i")
         turn_x(5, "y")
         square(0, 0)
-        cast_x(6, nc.scalar)
-        cast_x(7, nc.scalar)
+        widen_x(6, nc.scalar)
+        widen_x(7, nc.scalar)
         quant_x(1)
-        sign_v(2, vi_raw, nc.vector)
-        sign_v(1, vr_raw, nc.vector)
+        sign_v(2, vi_raw)
+        sign_v(1, vr_raw)
         dense_1(2, "r")
         square(0, 1)
         add_squares(0, nc.gpsimd)
@@ -371,121 +368,105 @@ def tile_complexdensemodrelupair_t_kernel(tc, x_bytes, x_scale, wr, wi, b, g, vr
         square(1, 0)
         square(1, 1)
         add_squares(1, nc.gpsimd)
-        cast_x(8, nc.scalar, 0, D // 2)
+        widen_x(8, nc.scalar, 0, D // 2)
         turn_x(6)
         dense_1(2, "i")
         scale_x(5)
-        rsqrt(0)
-        cast_x(8, nc.scalar, D // 2, D)
-        affine(0)
-        negate_vi()
+        inverse_root(0)
+        widen_x(8, nc.scalar, D // 2, D)
+        gain(0)
         quant_v()
-        hidden(0, 0)
-        hidden(0, 1)
+        hidden(0)
         quant_x(2)
-        for s in range(2, TILES - 4):
-            s_cols = S_COLS if live(s - 5) else D // 2
-            if live(s):
-                square(s, 0)
-                square(s, 1)
-                if s < TILES - 1:
-                    add_squares(s, nc.gpsimd)
-            if live(s + 7):
-                cast_x(s + 7, nc.gpsimd, s_cols, D)
-            if live(s - 1):
-                rsqrt(s - 1)
-            if live(s + 1):
-                dense_1(s + 1, "r")
-                dense_1(s + 1, "i")
-            if live(s + 4):
-                scale_x(s + 4)
-            if s == TILES - 1:
-                add_squares(s, nc.vector)
-            if live(s + 7):
-                cast_x(s + 7, nc.scalar, 0, s_cols)
-            if live(s - 5):
+
+        last_four = TILES - 4
+        for s in range(2, last_four):
+            has_y = s >= 5
+            widens = s + 7 < TILES
+            scalar_cols = SCALAR_COLS if has_y else D // 2
+            square(s, 0)
+            square(s, 1)
+            add_squares(s, nc.gpsimd)
+            if widens:
+                widen_x(s + 7, nc.gpsimd, scalar_cols, D)
+            inverse_root(s - 1)
+            dense_1(s + 1, "r")
+            dense_1(s + 1, "i")
+            scale_x(s + 4)
+            if widens:
+                widen_x(s + 7, nc.scalar, 0, scalar_cols)
+            if has_y:
                 emit_y(s - 5, nc.scalar)
                 if s % 4 == 0:
                     store_y(s - 8, 4)
-            if live(s - 4):
-                dense_2(s - 4, 0)
-                dense_2(s - 4, 1)
-            if live(s + 5):
+            if s >= 4:
+                dense_2(s - 4)
+            if s + 5 < TILES:
                 turn_x(s + 5)
-            if live(s - 1):
-                affine(s - 1)
-                hidden(s - 1, 0)
-                hidden(s - 1, 1)
-            if s % 2 == 1 and live(s + 3):
+            gain(s - 1)
+            hidden(s - 1)
+            if s % 2 == 1:
                 quant_x((s + 3) // 2)
             elif s == 2:
                 quant_h(0, 1)
-            elif s % 2 == 0:
+            else:
                 quant_h(s - 3, 2)
-        ta, tb, te, td = TILES - 4, TILES - 3, TILES - 2, TILES - 1
 
-        def finish(i, tag="y"):
-            dense_2(i, 0, tag)
-            dense_2(i, 1, tag)
-
-        def both_hidden(i):
-            hidden(i, 0)
-            hidden(i, 1)
-
+        ta, tb, te, td = last_four, last_four + 1, last_four + 2, last_four + 3
         dense_1(tb, "r", "xt")
         square(ta, 0)
         square(ta, 1)
         add_squares(ta, nc.vector)
-        rsqrt(ta - 1)
+        inverse_root(ta - 1)
         dense_1(tb, "i")
         dense_1(te, "r")
         square(tb, 0)
         quant_h(ta - 3, 2)
-        affine(ta - 1)
-        both_hidden(ta - 1)
+        gain(ta - 1)
+        hidden(ta - 1)
         emit_y(ta - 5, nc.vector)
         store_y(ta - 8, 4)
         dense_1(te, "i", "r")
         dense_1(td, "r", "i")
-        finish(ta - 4)
+        dense_2(ta - 4)
         square(tb, 1)
         add_squares(tb, nc.vector)
-        rsqrt(ta)
+        inverse_root(ta)
         square(te, 0)
-        affine(ta)
-        both_hidden(ta)
+        gain(ta)
+        hidden(ta)
         emit_y(ta - 4, nc.vector)
         dense_1(td, "i", "r")
-        finish(ta - 3)
-        finish(ta - 2, "i")
+        dense_2(ta - 3)
+        dense_2(ta - 2, "i")
         square(te, 1)
         add_squares(te, nc.vector)
-        rsqrt(tb)
+        inverse_root(tb)
         square(td, 0)
-        affine(tb)
+        gain(tb)
         square(td, 1)
-        both_hidden(tb)
+        hidden(tb)
         add_squares(td, nc.vector)
         quant_h(ta - 1, 2)
-        rsqrt(te)
+        inverse_root(te)
         emit_y(ta - 3, nc.scalar)
-        finish(ta - 1, "xt")
-        finish(ta, "i")
-        affine(te)
-        rsqrt(td)
+        dense_2(ta - 1, "xt")
+        dense_2(ta, "i")
+        gain(te)
+        inverse_root(td)
         emit_y(ta - 2, nc.scalar)
-        affine(td)
-        both_hidden(te)
+        gain(td)
+        hidden(te)
         quant_h(tb, 1)
-        finish(tb)
+        dense_2(tb)
         emit_y(ta - 1, nc.scalar)
         store_y(ta - 4, 4)
         emit_y(ta, nc.scalar)
-        both_hidden(td)
+        hidden(td)
         quant_h(te, 1)
-        finish(te, "r")
+        dense_2(te, "r")
         quant_h(td, 1)
-        finish(td, "r")
+        dense_2(td, "r")
         emit_y(tb, nc.scalar)
         store_y(ta, 2)
         emit_y(te, nc.scalar)

@@ -23,7 +23,8 @@ GROUPS = F // 4
 EPS = 1e-6
 SIGN_OF_ZERO = 1e-38
 PARTS = ("r", "i")
-SCALAR_COLS = 320
+SCALAR_COLS = 224
+GPSIMD_COLS = 640
 GPSIMD_GROUPS = {"r": 96, "i": 80}
 
 
@@ -34,7 +35,6 @@ def tile_complexdensemodrelupair_t_kernel(tc, x_bytes, x_scale, wr, wi, b, g, vr
 
     with ExitStack() as ctx:
         keep = ctx.enter_context(tc.tile_pool(name="keep", bufs=1))
-        xin = ctx.enter_context(tc.tile_pool(name="xin", bufs=6))
         xw = ctx.enter_context(tc.tile_pool(name="xw", bufs=3))
         xq = ctx.enter_context(tc.tile_pool(name="xq", bufs=4))
         wgp = ctx.enter_context(tc.tile_pool(name="wgp", bufs=1))
@@ -45,15 +45,11 @@ def tile_complexdensemodrelupair_t_kernel(tc, x_bytes, x_scale, wr, wi, b, g, vr
         z_ps = ctx.enter_context(tc.psum_pool(name="z_ps", bufs=3))
         ctx.enter_context(tc.manual_schedule())
 
-        x8 = {}
-        x8_first = []
+        x8 = keep.tile([P, TILES * D], U8, name="x8")
 
         def load_x(first, count):
-            name = "x8_" + str(first)
-            x8_part = keep.tile([P, count * D], U8, name=name)
-            nc.sync.dma_start(out=x8_part[:], in_=x_rows[:, first * D:(first + count) * D])
-            for i in range(count):
-                x8[first + i] = x8_part[:, i * D:(i + 1) * D]
+            cols = slice(first * D, (first + count) * D)
+            nc.sync.dma_start(out=x8[:, cols], in_=x_rows[:, cols])
 
         w_raw = {}
 
@@ -63,18 +59,17 @@ def tile_complexdensemodrelupair_t_kernel(tc, x_bytes, x_scale, wr, wi, b, g, vr
             nc.sync.dma_start(out=w_rows[:], in_=src[kp * K_PASS:(kp + 1) * K_PASS, :].rearrange("(p j) c -> p j c", j=4))
             w_raw[part, kp] = w_rows
 
-        first_pair = x_rows[:, 0:2 * D].rearrange("p (h c) -> p h c", h=2)
-        for kp in range(PASSES):
-            x8_half = keep.tile([P, 2, K_PASS], U8, name="x8_first_" + str(kp))
-            nc.sync.dma_start(out=x8_half[:], in_=first_pair[:, :, kp * K_PASS:(kp + 1) * K_PASS])
-            x8_first.append(x8_half)
+        load_x(0, 1)
+        load_x(1, 1)
         xs = keep.tile([P, PASSES, 4], F32)
         nc.sync.dma_start(out=xs[:], in_=x_scale.rearrange("o (q p t) -> p (o q) t", p=P, t=4))
+        load_x(2, 2)
         load_w("r", wr, 0)
         load_w("r", wr, 1)
-        load_x(2, 2)
+        load_x(4, 2)
         load_w("i", wi, 0)
         load_w("i", wi, 1)
+        load_x(6, 2)
         b_bf = keep.tile([P, 4], BF16)
         nc.sync.dma_start(out=b_bf[:], in_=b.rearrange("(p t) -> p t", t=4))
         g_bf = keep.tile([P, 4], BF16)
@@ -83,7 +78,7 @@ def tile_complexdensemodrelupair_t_kernel(tc, x_bytes, x_scale, wr, wi, b, g, vr
         nc.sync.dma_start(out=vr_raw[:], in_=vr.rearrange("(p j) e -> p j e", j=4))
         vi_raw = keep.tile([P, 4, E], BF16)
         nc.sync.dma_start(out=vi_raw[:], in_=vi.rearrange("(p j) e -> p j e", j=4))
-        for first in range(4, TILES, 4):
+        for first in range(8, TILES, 4):
             load_x(first, 4)
 
         warm = keep.tile([P, 1], F32)
@@ -91,73 +86,69 @@ def tile_complexdensemodrelupair_t_kernel(tc, x_bytes, x_scale, wr, wi, b, g, vr
         nc.scalar.activation(out=warm[:], in_=warm[:], func=ACT.Abs_reciprocal_sqrt)
         ident = keep.tile([P, P], F32)
         make_identity(nc, ident[:])
+        ident_bf = keep.tile([P, P], BF16)
+        nc.vector.tensor_copy(out=ident_bf[:], in_=ident[:])
 
-        xb = {}
+        xb = keep.tile([P, TILES * D], BF16)
+        widened = [0]
 
-        def widen_x(i, engine, lo=0, hi=D):
-            if i // 2 not in xb:
-                xb_pair = xin.tile([P, 2 * D], BF16)
-                xb[i // 2] = xb_pair
-            dst = xb[i // 2][:, (i % 2) * D + lo:(i % 2) * D + hi]
+        def widen_x(count, engine):
+            cols = slice(widened[0], min(widened[0] + count, TILES * D))
+            widened.append(cols.stop)
+            widened.remove(cols.start)
+            if cols.start == cols.stop:
+                return
             if engine is nc.scalar:
-                nc.scalar.copy(out=dst, in_=x8[i][:, lo:hi].bitcast(FP8))
+                nc.scalar.copy(out=xb[:, cols], in_=x8[:, cols].bitcast(FP8))
             else:
-                nc.gpsimd.tensor_copy(out=dst, in_=x8[i][:, lo:hi].bitcast(FP8))
-
-        def widen_first_pair(kp):
-            if kp == 0:
-                xb_pair = xin.tile([P, 2 * D], BF16)
-                xb[0] = xb_pair
-            lo, hi = kp * K_PASS, (kp + 1) * K_PASS
-            nc.scalar.copy(out=xb[0][:, lo:hi], in_=x8_first[kp][:, 0, :].bitcast(FP8))
-            nc.vector.tensor_copy(out=xb[0][:, D + lo:D + hi], in_=x8_first[kp][:, 1, :].bitcast(FP8))
+                engine.tensor_copy(out=xb[:, cols], in_=x8[:, cols].bitcast(FP8))
 
         xt = {}
 
-        def turn_x(v, tag="xt"):
-            pair, kp = divmod(v, PASSES)
-            words = xb[pair][:].bitcast(F32)
-            bank = side_ps.tile([P, 2, 2 * P], F32, tag=tag, name="xt_bank")
-            for side in range(2):
+        def turn_x(i, tag="xt"):
+            assert widened[0] >= (i + 1) * D
+            words = xb[:].bitcast(F32)
+            pool = z_ps if tag in PARTS else side_ps
+            bank = pool.tile([P, 2, PASSES, P], F32, tag=tag, name="xt_bank")
+            for kp in range(PASSES):
                 for u in range(2):
-                    first = (side * D + kp * K_PASS) // 2
-                    nc.tensor.transpose(
-                        bank[:, u, side * P:(side + 1) * P], words[:, first + u:first + K_PASS // 2:2], ident[:],
-                    )
-            xt[v] = bank
+                    first = (i * D + kp * K_PASS) // 2
+                    nc.tensor.transpose(bank[:, u, kp, :], words[:, first + u:first + K_PASS // 2:2], ident[:])
+            xt[i] = bank
 
         xg = {}
 
-        def scale_x(v):
-            pair, kp = divmod(v, PASSES)
-            if kp == 0:
-                xg_pair = xw.tile([P, PASSES, 2 * P, 4], BF16, align_bytes=64)
+        def scale_x(i):
+            pair, side = divmod(i, 2)
+            if side == 0:
+                xg_pair = xw.tile([P, 2, PASSES, P, 4], BF16, align_bytes=64)
                 xg[pair] = xg_pair
             nc.vector.tensor_tensor(
-                out=xg[pair][:, kp, :, :].rearrange("p n (u e) -> p n u e", u=2),
-                in0=xt[v][:].bitcast(BF16).rearrange("p u (n e) -> p n u e", e=2),
-                in1=xs[:, kp:kp + 1, :].to_broadcast([P, 2 * P, 4]).rearrange("p n (u e) -> p n u e", u=2),
+                out=xg[pair][:, side].rearrange("p q n (u e) -> p q n u e", u=2),
+                in0=xt[i][:].rearrange("p u q n -> p (u q n)").bitcast(BF16).rearrange("p (u q n e) -> p q n u e", u=2, q=PASSES, e=2),
+                in1=xs[:].unsqueeze(2).to_broadcast([P, PASSES, P, 4]).rearrange("p q n (u e) -> p q n u e", u=2),
                 op=ALU.mult,
             )
 
         xc = {}
 
         def quant_x(pair):
-            x_codes = xq.tile([P, PASSES, 2 * P], U32, align_bytes=64)
-            x_sc = xq.tile([P, PASSES, 2 * P], U8, align_bytes=64)
+            x_codes = xq.tile([P, 2, PASSES, P], U32, align_bytes=64)
+            x_sc = xq.tile([P, 2, PASSES, P], U8, align_bytes=64)
             nc.vector.quantize_mx(
-                out=x_codes[:].rearrange("p q n -> p (q n)").bitcast(FP8X4),
-                scales=x_sc[:].rearrange("p q n -> p (q n)"),
-                in_=xg[pair][:].rearrange("p q n t -> p (q n t)"),
+                out=x_codes[:].rearrange("p s q n -> p (s q n)").bitcast(FP8X4),
+                scales=x_sc[:].rearrange("p s q n -> p (s q n)"),
+                in_=xg[pair][:].rearrange("p s q n t -> p (s q n t)"),
             )
             xc[pair] = (x_codes, x_sc)
 
         w_grp = {}
+        w_bank = {}
         wc = {}
 
         def group_w(part, kp, lo, hi, engine):
             if (part, kp) not in w_grp:
-                w_grouped = wgp.tile([P, 4 * F], BF16, align_bytes=64, tag="second" if kp == 1 else part)
+                w_grouped = wgp.tile([P, 4 * F], BF16, align_bytes=64, name="w_grouped_" + part + str(kp))
                 w_grp[part, kp] = w_grouped
             dst = w_grp[part, kp][:].rearrange("p (t m j) -> p m t j", t=4, j=4)[:, lo:hi]
             src = w_raw[part, kp][:].rearrange("p j (m t) -> p m t j", t=4)[:, lo:hi]
@@ -167,6 +158,28 @@ def tile_complexdensemodrelupair_t_kernel(tc, x_bytes, x_scale, wr, wi, b, g, vr
                 nc.scalar.copy(out=dst, in_=src)
             else:
                 nc.gpsimd.tensor_scalar(out=dst, in0=src, scalar1=1.0, scalar2=0.0, op0=ALU.mult, op1=ALU.add)
+
+        def group_w_pe(part, kp, half, tag):
+            if (part, kp) not in w_grp:
+                w_grouped = wgp.tile([P, 4 * F], BF16, align_bytes=64, name="w_grouped_" + part + str(kp))
+                w_grp[part, kp] = w_grouped
+            bank = z_ps.tile([P, 4, GROUPS // 2, 4], BF16, tag=tag, name="w_bank")
+            quarter = GROUPS // 4
+            for q in range(2):
+                first = 4 * (half * GROUPS // 2 + q * quarter)
+                nc.tensor.matmul(
+                    out=bank[:, :, q * quarter:(q + 1) * quarter, :].rearrange("p t m j -> p m t j"),
+                    lhsT=ident_bf[:],
+                    rhs=w_raw[part, kp][:, :, first:first + 4 * quarter].rearrange("p j (m t) -> p m t j", t=4),
+                    start=True, stop=True,
+                )
+            w_bank[part, kp, half] = bank
+
+        def copy_w(part, kp, half):
+            nc.scalar.copy(
+                out=w_grp[part, kp][:].rearrange("p (t x) -> p t x", t=4)[:, :, half * F // 2:(half + 1) * F // 2],
+                in_=w_bank[part, kp, half][:].rearrange("p t m j -> p t (m j)"),
+            )
 
         def quant_w(part, kp):
             w_codes = keep.tile([P, F], U32, align_bytes=64, name="w_codes_" + part + str(kp))
@@ -181,20 +194,19 @@ def tile_complexdensemodrelupair_t_kernel(tc, x_bytes, x_scale, wr, wi, b, g, vr
                 bank = side_ps.tile([P, 4, P], F32, tag=tag, name="z_bank")
             else:
                 bank = z_ps.tile([P, 4, P], F32, tag=tag or part)
-            tokens = slice((i % 2) * P, (i % 2 + 1) * P)
-            for t in range(4):
-                for kp in range(PASSES):
-                    w_codes, w_sc = wc[part, kp]
-                    x_codes, x_sc = xc[i // 2]
+            x_codes, x_sc = xc[i // 2]
+            for kp in range(PASSES):
+                w_codes, w_sc = wc[part, kp]
+                for t in range(4):
                     channels = slice(t * P, (t + 1) * P)
                     nc.tensor.matmul_mx(
                         out=bank[:, t, :],
                         lhsT=w_codes[:, channels].bitcast(FP8X4),
                         lhsT_scale=w_sc[:, channels],
-                        rhs=x_codes[:, kp, tokens].bitcast(FP8X4),
-                        rhs_scale=x_sc[:, kp, tokens],
-                        start=(kp == 0),
-                        stop=(kp == PASSES - 1),
+                        rhs=x_codes[:, i % 2, kp, :].bitcast(FP8X4),
+                        rhs_scale=x_sc[:, i % 2, kp, :],
+                        start=(kp == 0 and t == 0),
+                        stop=(kp == PASSES - 1 and t == 3),
                     )
             z[i, part] = bank
 
@@ -295,7 +307,7 @@ def tile_complexdensemodrelupair_t_kernel(tc, x_bytes, x_scale, wr, wi, b, g, vr
             for o in range(2):
                 nc.sync.dma_start(out=y_rows[o][:, first:first + count, :], in_=ysb[group][:, o, place:place + count, :])
 
-        sgn = keep.tile([P, 4], F32)
+        sgn = keep.tile([P, 4], BF16)
         absg = keep.tile([P, 4], F32)
         beta = keep.tile([P, 4], F32)
         v_grp = keep.tile([P, 3, E, 4], BF16, align_bytes=64)
@@ -305,12 +317,20 @@ def tile_complexdensemodrelupair_t_kernel(tc, x_bytes, x_scale, wr, wi, b, g, vr
         def prep_gain():
             nc.scalar.activation(out=sgn[:], in_=g_bf[:], func=ACT.Sign, bias=SIGN_OF_ZERO)
             nc.scalar.activation(out=absg[:], in_=g_bf[:], func=ACT.Abs)
-            nc.vector.tensor_tensor(out=beta[:], in0=absg[:], in1=b_bf[:], op=ALU.mult)
+            nc.gpsimd.tensor_tensor(out=beta[:], in0=absg[:], in1=b_bf[:], op=ALU.mult)
 
-        def sign_v(slot, raw):
+        v_bank = []
+
+        def group_v():
+            bank = side_ps.tile([P, 2, E, 4], BF16, tag="y", name="v_bank")
+            for o, raw in enumerate((vr_raw, vi_raw)):
+                nc.tensor.matmul(out=bank[:, o, :, :], lhsT=ident_bf[:], rhs=raw[:].rearrange("p j e -> p e j"), start=True, stop=True)
+            v_bank.append(bank)
+
+        def sign_v():
             nc.vector.tensor_tensor(
-                out=v_grp[:, slot, :, :], in0=raw[:].rearrange("p j e -> p e j"),
-                in1=sgn[:].unsqueeze(1).to_broadcast([P, E, 4]), op=ALU.mult,
+                out=v_grp[:, 1:3, :, :].rearrange("p o e j -> p (o e) j"), in0=v_bank[0][:].rearrange("p o e j -> p (o e) j"),
+                in1=sgn[:].unsqueeze(1).to_broadcast([P, 2 * E, 4]), op=ALU.mult,
             )
 
         def quant_v():
@@ -322,79 +342,78 @@ def tile_complexdensemodrelupair_t_kernel(tc, x_bytes, x_scale, wr, wi, b, g, vr
                     in_=v_grp[:, lo:hi, :, :].rearrange("p o e j -> p (o e j)"),
                 )
 
-        widen_first_pair(0)
-        turn_x(0)
-        widen_first_pair(1)
-        turn_x(1, "y")
-        group_w("r", 0, 0, GROUPS // 2, nc.scalar)
-        group_w("r", 0, GROUPS // 2, GROUPS, nc.vector)
-        scale_x(0)
-        scale_x(1)
-        group_w("r", 1, 0, GROUPS - GPSIMD_GROUPS["r"], nc.scalar)
-        group_w("r", 1, GROUPS - GPSIMD_GROUPS["r"], GROUPS, nc.gpsimd)
-        widen_x(2, nc.scalar)
-        widen_x(3, nc.scalar)
-        turn_x(2)
-        turn_x(3, "y")
-        group_w("i", 0, 0, GROUPS, nc.scalar)
+        V, S, G = nc.vector, nc.scalar, nc.gpsimd
+        for i, tag in ((0, "xt"), (1, "y")):
+            widen_x(D // 2, S)
+            widen_x(D // 2, V)
+            turn_x(i, tag)
+        widen_x(D, S)
+        widen_x(D, V)
+        turn_x(2, "r")
+        turn_x(3, "i")
+        group_w("r", 0, 0, 64, S)
+        group_w("r", 0, 64, 128, G)
+        group_w_pe("r", 1, 0, "r")
+        group_w_pe("r", 1, 1, "i")
+        widen_x(D, S)
+        widen_x(D, G)
+        copy_w("r", 1, 0)
+        copy_w("r", 1, 1)
+        for i in range(4):
+            scale_x(i)
         quant_w("r", 0)
         quant_x(0)
         quant_w("r", 1)
-        group_w("i", 1, 0, GPSIMD_GROUPS["i"], nc.gpsimd)
-        group_w("i", 1, GPSIMD_GROUPS["i"], GROUPS, nc.scalar)
-        dense_1(0, "r")
-        scale_x(2)
-        scale_x(3)
-        quant_w("i", 0)
-        quant_w("i", 1)
-        prep_gain()
-        widen_x(4, nc.scalar)
-        dense_1(1, "r")
-        dense_1(0, "i")
-        widen_x(5, nc.scalar)
-        turn_x(4)
-        dense_1(1, "i")
-        turn_x(5, "y")
-        square(0, 0)
-        widen_x(6, nc.scalar)
-        widen_x(7, nc.scalar)
         quant_x(1)
-        sign_v(2, vi_raw)
-        sign_v(1, vr_raw)
-        dense_1(2, "r")
-        square(0, 1)
-        add_squares(0, nc.gpsimd)
+        for kp in range(PASSES):
+            group_w_pe("i", kp, 0, "r")
+            group_w_pe("i", kp, 1, "i")
+            copy_w("i", kp, 0)
+            copy_w("i", kp, 1)
+            quant_w("i", kp)
+        group_v()
+        turn_x(4)
+        dense_1(0, "r")
+        dense_1(0, "i")
+        widen_x(D, S)
+        prep_gain()
+        widen_x(D, G)
+        widen_x(D, S)
         scale_x(4)
+        sign_v()
+        dense_1(1, "r")
+        dense_1(1, "i")
+        square(0, 0)
+        square(0, 1)
+        add_squares(0, V)
+        quant_v()
+        turn_x(5, "y")
+        dense_1(2, "r")
+        dense_1(2, "i")
+        turn_x(6)
         square(1, 0)
         square(1, 1)
-        add_squares(1, nc.gpsimd)
-        widen_x(8, nc.scalar, 0, D // 2)
-        turn_x(6)
-        dense_1(2, "i")
-        scale_x(5)
+        add_squares(1, G)
+        widen_x(D, G)
         inverse_root(0)
-        widen_x(8, nc.scalar, D // 2, D)
+        widen_x(D // 2, S)
         gain(0)
-        quant_v()
+        scale_x(5)
         hidden(0)
         quant_x(2)
 
         last_four = TILES - 4
         for s in range(2, last_four):
             has_y = s >= 5
-            widens = s + 7 < TILES
-            scalar_cols = SCALAR_COLS if has_y else D // 2
             square(s, 0)
             square(s, 1)
             add_squares(s, nc.gpsimd)
-            if widens:
-                widen_x(s + 7, nc.gpsimd, scalar_cols, D)
+            widen_x(GPSIMD_COLS, nc.gpsimd)
             inverse_root(s - 1)
             dense_1(s + 1, "r")
             dense_1(s + 1, "i")
             scale_x(s + 4)
-            if widens:
-                widen_x(s + 7, nc.scalar, 0, scalar_cols)
+            widen_x(SCALAR_COLS if has_y else SCALAR_COLS + D // 2, nc.scalar)
             if has_y:
                 emit_y(s - 5, nc.scalar)
                 if s % 4 == 0:

@@ -23,9 +23,8 @@ GROUPS = F // 4
 EPS = 1e-6
 SIGN_OF_ZERO = 1e-38
 PARTS = ("r", "i")
-SCALAR_COLS = 224
+SCALAR_COLS = 288
 GPSIMD_COLS = 640
-GPSIMD_GROUPS = {"r": 96, "i": 80}
 
 
 def tile_complexdensemodrelupair_t_kernel(tc, x_bytes, x_scale, wr, wi, b, g, vr, vi, out_r, out_i):
@@ -86,8 +85,6 @@ def tile_complexdensemodrelupair_t_kernel(tc, x_bytes, x_scale, wr, wi, b, g, vr
         nc.scalar.activation(out=warm[:], in_=warm[:], func=ACT.Abs_reciprocal_sqrt)
         ident = keep.tile([P, P], F32)
         make_identity(nc, ident[:])
-        ident_bf = keep.tile([P, P], BF16)
-        nc.vector.tensor_copy(out=ident_bf[:], in_=ident[:])
 
         xb = keep.tile([P, TILES * D], BF16)
         widened = [0]
@@ -143,7 +140,6 @@ def tile_complexdensemodrelupair_t_kernel(tc, x_bytes, x_scale, wr, wi, b, g, vr
             xc[pair] = (x_codes, x_sc)
 
         w_grp = {}
-        w_bank = {}
         wc = {}
 
         def group_w(part, kp, lo, hi, engine):
@@ -158,28 +154,6 @@ def tile_complexdensemodrelupair_t_kernel(tc, x_bytes, x_scale, wr, wi, b, g, vr
                 nc.scalar.copy(out=dst, in_=src)
             else:
                 nc.gpsimd.tensor_scalar(out=dst, in0=src, scalar1=1.0, scalar2=0.0, op0=ALU.mult, op1=ALU.add)
-
-        def group_w_pe(part, kp, half, tag):
-            if (part, kp) not in w_grp:
-                w_grouped = wgp.tile([P, 4 * F], BF16, align_bytes=64, name="w_grouped_" + part + str(kp))
-                w_grp[part, kp] = w_grouped
-            bank = z_ps.tile([P, 4, GROUPS // 2, 4], BF16, tag=tag, name="w_bank")
-            quarter = GROUPS // 4
-            for q in range(2):
-                first = 4 * (half * GROUPS // 2 + q * quarter)
-                nc.tensor.matmul(
-                    out=bank[:, :, q * quarter:(q + 1) * quarter, :].rearrange("p t m j -> p m t j"),
-                    lhsT=ident_bf[:],
-                    rhs=w_raw[part, kp][:, :, first:first + 4 * quarter].rearrange("p j (m t) -> p m t j", t=4),
-                    start=True, stop=True,
-                )
-            w_bank[part, kp, half] = bank
-
-        def copy_w(part, kp, half):
-            nc.scalar.copy(
-                out=w_grp[part, kp][:].rearrange("p (t x) -> p t x", t=4)[:, :, half * F // 2:(half + 1) * F // 2],
-                in_=w_bank[part, kp, half][:].rearrange("p t m j -> p t (m j)"),
-            )
 
         def quant_w(part, kp):
             w_codes = keep.tile([P, F], U32, align_bytes=64, name="w_codes_" + part + str(kp))
@@ -317,30 +291,24 @@ def tile_complexdensemodrelupair_t_kernel(tc, x_bytes, x_scale, wr, wi, b, g, vr
         def prep_gain():
             nc.scalar.activation(out=sgn[:], in_=g_bf[:], func=ACT.Sign, bias=SIGN_OF_ZERO)
             nc.scalar.activation(out=absg[:], in_=g_bf[:], func=ACT.Abs)
-            nc.gpsimd.tensor_tensor(out=beta[:], in0=absg[:], in1=b_bf[:], op=ALU.mult)
+            nc.vector.tensor_tensor(out=beta[:], in0=absg[:], in1=b_bf[:], op=ALU.mult)
 
-        v_bank = []
-
-        def group_v():
-            bank = side_ps.tile([P, 2, E, 4], BF16, tag="y", name="v_bank")
-            for o, raw in enumerate((vr_raw, vi_raw)):
-                nc.tensor.matmul(out=bank[:, o, :, :], lhsT=ident_bf[:], rhs=raw[:].rearrange("p j e -> p e j"), start=True, stop=True)
-            v_bank.append(bank)
-
-        def sign_v():
+        def sign_v(slot, raw):
             nc.vector.tensor_tensor(
-                out=v_grp[:, 1:3, :, :].rearrange("p o e j -> p (o e) j"), in0=v_bank[0][:].rearrange("p o e j -> p (o e) j"),
-                in1=sgn[:].unsqueeze(1).to_broadcast([P, 2 * E, 4]), op=ALU.mult,
+                out=v_grp[:, slot, :, :].rearrange("p (c k) j -> p c j k", k=2),
+                in0=raw[:].rearrange("p j (c k) -> p c j k", k=2),
+                in1=sgn[:].unsqueeze(1).to_broadcast([P, E, 4]).rearrange("p (c k) j -> p c j k", k=2), op=ALU.mult,
             )
 
-        def quant_v():
+        def negate_v():
             nc.vector.tensor_scalar(out=v_grp[:, 0, :, :], in0=v_grp[:, 2, :, :], scalar1=-1.0, scalar2=None, op0=ALU.mult)
-            for lo, hi in ((1, 3), (0, 1)):
-                cols = slice(lo * E, hi * E)
-                nc.vector.quantize_mx(
-                    out=v_codes[:, cols].bitcast(FP8X4), scales=v_sc[:, cols],
-                    in_=v_grp[:, lo:hi, :, :].rearrange("p o e j -> p (o e j)"),
-                )
+
+        def quant_v(lo, hi):
+            cols = slice(lo * E, hi * E)
+            nc.vector.quantize_mx(
+                out=v_codes[:, cols].bitcast(FP8X4), scales=v_sc[:, cols],
+                in_=v_grp[:, lo:hi, :, :].rearrange("p o e j -> p (o e j)"),
+            )
 
         V, S, G = nc.vector, nc.scalar, nc.gpsimd
         for i, tag in ((0, "xt"), (1, "y")):
@@ -353,51 +321,48 @@ def tile_complexdensemodrelupair_t_kernel(tc, x_bytes, x_scale, wr, wi, b, g, vr
         turn_x(3, "i")
         group_w("r", 0, 0, 64, S)
         group_w("r", 0, 64, 128, G)
-        group_w_pe("r", 1, 0, "r")
-        group_w_pe("r", 1, 1, "i")
-        widen_x(D, S)
+        group_w("r", 1, 0, 76, S)
+        group_w("r", 1, 76, 128, G)
         widen_x(D, G)
-        copy_w("r", 1, 0)
-        copy_w("r", 1, 1)
+        turn_x(4)
         for i in range(4):
             scale_x(i)
         quant_w("r", 0)
         quant_x(0)
         quant_w("r", 1)
-        quant_x(1)
-        for kp in range(PASSES):
-            group_w_pe("i", kp, 0, "r")
-            group_w_pe("i", kp, 1, "i")
-            copy_w("i", kp, 0)
-            copy_w("i", kp, 1)
-            quant_w("i", kp)
-        group_v()
-        turn_x(4)
+        group_w("i", 0, 0, 128, S)
+        group_w("i", 1, 0, 72, S)
+        group_w("i", 1, 72, 128, V)
+        quant_w("i", 0)
+        quant_w("i", 1)
         dense_1(0, "r")
         dense_1(0, "i")
-        widen_x(D, S)
-        prep_gain()
-        widen_x(D, G)
-        widen_x(D, S)
-        scale_x(4)
-        sign_v()
         dense_1(1, "r")
         dense_1(1, "i")
+        widen_x(D, S)
+        prep_gain()
+        turn_x(5, "y")
+        quant_x(1)
+        sign_v(2, vi_raw)
+        sign_v(1, vr_raw)
+        negate_v()
+        quant_v(1, 3)
         square(0, 0)
+        widen_x(D, S)
         square(0, 1)
         add_squares(0, V)
-        quant_v()
-        turn_x(5, "y")
+        quant_v(0, 1)
+        scale_x(4)
         dense_1(2, "r")
         dense_1(2, "i")
         turn_x(6)
         square(1, 0)
         square(1, 1)
         add_squares(1, G)
-        widen_x(D, G)
         inverse_root(0)
         widen_x(D // 2, S)
         gain(0)
+        widen_x(D + D // 8, G)
         scale_x(5)
         hidden(0)
         quant_x(2)
@@ -408,7 +373,6 @@ def tile_complexdensemodrelupair_t_kernel(tc, x_bytes, x_scale, wr, wi, b, g, vr
             square(s, 0)
             square(s, 1)
             add_squares(s, nc.gpsimd)
-            widen_x(GPSIMD_COLS, nc.gpsimd)
             inverse_root(s - 1)
             dense_1(s + 1, "r")
             dense_1(s + 1, "i")
@@ -422,6 +386,7 @@ def tile_complexdensemodrelupair_t_kernel(tc, x_bytes, x_scale, wr, wi, b, g, vr
                 dense_2(s - 4)
             if s + 5 < TILES:
                 turn_x(s + 5)
+            widen_x(GPSIMD_COLS, nc.gpsimd)
             gain(s - 1)
             hidden(s - 1)
             if s % 2 == 1:

@@ -23,8 +23,8 @@ GROUPS = F // 4
 EPS = 1e-6
 SIGN_OF_ZERO = 1e-38
 PARTS = ("r", "i")
-SCALAR_COLS = 288
-GPSIMD_COLS = 640
+SCALAR_COLS = 320
+GPSIMD_COLS = 656
 
 
 def tile_complexdensemodrelupair_t_kernel(tc, x_bytes, x_scale, wr, wi, b, g, vr, vi, out_r, out_i):
@@ -34,8 +34,8 @@ def tile_complexdensemodrelupair_t_kernel(tc, x_bytes, x_scale, wr, wi, b, g, vr
 
     with ExitStack() as ctx:
         keep = ctx.enter_context(tc.tile_pool(name="keep", bufs=1))
-        xw = ctx.enter_context(tc.tile_pool(name="xw", bufs=3))
-        xq = ctx.enter_context(tc.tile_pool(name="xq", bufs=4))
+        qin = ctx.enter_context(tc.tile_pool(name="qin", bufs=3))
+        qout = ctx.enter_context(tc.tile_pool(name="qout", bufs=4))
         wgp = ctx.enter_context(tc.tile_pool(name="wgp", bufs=1))
         mh = ctx.enter_context(tc.tile_pool(name="mh", bufs=2))
         hid = ctx.enter_context(tc.tile_pool(name="hid", bufs=3))
@@ -65,14 +65,14 @@ def tile_complexdensemodrelupair_t_kernel(tc, x_bytes, x_scale, wr, wi, b, g, vr
         load_x(2, 2)
         load_w("r", wr, 0)
         load_w("r", wr, 1)
-        load_x(4, 2)
         load_w("i", wi, 0)
         load_w("i", wi, 1)
-        load_x(6, 2)
+        load_x(4, 2)
         b_bf = keep.tile([P, 4], BF16)
         nc.sync.dma_start(out=b_bf[:], in_=b.rearrange("(p t) -> p t", t=4))
         g_bf = keep.tile([P, 4], BF16)
         nc.sync.dma_start(out=g_bf[:], in_=g.rearrange("(p t) -> p t", t=4))
+        load_x(6, 2)
         vr_raw = keep.tile([P, 4, E], BF16)
         nc.sync.dma_start(out=vr_raw[:], in_=vr.rearrange("(p j) e -> p j e", j=4))
         vi_raw = keep.tile([P, 4, E], BF16)
@@ -113,31 +113,41 @@ def tile_complexdensemodrelupair_t_kernel(tc, x_bytes, x_scale, wr, wi, b, g, vr
                     nc.tensor.transpose(bank[:, u, kp, :], words[:, first + u:first + K_PASS // 2:2], ident[:])
             xt[i] = bank
 
-        xg = {}
+        staged = {}
+
+        def stage(call, half):
+            if call not in staged:
+                quant_in = qin.tile([P, 2, D], BF16, align_bytes=64)
+                staged[call] = quant_in
+            return staged[call][:, half, :]
+
+        def x_place(i):
+            return (i // 2 - 1, i % 2) if i < 4 else (i - 3, 0)
 
         def scale_x(i):
-            pair, side = divmod(i, 2)
-            if side == 0:
-                xg_pair = xw.tile([P, 2, PASSES, P, 4], BF16, align_bytes=64)
-                xg[pair] = xg_pair
             nc.vector.tensor_tensor(
-                out=xg[pair][:, side].rearrange("p q n (u e) -> p q n u e", u=2),
+                out=stage(*x_place(i)).rearrange("p (q n u e) -> p q n u e", q=PASSES, u=2, e=2),
                 in0=xt[i][:].rearrange("p u q n -> p (u q n)").bitcast(BF16).rearrange("p (u q n e) -> p q n u e", u=2, q=PASSES, e=2),
                 in1=xs[:].unsqueeze(2).to_broadcast([P, PASSES, P, 4]).rearrange("p q n (u e) -> p q n u e", u=2),
                 op=ALU.mult,
             )
 
-        xc = {}
+        quantised = {}
 
-        def quant_x(pair):
-            x_codes = xq.tile([P, 2, PASSES, P], U32, align_bytes=64)
-            x_sc = xq.tile([P, 2, PASSES, P], U8, align_bytes=64)
+        def quant(call, lo=0, hi=4):
+            if call not in quantised:
+                codes = qout.tile([P, 4 * P], U32, align_bytes=64)
+                scales = qout.tile([P, 4 * P], U8, align_bytes=64)
+                quantised[call] = (codes, scales)
+            codes, scales = quantised[call]
             nc.vector.quantize_mx(
-                out=x_codes[:].rearrange("p s q n -> p (s q n)").bitcast(FP8X4),
-                scales=x_sc[:].rearrange("p s q n -> p (s q n)"),
-                in_=xg[pair][:].rearrange("p s q n t -> p (s q n t)"),
+                out=codes[:, lo * P:hi * P].bitcast(FP8X4), scales=scales[:, lo * P:hi * P],
+                in_=staged[call][:].rearrange("p a c -> p (a c)")[:, lo * K_PASS:hi * K_PASS],
             )
-            xc[pair] = (x_codes, x_sc)
+
+        def quarter(call, n):
+            codes, scales = quantised[call]
+            return codes[:, n * P:(n + 1) * P].bitcast(FP8X4), scales[:, n * P:(n + 1) * P]
 
         w_grp = {}
         wc = {}
@@ -168,17 +178,18 @@ def tile_complexdensemodrelupair_t_kernel(tc, x_bytes, x_scale, wr, wi, b, g, vr
                 bank = side_ps.tile([P, 4, P], F32, tag=tag, name="z_bank")
             else:
                 bank = z_ps.tile([P, 4, P], F32, tag=tag or part)
-            x_codes, x_sc = xc[i // 2]
+            call, half = x_place(i)
             for kp in range(PASSES):
                 w_codes, w_sc = wc[part, kp]
+                x_codes, x_sc = quarter(call, 2 * half + kp)
                 for t in range(4):
                     channels = slice(t * P, (t + 1) * P)
                     nc.tensor.matmul_mx(
                         out=bank[:, t, :],
                         lhsT=w_codes[:, channels].bitcast(FP8X4),
                         lhsT_scale=w_sc[:, channels],
-                        rhs=x_codes[:, i % 2, kp, :].bitcast(FP8X4),
-                        rhs_scale=x_sc[:, i % 2, kp, :],
+                        rhs=x_codes,
+                        rhs_scale=x_sc,
                         start=(kp == 0 and t == 0),
                         stop=(kp == PASSES - 1 and t == 3),
                     )
@@ -195,7 +206,7 @@ def tile_complexdensemodrelupair_t_kernel(tc, x_bytes, x_scale, wr, wi, b, g, vr
         mg = {}
 
         def add_squares(i, engine):
-            m2_then_gain = mh.tile([P, 4, P], F32, tag="last" if i == TILES - 1 else "m2")
+            m2_then_gain = mh.tile([P, 4, P], F32, tag="last" if i >= TILES - 2 else "m2")
             mg[i] = m2_then_gain
             engine.tensor_tensor(out=mg[i][:].rearrange("p t n -> p (t n)"), in0=sq[i][:, 0, :], in1=sq[i][:, 1, :], op=ALU.add)
 
@@ -215,47 +226,38 @@ def tile_complexdensemodrelupair_t_kernel(tc, x_bytes, x_scale, wr, wi, b, g, vr
                     out=mg[i][:, t, :], in_=inv_m[i][:, t, :], func=ACT.Relu, scale=beta[:, t:t + 1], bias=absg[:, t:t + 1],
                 )
 
-        h = {}
+        def affine_on_vector(i):
+            for t in range(4):
+                nc.vector.tensor_scalar(
+                    out=mg[i][:, t, :], in0=inv_m[i][:, t, :], scalar1=beta[:, t:t + 1], scalar2=absg[:, t:t + 1],
+                    op0=ALU.mult, op1=ALU.add,
+                )
 
-        def hidden(i):
-            j, side = divmod(i + 1, 2)
-            if j not in h:
-                h_pair = hid.tile([P, 2, 2 * F], BF16, align_bytes=64)
-                h[j] = h_pair
-            for o in range(2):
+        def relu_on_vector(i):
+            flat = mg[i][:].rearrange("p t n -> p (t n)")
+            nc.vector.tensor_scalar(out=flat, in0=flat, scalar1=0.0, scalar2=None, op0=ALU.max)
+
+        def hidden(i, parts=(0, 1)):
+            for o in parts:
                 nc.vector.tensor_tensor(
-                    out=h[j][:, side, o * F:(o + 1) * F].rearrange("p (c k t) -> p c t k", k=2, t=4),
+                    out=stage(i + 2, 1)[:, o * F:(o + 1) * F].rearrange("p (c k t) -> p c t k", k=2, t=4),
                     in0=z[i, PARTS[o]][:].rearrange("p t (c k) -> p c t k", k=2),
                     in1=mg[i][:].rearrange("p t (c k) -> p c t k", k=2),
                     op=ALU.mult,
                 )
-
-        hc = {}
-
-        def quant_h(first, count):
-            h_codes = hid.tile([P, 4 * P], U32, align_bytes=64)
-            h_sc = hid.tile([P, 4 * P], U8, align_bytes=64)
-            j, side = divmod(first + 1, 2)
-            nc.vector.quantize_mx(
-                out=h_codes[:, 0:count * 2 * P].bitcast(FP8X4), scales=h_sc[:, 0:count * 2 * P],
-                in_=h[j][:, side:side + count, :].rearrange("p j c -> p (j c)"),
-            )
-            for n in range(count):
-                hc[first + n] = (h_codes[:, n * 2 * P:(n + 1) * 2 * P], h_sc[:, n * 2 * P:(n + 1) * 2 * P])
 
         y = {}
 
         def dense_2(i, tag="y"):
             pool = z_ps if tag in PARTS else side_ps
             y_bank = pool.tile([P, 2, E], F32, tag=tag)
-            h_codes, h_sc = hc[i]
             for o in range(2):
-                tokens = slice(o * P, (o + 1) * P)
+                h_codes, h_sc = quarter(i + 2, 2 + o)
                 cols = slice((1 - o) * E, (3 - o) * E)
                 nc.tensor.matmul_mx(
                     out=y_bank[:].rearrange("p o e -> p (o e)"),
-                    lhsT=h_codes[:, tokens].bitcast(FP8X4),
-                    lhsT_scale=h_sc[:, tokens],
+                    lhsT=h_codes,
+                    lhsT_scale=h_sc,
                     rhs=v_codes[:, cols].bitcast(FP8X4),
                     rhs_scale=v_sc[:, cols],
                     start=(o == 0),
@@ -321,28 +323,27 @@ def tile_complexdensemodrelupair_t_kernel(tc, x_bytes, x_scale, wr, wi, b, g, vr
         turn_x(3, "i")
         group_w("r", 0, 0, 64, S)
         group_w("r", 0, 64, 128, G)
-        group_w("r", 1, 0, 76, S)
-        group_w("r", 1, 76, 128, G)
-        widen_x(D, G)
-        turn_x(4)
+        group_w("r", 1, 0, 72, S)
+        group_w("r", 1, 72, 128, G)
+        group_w("i", 0, 0, 76, S)
+        group_w("i", 0, 76, 128, G)
+        group_w("i", 1, 0, 112, S)
         for i in range(4):
             scale_x(i)
         quant_w("r", 0)
-        quant_x(0)
+        quant(-1)
         quant_w("r", 1)
-        group_w("i", 0, 0, 128, S)
-        group_w("i", 1, 0, 72, S)
-        group_w("i", 1, 72, 128, V)
+        group_w("i", 1, 112, 128, V)
         quant_w("i", 0)
         quant_w("i", 1)
         dense_1(0, "r")
         dense_1(0, "i")
         dense_1(1, "r")
         dense_1(1, "i")
-        widen_x(D, S)
         prep_gain()
-        turn_x(5, "y")
-        quant_x(1)
+        widen_x(D, S)
+        turn_x(4)
+        quant(0)
         sign_v(2, vi_raw)
         sign_v(1, vr_raw)
         negate_v()
@@ -355,104 +356,87 @@ def tile_complexdensemodrelupair_t_kernel(tc, x_bytes, x_scale, wr, wi, b, g, vr
         scale_x(4)
         dense_1(2, "r")
         dense_1(2, "i")
-        turn_x(6)
         square(1, 0)
         square(1, 1)
         add_squares(1, G)
         inverse_root(0)
         widen_x(D // 2, S)
         gain(0)
-        widen_x(D + D // 8, G)
-        scale_x(5)
+        widen_x(D // 2, G)
+        turn_x(5)
         hidden(0)
-        quant_x(2)
+        quant(1, 0, 2)
 
-        last_four = TILES - 4
-        for s in range(2, last_four):
-            has_y = s >= 5
+        for s in range(2, TILES - 3):
+            has_y = s >= 4
             square(s, 0)
             square(s, 1)
             add_squares(s, nc.gpsimd)
             inverse_root(s - 1)
             dense_1(s + 1, "r")
             dense_1(s + 1, "i")
-            scale_x(s + 4)
+            scale_x(s + 3)
             widen_x(SCALAR_COLS if has_y else SCALAR_COLS + D // 2, nc.scalar)
             if has_y:
-                emit_y(s - 5, nc.scalar)
-                if s % 4 == 0:
-                    store_y(s - 8, 4)
-            if s >= 4:
-                dense_2(s - 4)
-            if s + 5 < TILES:
-                turn_x(s + 5)
+                emit_y(s - 4, nc.scalar)
+                if s % 4 == 3:
+                    store_y(s - 7, 4)
+            if s >= 3:
+                dense_2(s - 3)
+            if s + 4 < TILES:
+                turn_x(s + 4)
             widen_x(GPSIMD_COLS, nc.gpsimd)
             gain(s - 1)
             hidden(s - 1)
-            if s % 2 == 1:
-                quant_x((s + 3) // 2)
-            elif s == 2:
-                quant_h(0, 1)
-            else:
-                quant_h(s - 3, 2)
+            quant(s)
 
-        ta, tb, te, td = last_four, last_four + 1, last_four + 2, last_four + 3
+        ta, tb, te = TILES - 3, TILES - 2, TILES - 1
         dense_1(tb, "r", "xt")
         square(ta, 0)
         square(ta, 1)
-        add_squares(ta, nc.vector)
+        add_squares(ta, V)
         inverse_root(ta - 1)
+        emit_y(ta - 4, S)
+        gain(ta - 1)
         dense_1(tb, "i")
         dense_1(te, "r")
         square(tb, 0)
-        quant_h(ta - 3, 2)
-        gain(ta - 1)
         hidden(ta - 1)
-        emit_y(ta - 5, nc.vector)
-        store_y(ta - 8, 4)
         dense_1(te, "i", "r")
-        dense_1(td, "r", "i")
-        dense_2(ta - 4)
-        square(tb, 1)
-        add_squares(tb, nc.vector)
-        inverse_root(ta)
-        square(te, 0)
-        gain(ta)
-        hidden(ta)
-        emit_y(ta - 4, nc.vector)
-        dense_1(td, "i", "r")
+        quant(ta, 2, 4)
         dense_2(ta - 3)
         dense_2(ta - 2, "i")
+        square(tb, 1)
+        add_squares(tb, V)
+        inverse_root(ta)
+        affine_on_vector(ta)
+        quant(tb, 2, 4)
+        relu_on_vector(ta)
+        square(te, 0)
         square(te, 1)
-        add_squares(te, nc.vector)
         inverse_root(tb)
-        square(td, 0)
+        emit_y(ta - 3, S)
+        dense_2(ta - 1)
         gain(tb)
-        square(td, 1)
-        hidden(tb)
-        add_squares(td, nc.vector)
-        quant_h(ta - 1, 2)
+        add_squares(te, V)
+        hidden(ta)
         inverse_root(te)
-        emit_y(ta - 3, nc.scalar)
-        dense_2(ta - 1, "xt")
-        dense_2(ta, "i")
+        emit_y(ta - 2, S)
+        store_y(ta - 5, 4)
         gain(te)
-        inverse_root(td)
-        emit_y(ta - 2, nc.scalar)
-        gain(td)
+        hidden(tb)
+        quant(te, 2, 4)
+        dense_2(ta, "i")
+        quant(te + 1, 2, 4)
+        dense_2(tb, "r")
+        emit_y(ta - 1, S)
         hidden(te)
-        quant_h(tb, 1)
-        dense_2(tb)
-        emit_y(ta - 1, nc.scalar)
-        store_y(ta - 4, 4)
-        emit_y(ta, nc.scalar)
-        hidden(td)
-        quant_h(te, 1)
-        dense_2(te, "r")
-        quant_h(td, 1)
-        dense_2(td, "r")
-        emit_y(tb, nc.scalar)
-        store_y(ta, 2)
-        emit_y(te, nc.scalar)
-        emit_y(td, nc.vector)
-        store_y(te, 2)
+        emit_y(ta, S)
+        store_y(ta - 1, 2)
+        quant(te + 2, 2, 3)
+        quant(te + 2, 3, 4)
+        dense_2(te)
+        emit_y(tb, S)
+        store_y(tb, 1)
+        emit_y(te, V)
+        store_y(te, 1)

@@ -24,7 +24,7 @@ EPS = 1e-6
 SIGN_OF_ZERO = 1e-38
 PARTS = ("r", "i")
 SCALAR_COLS = 320
-GPSIMD_COLS = 656
+GPSIMD_COLS = 640
 
 
 def tile_complexdensemodrelupair_t_kernel(tc, x_bytes, x_scale, wr, wi, b, g, vr, vi, out_r, out_i):
@@ -278,10 +278,10 @@ def tile_complexdensemodrelupair_t_kernel(tc, x_bytes, x_scale, wr, wi, b, g, vr
             else:
                 nc.vector.tensor_copy(out=dst, in_=y[i][:])
 
-        def store_y(first, count):
+        def store_y(first, count, queues=(nc.sync, nc.sync)):
             group, place = divmod(first, 4)
             for o in range(2):
-                nc.sync.dma_start(out=y_rows[o][:, first:first + count, :], in_=ysb[group][:, o, place:place + count, :])
+                queues[o].dma_start(out=y_rows[o][:, first:first + count, :], in_=ysb[group][:, o, place:place + count, :])
 
         sgn = keep.tile([P, 4], BF16)
         absg = keep.tile([P, 4], F32)
@@ -290,13 +290,15 @@ def tile_complexdensemodrelupair_t_kernel(tc, x_bytes, x_scale, wr, wi, b, g, vr
         v_codes = keep.tile([P, 3 * E], U32, align_bytes=64)
         v_sc = keep.tile([P, 3 * E], U8, align_bytes=64)
 
-        def prep_gain():
+        def prep_signs():
             nc.scalar.activation(out=sgn[:], in_=g_bf[:], func=ACT.Sign, bias=SIGN_OF_ZERO)
             nc.scalar.activation(out=absg[:], in_=g_bf[:], func=ACT.Abs)
+
+        def prep_beta():
             nc.vector.tensor_tensor(out=beta[:], in0=absg[:], in1=b_bf[:], op=ALU.mult)
 
-        def sign_v(slot, raw):
-            nc.vector.tensor_tensor(
+        def sign_v(slot, raw, engine):
+            engine.tensor_tensor(
                 out=v_grp[:, slot, :, :].rearrange("p (c k) j -> p c j k", k=2),
                 in0=raw[:].rearrange("p j (c k) -> p c j k", k=2),
                 in1=sgn[:].unsqueeze(1).to_broadcast([P, E, 4]).rearrange("p (c k) j -> p c j k", k=2), op=ALU.mult,
@@ -323,46 +325,47 @@ def tile_complexdensemodrelupair_t_kernel(tc, x_bytes, x_scale, wr, wi, b, g, vr
         turn_x(3, "i")
         group_w("r", 0, 0, 64, S)
         group_w("r", 0, 64, 128, G)
-        group_w("r", 1, 0, 72, S)
-        group_w("r", 1, 72, 128, G)
-        group_w("i", 0, 0, 76, S)
-        group_w("i", 0, 76, 128, G)
-        group_w("i", 1, 0, 112, S)
-        for i in range(4):
+        group_w("r", 1, 0, 64, S)
+        group_w("r", 1, 64, 128, G)
+        group_w("i", 0, 0, 128, S)
+        group_w("i", 1, 0, 40, S)
+        for i in range(3):
             scale_x(i)
         quant_w("r", 0)
         quant(-1)
         quant_w("r", 1)
-        group_w("i", 1, 112, 128, V)
+        group_w("i", 1, 40, 128, V)
         quant_w("i", 0)
         quant_w("i", 1)
         dense_1(0, "r")
         dense_1(0, "i")
         dense_1(1, "r")
-        dense_1(1, "i")
-        prep_gain()
         widen_x(D, S)
+        prep_signs()
         turn_x(4)
-        quant(0)
-        sign_v(2, vi_raw)
-        sign_v(1, vr_raw)
-        negate_v()
-        quant_v(1, 3)
+        dense_1(1, "i")
+        scale_x(3)
+        sign_v(2, vi_raw, G)
+        sign_v(1, vr_raw, V)
         square(0, 0)
-        widen_x(D, S)
+        widen_x(D + D // 2, S)
         square(0, 1)
         add_squares(0, V)
+        quant(0)
+        prep_beta()
+        negate_v()
+        quant_v(1, 3)
         quant_v(0, 1)
         scale_x(4)
         dense_1(2, "r")
         dense_1(2, "i")
         square(1, 0)
+        widen_x(7 * D // 8, S)
+        inverse_root(0)
         square(1, 1)
         add_squares(1, G)
-        inverse_root(0)
-        widen_x(D // 2, S)
         gain(0)
-        widen_x(D // 2, G)
+        widen_x(3 * D // 8, G)
         turn_x(5)
         hidden(0)
         quant(1, 0, 2)
@@ -376,7 +379,7 @@ def tile_complexdensemodrelupair_t_kernel(tc, x_bytes, x_scale, wr, wi, b, g, vr
             dense_1(s + 1, "r")
             dense_1(s + 1, "i")
             scale_x(s + 3)
-            widen_x(SCALAR_COLS if has_y else SCALAR_COLS + D // 2, nc.scalar)
+            widen_x(SCALAR_COLS if has_y else 2 * SCALAR_COLS, nc.scalar)
             if has_y:
                 emit_y(s - 4, nc.scalar)
                 if s % 4 == 3:
@@ -439,4 +442,4 @@ def tile_complexdensemodrelupair_t_kernel(tc, x_bytes, x_scale, wr, wi, b, g, vr
         emit_y(tb, S)
         store_y(tb, 1)
         emit_y(te, V)
-        store_y(te, 1)
+        store_y(te, 1, (nc.sync, nc.scalar))

@@ -156,14 +156,17 @@ def tile_complexdensemodrelupair_t_kernel(tc, x_bytes, x_scale, wr, wi, b, g, vr
             if (part, kp) not in w_grp:
                 w_grouped = wgp.tile([P, 4 * F], BF16, align_bytes=64, name="w_grouped_" + part + str(kp))
                 w_grp[part, kp] = w_grouped
-            dst = w_grp[part, kp][:].rearrange("p (t m j) -> p m t j", t=4, j=4)[:, lo:hi]
-            src = w_raw[part, kp][:].rearrange("p j (m t) -> p m t j", t=4)[:, lo:hi]
+            if engine is nc.gpsimd:
+                dst = w_grp[part, kp][:].rearrange("p (t m j) -> p m t j", t=4, j=4)[:, lo:hi]
+                src = w_raw[part, kp][:].rearrange("p j (m t) -> p m t j", t=4)[:, lo:hi]
+                nc.gpsimd.tensor_scalar(out=dst, in0=src, scalar1=1.0, scalar2=0.0, op0=ALU.mult, op1=ALU.add)
+                return
+            dst = w_grp[part, kp][:].rearrange("p (t m k j) -> p m t k j", t=4, k=2, j=4)[:, lo // 2:hi // 2]
+            src = w_raw[part, kp][:].rearrange("p j (m k t) -> p m t k j", k=2, t=4)[:, lo // 2:hi // 2]
             if engine is nc.vector:
                 nc.vector.tensor_copy(out=dst, in_=src)
-            elif engine is nc.scalar:
-                nc.scalar.copy(out=dst, in_=src)
             else:
-                nc.gpsimd.tensor_scalar(out=dst, in0=src, scalar1=1.0, scalar2=0.0, op0=ALU.mult, op1=ALU.add)
+                nc.scalar.copy(out=dst, in_=src)
 
         def quant_w(part, kp):
             w_codes = keep.tile([P, F], U32, align_bytes=64, name="w_codes_" + part + str(kp))
@@ -206,7 +209,7 @@ def tile_complexdensemodrelupair_t_kernel(tc, x_bytes, x_scale, wr, wi, b, g, vr
         mg = {}
 
         def add_squares(i, engine):
-            m2_then_gain = mh.tile([P, 4, P], F32, tag="last" if i >= TILES - 2 else "m2")
+            m2_then_gain = mh.tile([P, 4, P], F32, align_bytes=64, tag="last" if i >= TILES - 2 else "m2")
             mg[i] = m2_then_gain
             engine.tensor_tensor(out=mg[i][:].rearrange("p t n -> p (t n)"), in0=sq[i][:, 0, :], in1=sq[i][:, 1, :], op=ALU.add)
 
@@ -286,7 +289,7 @@ def tile_complexdensemodrelupair_t_kernel(tc, x_bytes, x_scale, wr, wi, b, g, vr
         sgn = keep.tile([P, 4], BF16)
         absg = keep.tile([P, 4], F32)
         beta = keep.tile([P, 4], F32)
-        v_grp = keep.tile([P, 3, E, 4], BF16, align_bytes=64)
+        v_grp = mh.tile([P, 3, E, 4], BF16, align_bytes=64, tag="m2")
         v_codes = keep.tile([P, 3 * E], U32, align_bytes=64)
         v_sc = keep.tile([P, 3 * E], U8, align_bytes=64)
 
@@ -298,10 +301,11 @@ def tile_complexdensemodrelupair_t_kernel(tc, x_bytes, x_scale, wr, wi, b, g, vr
             nc.vector.tensor_tensor(out=beta[:], in0=absg[:], in1=b_bf[:], op=ALU.mult)
 
         def sign_v(slot, raw, engine):
+            walk = "p c j k" if engine is nc.vector else "p c k j"
             engine.tensor_tensor(
-                out=v_grp[:, slot, :, :].rearrange("p (c k) j -> p c j k", k=2),
-                in0=raw[:].rearrange("p j (c k) -> p c j k", k=2),
-                in1=sgn[:].unsqueeze(1).to_broadcast([P, E, 4]).rearrange("p (c k) j -> p c j k", k=2), op=ALU.mult,
+                out=v_grp[:, slot, :, :].rearrange("p (c k) j -> " + walk, k=2),
+                in0=raw[:].rearrange("p j (c k) -> " + walk, k=2),
+                in1=sgn[:].unsqueeze(1).to_broadcast([P, E, 4]).rearrange("p (c k) j -> " + walk, k=2), op=ALU.mult,
             )
 
         def negate_v():
@@ -352,8 +356,8 @@ def tile_complexdensemodrelupair_t_kernel(tc, x_bytes, x_scale, wr, wi, b, g, vr
         square(0, 1)
         add_squares(0, V)
         quant(0)
-        prep_beta()
         negate_v()
+        prep_beta()
         quant_v(1, 3)
         quant_v(0, 1)
         scale_x(4)
@@ -442,4 +446,4 @@ def tile_complexdensemodrelupair_t_kernel(tc, x_bytes, x_scale, wr, wi, b, g, vr
         emit_y(tb, S)
         store_y(tb, 1)
         emit_y(te, V)
-        store_y(te, 1, (nc.sync, nc.scalar))
+        store_y(te, 1)

@@ -35,13 +35,12 @@ def tile_complexdensemodrelupair_t_kernel(tc, x_bytes, x_scale, wr, wi, b, g, vr
     with ExitStack() as ctx:
         keep = ctx.enter_context(tc.tile_pool(name="keep", bufs=1))
         qin = ctx.enter_context(tc.tile_pool(name="qin", bufs=3))
-        qout = ctx.enter_context(tc.tile_pool(name="qout", bufs=4))
+        qout = ctx.enter_context(tc.tile_pool(name="qout", bufs=8))
         wgp = ctx.enter_context(tc.tile_pool(name="wgp", bufs=1))
         mh = ctx.enter_context(tc.tile_pool(name="mh", bufs=2))
         hid = ctx.enter_context(tc.tile_pool(name="hid", bufs=3))
         outp = ctx.enter_context(tc.tile_pool(name="outp", bufs=3))
-        side_ps = ctx.enter_context(tc.psum_pool(name="side_ps", bufs=1))
-        z_ps = ctx.enter_context(tc.psum_pool(name="z_ps", bufs=3))
+        banks = ctx.enter_context(tc.psum_pool(name="banks", bufs=1))
         ctx.enter_context(tc.manual_schedule())
 
         x8 = keep.tile([P, TILES * D], U8, name="x8")
@@ -105,8 +104,7 @@ def tile_complexdensemodrelupair_t_kernel(tc, x_bytes, x_scale, wr, wi, b, g, vr
         def turn_x(i, tag="xt"):
             assert widened[0] >= (i + 1) * D
             words = xb[:].bitcast(F32)
-            pool = z_ps if tag in PARTS else side_ps
-            bank = pool.tile([P, 2, PASSES, P], F32, tag=tag, name="xt_bank")
+            bank = banks.tile([P, 2, PASSES, P], F32, tag=tag, name="xt_bank")
             for kp in range(PASSES):
                 for u in range(2):
                     first = (i * D + kp * K_PASS) // 2
@@ -177,10 +175,7 @@ def tile_complexdensemodrelupair_t_kernel(tc, x_bytes, x_scale, wr, wi, b, g, vr
         z = {}
 
         def dense_1(i, part, tag=None):
-            if tag == "xt":
-                bank = side_ps.tile([P, 4, P], F32, tag=tag, name="z_bank")
-            else:
-                bank = z_ps.tile([P, 4, P], F32, tag=tag or part)
+            bank = banks.tile([P, 4, P], F32, tag=tag or part + str(i % 3), name="z_bank")
             call, half = x_place(i)
             for kp in range(PASSES):
                 w_codes, w_sc = wc[part, kp]
@@ -223,21 +218,21 @@ def tile_complexdensemodrelupair_t_kernel(tc, x_bytes, x_scale, wr, wi, b, g, vr
             )
             inv_m[i] = r_tile
 
-        def gain(i):
-            for t in range(4):
+        def gain(i, slots=range(4)):
+            for t in slots:
                 nc.scalar.activation(
                     out=mg[i][:, t, :], in_=inv_m[i][:, t, :], func=ACT.Relu, scale=beta[:, t:t + 1], bias=absg[:, t:t + 1],
                 )
 
-        def affine_on_vector(i):
-            for t in range(4):
+        def affine_on_vector(i, slots):
+            for t in slots:
                 nc.vector.tensor_scalar(
                     out=mg[i][:, t, :], in0=inv_m[i][:, t, :], scalar1=beta[:, t:t + 1], scalar2=absg[:, t:t + 1],
                     op0=ALU.mult, op1=ALU.add,
                 )
 
-        def relu_on_vector(i):
-            flat = mg[i][:].rearrange("p t n -> p (t n)")
+        def relu_on_vector(i, slots):
+            flat = mg[i][:, slots.start:slots.stop, :].rearrange("p t n -> p (t n)")
             nc.vector.tensor_scalar(out=flat, in0=flat, scalar1=0.0, scalar2=None, op0=ALU.max)
 
         def hidden(i, parts=(0, 1)):
@@ -252,8 +247,7 @@ def tile_complexdensemodrelupair_t_kernel(tc, x_bytes, x_scale, wr, wi, b, g, vr
         y = {}
 
         def dense_2(i, tag="y"):
-            pool = z_ps if tag in PARTS else side_ps
-            y_bank = pool.tile([P, 2, E], F32, tag=tag)
+            y_bank = banks.tile([P, 2, E], F32, tag=tag)
             for o in range(2):
                 h_codes, h_sc = quarter(i + 2, 2 + o)
                 cols = slice((1 - o) * E, (3 - o) * E)
@@ -285,6 +279,29 @@ def tile_complexdensemodrelupair_t_kernel(tc, x_bytes, x_scale, wr, wi, b, g, vr
             group, place = divmod(first, 4)
             for o in range(2):
                 queues[o].dma_start(out=y_rows[o][:, first:first + count, :], in_=ysb[group][:, o, place:place + count, :])
+
+        def last_y(i, tags):
+            halves = []
+            for tag in tags:
+                y_half = banks.tile([P, E], F32, tag=tag, name="y_half")
+                halves.append(y_half)
+            for o in range(2):
+                h_codes, h_sc = quarter(i + 2, 2 + o)
+                for part in range(2):
+                    cols = slice((1 - o + part) * E, (2 - o + part) * E)
+                    nc.tensor.matmul_mx(
+                        out=halves[part][:],
+                        lhsT=h_codes,
+                        lhsT_scale=h_sc,
+                        rhs=v_codes[:, cols].bitcast(FP8X4),
+                        rhs_scale=v_sc[:, cols],
+                        start=(o == 0),
+                        stop=(o == 1),
+                    )
+            group, place = divmod(i, 4)
+            nc.vector.tensor_copy(out=ysb[group][:, 0, place, :], in_=halves[0][:])
+            nc.scalar.copy(out=ysb[group][:, 1, place, :], in_=halves[1][:])
+            store_y(i, 1)
 
         sgn = keep.tile([P, 4], BF16)
         absg = keep.tile([P, 4], F32)
@@ -325,8 +342,8 @@ def tile_complexdensemodrelupair_t_kernel(tc, x_bytes, x_scale, wr, wi, b, g, vr
             turn_x(i, tag)
         widen_x(D, S)
         widen_x(D, V)
-        turn_x(2, "r")
-        turn_x(3, "i")
+        turn_x(2, "r2")
+        turn_x(3, "i2")
         group_w("r", 0, 0, 64, S)
         group_w("r", 0, 64, 128, G)
         group_w("r", 1, 0, 64, S)
@@ -374,7 +391,7 @@ def tile_complexdensemodrelupair_t_kernel(tc, x_bytes, x_scale, wr, wi, b, g, vr
         hidden(0)
         quant(1, 0, 2)
 
-        for s in range(2, TILES - 3):
+        for s in range(2, TILES - 5):
             has_y = s >= 4
             square(s, 0)
             square(s, 1)
@@ -397,53 +414,79 @@ def tile_complexdensemodrelupair_t_kernel(tc, x_bytes, x_scale, wr, wi, b, g, vr
             hidden(s - 1)
             quant(s)
 
-        ta, tb, te = TILES - 3, TILES - 2, TILES - 1
-        dense_1(tb, "r", "xt")
-        square(ta, 0)
-        square(ta, 1)
-        add_squares(ta, V)
-        inverse_root(ta - 1)
-        emit_y(ta - 4, S)
-        gain(ta - 1)
-        dense_1(tb, "i")
-        dense_1(te, "r")
-        square(tb, 0)
-        hidden(ta - 1)
-        dense_1(te, "i", "r")
-        quant(ta, 2, 4)
-        dense_2(ta - 3)
-        dense_2(ta - 2, "i")
-        square(tb, 1)
-        add_squares(tb, V)
-        inverse_root(ta)
-        affine_on_vector(ta)
-        quant(tb, 2, 4)
-        relu_on_vector(ta)
-        square(te, 0)
-        square(te, 1)
-        inverse_root(tb)
-        emit_y(ta - 3, S)
-        dense_2(ta - 1)
-        gain(tb)
-        add_squares(te, V)
-        hidden(ta)
-        inverse_root(te)
-        emit_y(ta - 2, S)
-        store_y(ta - 5, 4)
-        gain(te)
-        hidden(tb)
-        quant(te, 2, 4)
-        dense_2(ta, "i")
-        quant(te + 1, 2, 4)
-        dense_2(tb, "r")
-        emit_y(ta - 1, S)
-        hidden(te)
-        emit_y(ta, S)
-        store_y(ta - 1, 2)
-        quant(te + 2, 2, 3)
-        quant(te + 2, 3, 4)
-        dense_2(te)
-        emit_y(tb, S)
-        store_y(tb, 1)
-        emit_y(te, V)
-        store_y(te, 1)
+        t27, t28, t29, t30, t31 = range(TILES - 5, TILES)
+        square(t27, 0)
+        square(t27, 1)
+        add_squares(t27, G)
+        inverse_root(t27 - 1)
+        widen_x(SCALAR_COLS, S)
+        emit_y(t27 - 4, S)
+        store_y(t27 - 7, 4)
+        dense_1(t28, "r")
+        dense_1(t28, "i")
+        scale_x(t30)
+        dense_1(t29, "r", "y")
+        turn_x(t31)
+        gain(t27 - 1)
+        hidden(t27 - 1)
+        quant(t27)
+        square(t28, 0)
+        square(t28, 1)
+        add_squares(t28, G)
+        inverse_root(t27)
+        square(t29, 0)
+        gain(t27)
+        dense_1(t29, "i", "r2")
+        dense_1(t30, "r", "i2")
+        scale_x(t31)
+        dense_1(t30, "i", "xt")
+        hidden(t27)
+        quant(t28)
+        dense_1(t31, "r", "r0")
+        dense_1(t31, "i", "i0")
+        square(t29, 1)
+        add_squares(t29, V)
+        square(t30, 0)
+        inverse_root(t28)
+        square(t30, 1)
+        add_squares(t30, V)
+        gain(t28)
+        hidden(t28)
+        dense_2(t28 - 4, "r1")
+        dense_2(t28 - 3, "i1")
+        inverse_root(t29)
+        affine_on_vector(t29, range(2, 4))
+        quant(t29, 2, 4)
+        relu_on_vector(t29, range(2, 4))
+        quant(t30, 2, 4)
+        square(t31, 0)
+        gain(t29, range(2))
+        square(t31, 1)
+        add_squares(t31, V)
+        hidden(t29)
+        inverse_root(t30)
+        emit_y(t28 - 4, S)
+        gain(t30)
+        inverse_root(t31)
+        emit_y(t28 - 3, S)
+        gain(t31)
+        dense_2(t28 - 2, "y")
+        dense_2(t27, "r2")
+        dense_2(t28, "r1")
+        hidden(t30)
+        quant(t31, 2, 4)
+        quant(t31 + 1, 2, 4)
+        emit_y(t28 - 2, S)
+        emit_y(t27, S)
+        store_y(t28 - 4, 4)
+        dense_2(t29, "i1")
+        dense_2(t30, "i2")
+        emit_y(t28, S)
+        hidden(t31)
+        emit_y(t29, S)
+        store_y(t28, 2)
+        quant(t31 + 2, 2, 3)
+        quant(t31 + 2, 3, 4)
+        emit_y(t30, S)
+        store_y(t30, 1)
+        last_y(t31, ("xt", "y"))

@@ -115,7 +115,10 @@ def tile_complexdensemodrelupair_t_kernel(tc, x_bytes, x_scale, wr, wi, b, g, vr
 
         def stage(call, half):
             if call not in staged:
-                quant_in = qin.tile([P, 2, D], BF16, align_bytes=64)
+                if call == TILES - 4:
+                    quant_in = keep.tile([P, 2, D], BF16, align_bytes=64, name="quant_in_then_m2")
+                else:
+                    quant_in = qin.tile([P, 2, D], BF16, align_bytes=64, name="quant_in")
                 staged[call] = quant_in
             return staged[call][:, half, :]
 
@@ -204,19 +207,24 @@ def tile_complexdensemodrelupair_t_kernel(tc, x_bytes, x_scale, wr, wi, b, g, vr
         mg = {}
 
         def add_squares(i, engine):
-            m2_then_gain = mh.tile([P, 4, P], F32, align_bytes=64, tag="last" if i >= TILES - 2 else "m2")
+            if i < TILES - 4:
+                m2_then_gain = mh.tile([P, 4, P], F32, align_bytes=64, tag="m2")
+            else:
+                m2_then_gain = keep.tile([P, 4, P], F32, align_bytes=64, name="quant_in_then_m2" if i == TILES - 3 else "m2_" + str(i))
             mg[i] = m2_then_gain
             engine.tensor_tensor(out=mg[i][:].rearrange("p t n -> p (t n)"), in0=sq[i][:, 0, :], in1=sq[i][:, 1, :], op=ALU.add)
 
         inv_m = {}
 
-        def inverse_root(i):
-            r_tile = hid.tile([P, 4, P], F32)
+        def inverse_root(i, slots=range(4)):
+            if slots.start == 0:
+                r_tile = hid.tile([P, 4, P], F32)
+                inv_m[i] = r_tile
             nc.scalar.activation(
-                out=r_tile[:].rearrange("p t n -> p (t n)"), in_=mg[i][:].rearrange("p t n -> p (t n)"),
+                out=inv_m[i][:, slots.start:slots.stop, :].rearrange("p t n -> p (t n)"),
+                in_=mg[i][:, slots.start:slots.stop, :].rearrange("p t n -> p (t n)"),
                 func=ACT.Abs_reciprocal_sqrt, bias=EPS,
             )
-            inv_m[i] = r_tile
 
         def gain(i, slots=range(4)):
             for t in slots:
@@ -317,12 +325,12 @@ def tile_complexdensemodrelupair_t_kernel(tc, x_bytes, x_scale, wr, wi, b, g, vr
         def prep_beta():
             nc.vector.tensor_tensor(out=beta[:], in0=absg[:], in1=b_bf[:], op=ALU.mult)
 
-        def sign_v(slot, raw, engine):
+        def sign_v(slot, raw, engine, lo=0, hi=E):
             walk = "p c j k" if engine is nc.vector else "p c k j"
             engine.tensor_tensor(
-                out=v_grp[:, slot, :, :].rearrange("p (c k) j -> " + walk, k=2),
-                in0=raw[:].rearrange("p j (c k) -> " + walk, k=2),
-                in1=sgn[:].unsqueeze(1).to_broadcast([P, E, 4]).rearrange("p (c k) j -> " + walk, k=2), op=ALU.mult,
+                out=v_grp[:, slot, lo:hi, :].rearrange("p (c k) j -> " + walk, k=2),
+                in0=raw[:, :, lo:hi].rearrange("p j (c k) -> " + walk, k=2),
+                in1=sgn[:].unsqueeze(1).to_broadcast([P, hi - lo, 4]).rearrange("p (c k) j -> " + walk, k=2), op=ALU.mult,
             )
 
         def negate_v():
@@ -349,49 +357,67 @@ def tile_complexdensemodrelupair_t_kernel(tc, x_bytes, x_scale, wr, wi, b, g, vr
         group_w("r", 1, 0, 64, S)
         group_w("r", 1, 64, 128, G)
         group_w("i", 0, 0, 128, S)
-        group_w("i", 1, 0, 40, S)
-        for i in range(3):
-            scale_x(i)
+        group_w("i", 1, 0, 56, S)
+        for i in range(3): scale_x(i)
         quant_w("r", 0)
         quant(-1)
         quant_w("r", 1)
-        group_w("i", 1, 40, 128, V)
+        group_w("i", 1, 56, 128, V)
         quant_w("i", 0)
         quant_w("i", 1)
         dense_1(0, "r")
         dense_1(0, "i")
         dense_1(1, "r")
-        widen_x(D, S)
-        prep_signs()
-        turn_x(4)
         dense_1(1, "i")
+        prep_signs()
+        widen_x(D, S)
+        turn_x(4)
         scale_x(3)
-        sign_v(2, vi_raw, G)
+        sign_v(2, vi_raw, G, 0, 104)
+        sign_v(2, vi_raw, V, 104, E)
         sign_v(1, vr_raw, V)
+        prep_beta()
+        negate_v()
         square(0, 0)
-        widen_x(D + D // 2, S)
+        widen_x(1888, S)
         square(0, 1)
         add_squares(0, V)
         quant(0)
-        negate_v()
-        prep_beta()
         quant_v(1, 3)
         quant_v(0, 1)
         scale_x(4)
         dense_1(2, "r")
         dense_1(2, "i")
+        widen_x(96, S)
         square(1, 0)
-        widen_x(7 * D // 8, S)
-        inverse_root(0)
+        widen_x(96, S)
         square(1, 1)
+        inverse_root(0, range(0, 2))
+        inverse_root(0, range(2, 4))
         add_squares(1, G)
         gain(0)
-        widen_x(3 * D // 8, G)
+        widen_x(640, S)
+        widen_x(384, G)
         turn_x(5)
         hidden(0)
         quant(1, 0, 2)
+        square(2, 0)
+        widen_x(128, S)
+        square(2, 1)
+        add_squares(2, G)
+        inverse_root(1, range(0, 2))
+        inverse_root(1, range(2, 4))
+        dense_1(3, "r")
+        dense_1(3, "i")
+        scale_x(5)
+        gain(1)
+        widen_x(320, S)
+        turn_x(6)
+        widen_x(704, G)
+        hidden(1)
+        quant(2)
 
-        for s in range(2, TILES - 5):
+        for s in range(3, TILES - 5):
             has_y = s >= 4
             square(s, 0)
             square(s, 1)
@@ -400,7 +426,7 @@ def tile_complexdensemodrelupair_t_kernel(tc, x_bytes, x_scale, wr, wi, b, g, vr
             dense_1(s + 1, "r")
             dense_1(s + 1, "i")
             scale_x(s + 3)
-            widen_x(SCALAR_COLS if has_y else 2 * SCALAR_COLS, nc.scalar)
+            widen_x(SCALAR_COLS if has_y else 544, nc.scalar)
             if has_y:
                 emit_y(s - 4, nc.scalar)
                 if s % 4 == 3:
@@ -428,8 +454,9 @@ def tile_complexdensemodrelupair_t_kernel(tc, x_bytes, x_scale, wr, wi, b, g, vr
         dense_1(t29, "r", "y")
         turn_x(t31)
         gain(t27 - 1)
-        hidden(t27 - 1)
+        hidden(t27 - 1, (0,))
         quant(t27)
+        hidden(t27 - 1, (1,))
         square(t28, 0)
         square(t28, 1)
         add_squares(t28, G)
@@ -440,49 +467,54 @@ def tile_complexdensemodrelupair_t_kernel(tc, x_bytes, x_scale, wr, wi, b, g, vr
         dense_1(t30, "r", "i2")
         scale_x(t31)
         dense_1(t30, "i", "xt")
-        hidden(t27)
+        hidden(t27, (0,))
         quant(t28)
+        hidden(t27, (1,))
         dense_1(t31, "r", "r0")
         dense_1(t31, "i", "i0")
         square(t29, 1)
-        add_squares(t29, V)
-        square(t30, 0)
-        inverse_root(t28)
-        square(t30, 1)
-        add_squares(t30, V)
+        add_squares(t29, G)
+        inverse_root(t28, range(0, 2))
+        inverse_root(t28, range(2, 4))
         gain(t28)
+        square(t30, 0)
+        square(t30, 1)
         hidden(t28)
+        add_squares(t30, V)
         dense_2(t28 - 4, "r1")
         dense_2(t28 - 3, "i1")
-        inverse_root(t29)
-        affine_on_vector(t29, range(2, 4))
-        quant(t29, 2, 4)
-        relu_on_vector(t29, range(2, 4))
-        quant(t30, 2, 4)
         square(t31, 0)
-        gain(t29, range(2))
+        inverse_root(t29)
+        quant(t29, 2, 4)
+        quant(t30, 2, 4)
+        affine_on_vector(t29, range(2, 4))
+        relu_on_vector(t29, range(2, 4))
         square(t31, 1)
+        gain(t29, range(2))
         add_squares(t31, V)
         hidden(t29)
-        inverse_root(t30)
-        emit_y(t28 - 4, S)
+        inverse_root(t30, range(0, 2))
+        inverse_root(t30, range(2, 4))
         gain(t30)
-        inverse_root(t31)
-        emit_y(t28 - 3, S)
+        inverse_root(t31, range(0, 2))
+        inverse_root(t31, range(2, 4))
         gain(t31)
+        emit_y(t28 - 4, S)
+        emit_y(t28 - 3, S)
         dense_2(t28 - 2, "y")
         dense_2(t27, "r2")
         dense_2(t28, "r1")
         hidden(t30)
         quant(t31, 2, 4)
-        quant(t31 + 1, 2, 4)
         emit_y(t28 - 2, S)
         emit_y(t27, S)
         store_y(t28 - 4, 4)
         dense_2(t29, "i1")
-        dense_2(t30, "i2")
         emit_y(t28, S)
-        hidden(t31)
+        hidden(t31, (0,))
+        quant(t31 + 1, 2, 4)
+        hidden(t31, (1,))
+        dense_2(t30, "i2")
         emit_y(t29, S)
         store_y(t28, 2)
         quant(t31 + 2, 2, 3)

@@ -23,22 +23,23 @@ GROUPS = F // 4
 EPS = 1e-6
 SIGN_OF_ZERO = 1e-38
 PARTS = ("r", "i")
-SCALAR_COLS = 320
+SCALAR_COLS = 336
 GPSIMD_COLS = 640
 
 
 def tile_complexdensemodrelupair_t_kernel(tc, x_bytes, x_scale, wr, wi, b, g, vr, vi, out_r, out_i):
     nc = tc.nc
+    V, S, G = nc.vector, nc.scalar, nc.gpsimd
     x_rows = x_bytes.rearrange("(p i) k -> p (i k)", p=P)
     y_rows = [out_r.rearrange("(p i) e -> p i e", p=P), out_i.rearrange("(p i) e -> p i e", p=P)]
 
     with ExitStack() as ctx:
         keep = ctx.enter_context(tc.tile_pool(name="keep", bufs=1))
-        qin = ctx.enter_context(tc.tile_pool(name="qin", bufs=3))
-        qout = ctx.enter_context(tc.tile_pool(name="qout", bufs=8))
-        wgp = ctx.enter_context(tc.tile_pool(name="wgp", bufs=1))
-        mh = ctx.enter_context(tc.tile_pool(name="mh", bufs=2))
-        hid = ctx.enter_context(tc.tile_pool(name="hid", bufs=3))
+        stage = ctx.enter_context(tc.tile_pool(name="stage", bufs=3))
+        xq = ctx.enter_context(tc.tile_pool(name="xq", bufs=4))
+        hq = ctx.enter_context(tc.tile_pool(name="hq", bufs=8))
+        mid = ctx.enter_context(tc.tile_pool(name="mid", bufs=3))
+        gains = ctx.enter_context(tc.tile_pool(name="gains", bufs=4))
         outp = ctx.enter_context(tc.tile_pool(name="outp", bufs=3))
         banks = ctx.enter_context(tc.psum_pool(name="banks", bufs=1))
         ctx.enter_context(tc.manual_schedule())
@@ -52,8 +53,7 @@ def tile_complexdensemodrelupair_t_kernel(tc, x_bytes, x_scale, wr, wi, b, g, vr
         w_raw = {}
 
         def load_w(part, src, kp):
-            name = "w_raw_" + part + str(kp)
-            w_rows = keep.tile([P, 4, F], BF16, name=name)
+            w_rows = keep.tile([P, 4, F], BF16, name="w_raw_" + part + str(kp))
             nc.sync.dma_start(out=w_rows[:], in_=src[kp * K_PASS:(kp + 1) * K_PASS, :].rearrange("(p j) c -> p j c", j=4))
             w_raw[part, kp] = w_rows
 
@@ -80,8 +80,8 @@ def tile_complexdensemodrelupair_t_kernel(tc, x_bytes, x_scale, wr, wi, b, g, vr
             load_x(first, 4)
 
         warm = keep.tile([P, 1], F32)
-        nc.vector.memset(warm[:], 1.0)
-        nc.scalar.activation(out=warm[:], in_=warm[:], func=ACT.Abs_reciprocal_sqrt)
+        V.memset(warm[:], 1.0)
+        S.activation(out=warm[:], in_=warm[:], func=ACT.Abs_reciprocal_sqrt)
         ident = keep.tile([P, P], F32)
         make_identity(nc, ident[:])
 
@@ -94,199 +94,207 @@ def tile_complexdensemodrelupair_t_kernel(tc, x_bytes, x_scale, wr, wi, b, g, vr
             widened.remove(cols.start)
             if cols.start == cols.stop:
                 return
-            if engine is nc.scalar:
-                nc.scalar.copy(out=xb[:, cols], in_=x8[:, cols].bitcast(FP8))
+            if engine is S:
+                S.copy(out=xb[:, cols], in_=x8[:, cols].bitcast(FP8))
             else:
                 engine.tensor_copy(out=xb[:, cols], in_=x8[:, cols].bitcast(FP8))
 
         xt = {}
 
-        def turn_x(i, tag="xt"):
+        def turn_x(i, tag="xt", passes=range(PASSES)):
             assert widened[0] >= (i + 1) * D
             words = xb[:].bitcast(F32)
-            bank = banks.tile([P, 2, PASSES, P], F32, tag=tag, name="xt_bank")
-            for kp in range(PASSES):
+            if i not in xt:
+                xt_bank = banks.tile([P, 2, PASSES, P], F32, tag=tag, name="xt_bank")
+                xt[i] = xt_bank
+            for kp in passes:
                 for u in range(2):
                     first = (i * D + kp * K_PASS) // 2
-                    nc.tensor.transpose(bank[:, u, kp, :], words[:, first + u:first + K_PASS // 2:2], ident[:])
-            xt[i] = bank
+                    nc.tensor.transpose(xt[i][:, u, kp, :], words[:, first + u:first + K_PASS // 2:2], ident[:])
 
-        staged = {}
-
-        def stage(call, half):
-            if call not in staged:
-                if call == TILES - 4:
-                    quant_in = keep.tile([P, 2, D], BF16, align_bytes=64, name="quant_in_then_m2")
-                else:
-                    quant_in = qin.tile([P, 2, D], BF16, align_bytes=64, name="quant_in")
-                staged[call] = quant_in
-            return staged[call][:, half, :]
-
-        def x_place(i):
-            return (i // 2 - 1, i % 2) if i < 4 else (i - 3, 0)
+        x_in = {}
 
         def scale_x(i):
-            nc.vector.tensor_tensor(
-                out=stage(*x_place(i)).rearrange("p (q n u e) -> p q n u e", q=PASSES, u=2, e=2),
+            x_scaled = stage.tile([P, D], BF16, align_bytes=64, name="x_scaled")
+            V.tensor_tensor(
+                out=x_scaled[:].rearrange("p (q n u e) -> p q n u e", q=PASSES, u=2, e=2),
                 in0=xt[i][:].rearrange("p u q n -> p (u q n)").bitcast(BF16).rearrange("p (u q n e) -> p q n u e", u=2, q=PASSES, e=2),
                 in1=xs[:].unsqueeze(2).to_broadcast([P, PASSES, P, 4]).rearrange("p q n (u e) -> p q n u e", u=2),
                 op=ALU.mult,
             )
+            x_in[i] = x_scaled
 
-        quantised = {}
+        def quantise(codes, scales, values):
+            V.quantize_mx(out=codes.bitcast(FP8X4), scales=scales, in_=values)
 
-        def quant(call, lo=0, hi=4):
-            if call not in quantised:
-                codes = qout.tile([P, 4 * P], U32, align_bytes=64)
-                scales = qout.tile([P, 4 * P], U8, align_bytes=64)
-                quantised[call] = (codes, scales)
-            codes, scales = quantised[call]
-            nc.vector.quantize_mx(
-                out=codes[:, lo * P:hi * P].bitcast(FP8X4), scales=scales[:, lo * P:hi * P],
-                in_=staged[call][:].rearrange("p a c -> p (a c)")[:, lo * K_PASS:hi * K_PASS],
-            )
+        x_mx = {}
 
-        def quarter(call, n):
-            codes, scales = quantised[call]
-            return codes[:, n * P:(n + 1) * P].bitcast(FP8X4), scales[:, n * P:(n + 1) * P]
+        def quant_x(i):
+            x_codes = xq.tile([P, PASSES * P], U32, align_bytes=64, name="x_codes")
+            x_sc = xq.tile([P, PASSES * P], U8, align_bytes=64, name="x_sc")
+            quantise(x_codes[:], x_sc[:], x_in[i][:])
+            x_mx[i] = (x_codes, x_sc)
 
         w_grp = {}
-        wc = {}
+        w_mx = {}
 
         def group_w(part, kp, lo, hi, engine):
             if (part, kp) not in w_grp:
-                w_grouped = wgp.tile([P, 4 * F], BF16, align_bytes=64, name="w_grouped_" + part + str(kp))
+                w_grouped = keep.tile([P, 4 * F], BF16, align_bytes=64, name="w_grouped_" + part + str(kp))
                 w_grp[part, kp] = w_grouped
-            if engine is nc.gpsimd:
+            if engine is G:
                 dst = w_grp[part, kp][:].rearrange("p (t m j) -> p m t j", t=4, j=4)[:, lo:hi]
                 src = w_raw[part, kp][:].rearrange("p j (m t) -> p m t j", t=4)[:, lo:hi]
-                nc.gpsimd.tensor_scalar(out=dst, in0=src, scalar1=1.0, scalar2=0.0, op0=ALU.mult, op1=ALU.add)
+                G.tensor_scalar(out=dst, in0=src, scalar1=1.0, scalar2=0.0, op0=ALU.mult, op1=ALU.add)
                 return
             dst = w_grp[part, kp][:].rearrange("p (t m k j) -> p m t k j", t=4, k=2, j=4)[:, lo // 2:hi // 2]
             src = w_raw[part, kp][:].rearrange("p j (m k t) -> p m t k j", k=2, t=4)[:, lo // 2:hi // 2]
-            if engine is nc.vector:
-                nc.vector.tensor_copy(out=dst, in_=src)
+            if engine is V:
+                V.tensor_copy(out=dst, in_=src)
             else:
-                nc.scalar.copy(out=dst, in_=src)
+                S.copy(out=dst, in_=src)
 
         def quant_w(part, kp):
             w_codes = keep.tile([P, F], U32, align_bytes=64, name="w_codes_" + part + str(kp))
             w_sc = keep.tile([P, F], U8, align_bytes=64, name="w_sc_" + part + str(kp))
-            nc.vector.quantize_mx(out=w_codes[:].bitcast(FP8X4), scales=w_sc[:], in_=w_grp[part, kp][:])
-            wc[part, kp] = (w_codes, w_sc)
+            quantise(w_codes[:], w_sc[:], w_grp[part, kp][:])
+            w_mx[part, kp] = (w_codes, w_sc)
 
         z = {}
 
-        def dense_1(i, part, tag=None):
-            bank = banks.tile([P, 4, P], F32, tag=tag or part + str(i % 3), name="z_bank")
-            call, half = x_place(i)
+        def dense_1(i, o, tag=None):
+            bank = banks.tile([P, 4, P], F32, tag=tag or PARTS[o] + str(i % 3), name="z_bank")
+            x_codes, x_sc = x_mx[i]
             for kp in range(PASSES):
-                w_codes, w_sc = wc[part, kp]
-                x_codes, x_sc = quarter(call, 2 * half + kp)
+                w_codes, w_sc = w_mx[PARTS[o], kp]
+                tokens = slice(kp * P, (kp + 1) * P)
                 for t in range(4):
                     channels = slice(t * P, (t + 1) * P)
                     nc.tensor.matmul_mx(
                         out=bank[:, t, :],
                         lhsT=w_codes[:, channels].bitcast(FP8X4),
                         lhsT_scale=w_sc[:, channels],
-                        rhs=x_codes,
-                        rhs_scale=x_sc,
+                        rhs=x_codes[:, tokens].bitcast(FP8X4),
+                        rhs_scale=x_sc[:, tokens],
                         start=(kp == 0 and t == 0),
                         stop=(kp == PASSES - 1 and t == 3),
                     )
-            z[i, part] = bank
+            z[i, o] = bank
 
         sq = {}
 
         def square(i, o):
-            if o == 0:
-                sq_pair = hid.tile([P, 2, F], F32)
+            if i not in sq:
+                sq_pair = mid.tile([P, 2, F], F32, name="sq_pair")
                 sq[i] = sq_pair
-            nc.scalar.activation(out=sq[i][:, o, :], in_=z[i, PARTS[o]][:].rearrange("p t n -> p (t n)"), func=ACT.Square)
+            S.activation(out=sq[i][:, o, :], in_=z[i, o][:].rearrange("p t n -> p (t n)"), func=ACT.Square)
 
         mg = {}
 
-        def add_squares(i, engine):
-            if i < TILES - 4:
-                m2_then_gain = mh.tile([P, 4, P], F32, align_bytes=64, tag="m2")
+        def add_squares(i, engine, tag=None):
+            if tag is None:
+                m2_then_gain = gains.tile([P, 4, P], F32, align_bytes=64, name="m2_then_gain")
             else:
-                m2_then_gain = keep.tile([P, 4, P], F32, align_bytes=64, name="quant_in_then_m2" if i == TILES - 3 else "m2_" + str(i))
+                m2_then_gain = keep.tile([P, 4, P], F32, align_bytes=64, name=tag)
             mg[i] = m2_then_gain
             engine.tensor_tensor(out=mg[i][:].rearrange("p t n -> p (t n)"), in0=sq[i][:, 0, :], in1=sq[i][:, 1, :], op=ALU.add)
 
         inv_m = {}
 
-        def inverse_root(i, slots=range(4)):
-            if slots.start == 0:
-                r_tile = hid.tile([P, 4, P], F32)
-                inv_m[i] = r_tile
-            nc.scalar.activation(
-                out=inv_m[i][:, slots.start:slots.stop, :].rearrange("p t n -> p (t n)"),
-                in_=mg[i][:, slots.start:slots.stop, :].rearrange("p t n -> p (t n)"),
-                func=ACT.Abs_reciprocal_sqrt, bias=EPS,
-            )
+        def inverse_root(i, halves=1):
+            r_tile = mid.tile([P, F], F32, name="r_tile")
+            inv_m[i] = r_tile
+            for half in range(halves):
+                cols = slice(half * F // halves, (half + 1) * F // halves)
+                S.activation(
+                    out=r_tile[:, cols], in_=mg[i][:].rearrange("p t n -> p (t n)")[:, cols],
+                    func=ACT.Abs_reciprocal_sqrt, bias=EPS,
+                )
 
         def gain(i, slots=range(4)):
             for t in slots:
-                nc.scalar.activation(
-                    out=mg[i][:, t, :], in_=inv_m[i][:, t, :], func=ACT.Relu, scale=beta[:, t:t + 1], bias=absg[:, t:t + 1],
+                S.activation(
+                    out=mg[i][:, t, :], in_=inv_m[i][:, t * P:(t + 1) * P], func=ACT.Relu,
+                    scale=beta[:, t:t + 1], bias=absg[:, t:t + 1],
                 )
 
         def affine_on_vector(i, slots):
             for t in slots:
-                nc.vector.tensor_scalar(
-                    out=mg[i][:, t, :], in0=inv_m[i][:, t, :], scalar1=beta[:, t:t + 1], scalar2=absg[:, t:t + 1],
+                V.tensor_scalar(
+                    out=mg[i][:, t, :], in0=inv_m[i][:, t * P:(t + 1) * P], scalar1=beta[:, t:t + 1], scalar2=absg[:, t:t + 1],
                     op0=ALU.mult, op1=ALU.add,
                 )
 
         def relu_on_vector(i, slots):
             flat = mg[i][:, slots.start:slots.stop, :].rearrange("p t n -> p (t n)")
-            nc.vector.tensor_scalar(out=flat, in0=flat, scalar1=0.0, scalar2=None, op0=ALU.max)
+            V.tensor_scalar(out=flat, in0=flat, scalar1=0.0, scalar2=None, op0=ALU.max)
 
-        def hidden(i, parts=(0, 1)):
-            for o in parts:
-                nc.vector.tensor_tensor(
-                    out=stage(i + 2, 1)[:, o * F:(o + 1) * F].rearrange("p (c k t) -> p c t k", k=2, t=4),
-                    in0=z[i, PARTS[o]][:].rearrange("p t (c k) -> p c t k", k=2),
-                    in1=mg[i][:].rearrange("p t (c k) -> p c t k", k=2),
-                    op=ALU.mult,
-                )
+        h_in = {}
+        h_run = {}
+
+        def stage_h(first, count):
+            h_tile = stage.tile([P, count * 2 * F], BF16, align_bytes=64, name="h_tile")
+            h_run[first] = h_tile
+            for n in range(count):
+                h_in[first + n] = h_tile[:, n * 2 * F:(n + 1) * 2 * F]
+
+        def hidden(i, o):
+            if i not in h_in:
+                stage_h(i, 1)
+            V.tensor_tensor(
+                out=h_in[i][:, o * F:(o + 1) * F].rearrange("p (c k t) -> p c t k", k=2, t=4),
+                in0=z[i, o][:].rearrange("p t (c k) -> p c t k", k=2),
+                in1=mg[i][:].rearrange("p t (c k) -> p c t k", k=2),
+                op=ALU.mult,
+            )
+
+        h_mx = {}
+
+        def quant_h(first, count=1, lo=0, hi=None):
+            hi = 2 * count if hi is None else hi
+            if first not in h_mx:
+                h_codes = hq.tile([P, count * 2 * P], U32, align_bytes=64, name="h_codes")
+                h_sc = hq.tile([P, count * 2 * P], U8, align_bytes=64, name="h_sc")
+                for n in range(count):
+                    h_mx[first + n] = (h_codes, h_sc, 2 * n)
+            h_codes, h_sc, start = h_mx[first]
+            quantise(h_codes[:, lo * P:hi * P], h_sc[:, lo * P:hi * P], h_run[first][:, lo * F:hi * F])
 
         y = {}
 
+        def product_2(out, i, o, cols):
+            h_codes, h_sc, start = h_mx[i]
+            tokens = slice((start + o) * P, (start + o + 1) * P)
+            nc.tensor.matmul_mx(
+                out=out, lhsT=h_codes[:, tokens].bitcast(FP8X4), lhsT_scale=h_sc[:, tokens],
+                rhs=v_codes[:, cols].bitcast(FP8X4), rhs_scale=v_sc[:, cols], start=(o == 0), stop=(o == 1),
+            )
+
         def dense_2(i, tag="y"):
-            y_bank = banks.tile([P, 2, E], F32, tag=tag)
+            y_bank = banks.tile([P, 2, E], F32, tag=tag, name="y_bank")
             for o in range(2):
-                h_codes, h_sc = quarter(i + 2, 2 + o)
-                cols = slice((1 - o) * E, (3 - o) * E)
-                nc.tensor.matmul_mx(
-                    out=y_bank[:].rearrange("p o e -> p (o e)"),
-                    lhsT=h_codes,
-                    lhsT_scale=h_sc,
-                    rhs=v_codes[:, cols].bitcast(FP8X4),
-                    rhs_scale=v_sc[:, cols],
-                    start=(o == 0),
-                    stop=(o == 1),
-                )
+                product_2(y_bank[:].rearrange("p o e -> p (o e)"), i, o, slice((1 - o) * E, (3 - o) * E))
             y[i] = y_bank
 
         ysb = {}
 
-        def emit_y(i, engine):
+        def y_tile(i):
             group, place = divmod(i, 4)
-            if place == 0:
-                y_tile = outp.tile([P, 2, 4, E], F32)
-                ysb[group] = y_tile
-            dst = ysb[group][:, :, place, :]
-            if engine is nc.scalar:
-                nc.scalar.copy(out=dst, in_=y[i][:])
-            else:
-                nc.vector.tensor_copy(out=dst, in_=y[i][:])
+            if group not in ysb:
+                y_group = outp.tile([P, 2, 4, E], F32, name="y_group")
+                ysb[group] = y_group
+            return ysb[group][:, :, place, :]
 
-        def store_y(first, count, queues=(nc.sync, nc.sync)):
+        def emit_y(i, engine=S):
+            if engine is S:
+                S.copy(out=y_tile(i), in_=y[i][:])
+            else:
+                V.tensor_copy(out=y_tile(i), in_=y[i][:])
+
+        def store_y(first, count):
             group, place = divmod(first, 4)
             for o in range(2):
-                queues[o].dma_start(out=y_rows[o][:, first:first + count, :], in_=ysb[group][:, o, place:place + count, :])
+                nc.sync.dma_start(out=y_rows[o][:, first:first + count, :], in_=ysb[group][:, o, place:place + count, :])
 
         def last_y(i, tags):
             halves = []
@@ -294,39 +302,28 @@ def tile_complexdensemodrelupair_t_kernel(tc, x_bytes, x_scale, wr, wi, b, g, vr
                 y_half = banks.tile([P, E], F32, tag=tag, name="y_half")
                 halves.append(y_half)
             for o in range(2):
-                h_codes, h_sc = quarter(i + 2, 2 + o)
                 for part in range(2):
-                    cols = slice((1 - o + part) * E, (2 - o + part) * E)
-                    nc.tensor.matmul_mx(
-                        out=halves[part][:],
-                        lhsT=h_codes,
-                        lhsT_scale=h_sc,
-                        rhs=v_codes[:, cols].bitcast(FP8X4),
-                        rhs_scale=v_sc[:, cols],
-                        start=(o == 0),
-                        stop=(o == 1),
-                    )
-            group, place = divmod(i, 4)
-            nc.vector.tensor_copy(out=ysb[group][:, 0, place, :], in_=halves[0][:])
-            nc.scalar.copy(out=ysb[group][:, 1, place, :], in_=halves[1][:])
+                    product_2(halves[part][:], i, o, slice((1 - o + part) * E, (2 - o + part) * E))
+            V.tensor_copy(out=y_tile(i)[:, 0, :], in_=halves[0][:])
+            S.copy(out=y_tile(i)[:, 1, :], in_=halves[1][:])
             store_y(i, 1)
 
         sgn = keep.tile([P, 4], BF16)
         absg = keep.tile([P, 4], F32)
         beta = keep.tile([P, 4], F32)
-        v_grp = mh.tile([P, 3, E, 4], BF16, align_bytes=64, tag="m2")
+        v_grp = keep.tile([P, 3, E, 4], BF16, align_bytes=64, name="v_grp_then_m2")
         v_codes = keep.tile([P, 3 * E], U32, align_bytes=64)
         v_sc = keep.tile([P, 3 * E], U8, align_bytes=64)
 
         def prep_signs():
-            nc.scalar.activation(out=sgn[:], in_=g_bf[:], func=ACT.Sign, bias=SIGN_OF_ZERO)
-            nc.scalar.activation(out=absg[:], in_=g_bf[:], func=ACT.Abs)
+            S.activation(out=sgn[:], in_=g_bf[:], func=ACT.Sign, bias=SIGN_OF_ZERO)
+            S.activation(out=absg[:], in_=g_bf[:], func=ACT.Abs)
 
         def prep_beta():
-            nc.vector.tensor_tensor(out=beta[:], in0=absg[:], in1=b_bf[:], op=ALU.mult)
+            V.tensor_tensor(out=beta[:], in0=absg[:], in1=b_bf[:], op=ALU.mult)
 
         def sign_v(slot, raw, engine, lo=0, hi=E):
-            walk = "p c j k" if engine is nc.vector else "p c k j"
+            walk = "p c j k" if engine is V else "p c k j"
             engine.tensor_tensor(
                 out=v_grp[:, slot, lo:hi, :].rearrange("p (c k) j -> " + walk, k=2),
                 in0=raw[:, :, lo:hi].rearrange("p j (c k) -> " + walk, k=2),
@@ -334,191 +331,180 @@ def tile_complexdensemodrelupair_t_kernel(tc, x_bytes, x_scale, wr, wi, b, g, vr
             )
 
         def negate_v():
-            nc.vector.tensor_scalar(out=v_grp[:, 0, :, :], in0=v_grp[:, 2, :, :], scalar1=-1.0, scalar2=None, op0=ALU.mult)
+            V.tensor_scalar(out=v_grp[:, 0, :, :], in0=v_grp[:, 2, :, :], scalar1=-1.0, scalar2=None, op0=ALU.mult)
 
         def quant_v(lo, hi):
             cols = slice(lo * E, hi * E)
-            nc.vector.quantize_mx(
-                out=v_codes[:, cols].bitcast(FP8X4), scales=v_sc[:, cols],
-                in_=v_grp[:, lo:hi, :, :].rearrange("p o e j -> p (o e j)"),
-            )
+            quantise(v_codes[:, cols], v_sc[:, cols], v_grp[:, lo:hi, :, :].rearrange("p o e j -> p (o e j)"))
 
-        V, S, G = nc.vector, nc.scalar, nc.gpsimd
-        for i, tag in ((0, "xt"), (1, "y")):
-            widen_x(D // 2, S)
-            widen_x(D // 2, V)
-            turn_x(i, tag)
+        widen_x(D // 2, S)
+        widen_x(D // 2, V)
+        turn_x(0, "xt")
+        widen_x(D // 2, S)
+        widen_x(D // 2, V)
+        turn_x(1, "y")
         widen_x(D, S)
         widen_x(D, V)
         turn_x(2, "r2")
-        turn_x(3, "i2")
         group_w("r", 0, 0, 64, S)
         group_w("r", 0, 64, 128, G)
-        group_w("r", 1, 0, 64, S)
-        group_w("r", 1, 64, 128, G)
-        group_w("i", 0, 0, 128, S)
-        group_w("i", 1, 0, 56, S)
-        for i in range(3): scale_x(i)
+        group_w("r", 1, 0, 112, S)
+        group_w("r", 1, 112, 128, G)
+        group_w("i", 0, 0, 96, S)
+        group_w("i", 1, 0, 24, S)
+        scale_x(0)
+        turn_x(3, "xt")
+        scale_x(1)
         quant_w("r", 0)
-        quant(-1)
+        quant_x(0)
+        quant_x(1)
+        group_w("i", 0, 96, 128, V)
         quant_w("r", 1)
-        group_w("i", 1, 56, 128, V)
+        group_w("i", 1, 24, 128, V)
         quant_w("i", 0)
         quant_w("i", 1)
-        dense_1(0, "r")
-        dense_1(0, "i")
-        dense_1(1, "r")
-        dense_1(1, "i")
+        dense_1(0, 0)
+        dense_1(1, 0)
+        dense_1(0, 1)
+        dense_1(1, 1)
         prep_signs()
-        widen_x(D, S)
-        turn_x(4)
-        scale_x(3)
+        scale_x(2)
         sign_v(2, vi_raw, G, 0, 104)
         sign_v(2, vi_raw, V, 104, E)
         sign_v(1, vr_raw, V)
-        prep_beta()
-        negate_v()
+        quant_x(2)
+        widen_x(D, S)
         square(0, 0)
-        widen_x(1888, S)
+        widen_x(384, S)
+        square(1, 0)
+        widen_x(384, S)
         square(0, 1)
         add_squares(0, V)
-        quant(0)
+        prep_beta()
+        negate_v()
+        dense_1(2, 0)
+        turn_x(4, "y", range(0, 1))
+        dense_1(2, 1)
+        turn_x(4, "y", range(1, 2))
+        square(1, 1)
+        widen_x(896, S)
         quant_v(1, 3)
         quant_v(0, 1)
-        scale_x(4)
-        dense_1(2, "r")
-        dense_1(2, "i")
-        widen_x(96, S)
-        square(1, 0)
-        widen_x(96, S)
-        square(1, 1)
-        inverse_root(0, range(0, 2))
-        inverse_root(0, range(2, 4))
-        add_squares(1, G)
+        add_squares(1, G, "v_grp_then_m2")
+        inverse_root(0, 2)
         gain(0)
-        widen_x(640, S)
-        widen_x(384, G)
+        scale_x(3)
         turn_x(5)
-        hidden(0)
-        quant(1, 0, 2)
+        hidden(0, 0)
+        quant_x(3)
+        dense_1(3, 0)
+        hidden(0, 1)
+        dense_1(3, 1)
         square(2, 0)
-        widen_x(128, S)
         square(2, 1)
         add_squares(2, G)
-        inverse_root(1, range(0, 2))
-        inverse_root(1, range(2, 4))
-        dense_1(3, "r")
-        dense_1(3, "i")
-        scale_x(5)
+        widen_x(448, G)
+        inverse_root(1, 2)
         gain(1)
-        widen_x(320, S)
-        turn_x(6)
-        widen_x(704, G)
-        hidden(1)
-        quant(2)
+        widen_x(384, S)
+        square(3, 0)
+        widen_x(64, S)
+        square(3, 1)
+        add_squares(3, G)
+        inverse_root(2)
+        widen_x(704, S)
+        widen_x(GPSIMD_COLS, G)
+        gain(2)
 
-        for s in range(3, TILES - 5):
-            has_y = s >= 4
-            square(s, 0)
-            square(s, 1)
-            add_squares(s, nc.gpsimd)
-            inverse_root(s - 1)
-            dense_1(s + 1, "r")
-            dense_1(s + 1, "i")
-            scale_x(s + 3)
-            widen_x(SCALAR_COLS if has_y else 544, nc.scalar)
-            if has_y:
-                emit_y(s - 4, nc.scalar)
-                if s % 4 == 3:
-                    store_y(s - 7, 4)
-            if s >= 3:
-                dense_2(s - 3)
-            if s + 4 < TILES:
-                turn_x(s + 4)
-            widen_x(GPSIMD_COLS, nc.gpsimd)
-            gain(s - 1)
-            hidden(s - 1)
-            quant(s)
+        for c in range(4, 29):
+            scale_x(c)
+            if c > 4:
+                turn_x(c + 1)
+            hidden(c - 3, 0)
+            quant_x(c)
+            if c >= 4:
+                quant_h(c - 4)
+            dense_1(c, 0)
+            hidden(c - 3, 1)
+            dense_1(c, 1)
+            square(c, 0)
+            widen_x(SCALAR_COLS, S)
+            square(c, 1)
+            add_squares(c, G)
+            widen_x(GPSIMD_COLS, G)
+            inverse_root(c - 1)
+            if c >= 4:
+                dense_2(c - 4)
+                emit_y(c - 4)
+                if c % 4 == 3:
+                    store_y(c - 7, 4)
+            gain(c - 1)
 
-        t27, t28, t29, t30, t31 = range(TILES - 5, TILES)
-        square(t27, 0)
-        square(t27, 1)
-        add_squares(t27, G)
-        inverse_root(t27 - 1)
-        widen_x(SCALAR_COLS, S)
-        emit_y(t27 - 4, S)
-        store_y(t27 - 7, 4)
-        dense_1(t28, "r")
-        dense_1(t28, "i")
-        scale_x(t30)
-        dense_1(t29, "r", "y")
-        turn_x(t31)
-        gain(t27 - 1)
-        hidden(t27 - 1, (0,))
-        quant(t27)
-        hidden(t27 - 1, (1,))
-        square(t28, 0)
-        square(t28, 1)
-        add_squares(t28, G)
-        inverse_root(t27)
-        square(t29, 0)
-        gain(t27)
-        dense_1(t29, "i", "r2")
-        dense_1(t30, "r", "i2")
-        scale_x(t31)
-        dense_1(t30, "i", "xt")
-        hidden(t27, (0,))
-        quant(t28)
-        hidden(t27, (1,))
-        dense_1(t31, "r", "r0")
-        dense_1(t31, "i", "i0")
-        square(t29, 1)
-        add_squares(t29, G)
-        inverse_root(t28, range(0, 2))
-        inverse_root(t28, range(2, 4))
-        gain(t28)
-        square(t30, 0)
-        square(t30, 1)
-        hidden(t28)
-        add_squares(t30, V)
-        dense_2(t28 - 4, "r1")
-        dense_2(t28 - 3, "i1")
-        square(t31, 0)
-        inverse_root(t29)
-        quant(t29, 2, 4)
-        quant(t30, 2, 4)
-        affine_on_vector(t29, range(2, 4))
-        relu_on_vector(t29, range(2, 4))
-        square(t31, 1)
-        gain(t29, range(2))
-        add_squares(t31, V)
-        hidden(t29)
-        inverse_root(t30, range(0, 2))
-        inverse_root(t30, range(2, 4))
-        gain(t30)
-        inverse_root(t31, range(0, 2))
-        inverse_root(t31, range(2, 4))
-        gain(t31)
-        emit_y(t28 - 4, S)
-        emit_y(t28 - 3, S)
-        dense_2(t28 - 2, "y")
-        dense_2(t27, "r2")
-        dense_2(t28, "r1")
-        hidden(t30)
-        quant(t31, 2, 4)
-        emit_y(t28 - 2, S)
-        emit_y(t27, S)
-        store_y(t28 - 4, 4)
-        dense_2(t29, "i1")
-        emit_y(t28, S)
-        hidden(t31, (0,))
-        quant(t31 + 1, 2, 4)
-        hidden(t31, (1,))
-        dense_2(t30, "i2")
-        emit_y(t29, S)
-        store_y(t28, 2)
-        quant(t31 + 2, 2, 3)
-        quant(t31 + 2, 3, 4)
-        emit_y(t30, S)
-        store_y(t30, 1)
-        last_y(t31, ("xt", "y"))
+        scale_x(29)
+        turn_x(30)
+        stage_h(26, 2)
+        hidden(26, 0)
+        quant_x(29)
+        dense_1(29, 0)
+        hidden(26, 1)
+        dense_1(29, 1)
+        square(29, 0)
+        widen_x(D, S)
+        turn_x(31, "y")
+        square(29, 1)
+        scale_x(30)
+        quant_h(25)
+        quant_x(30)
+        add_squares(29, G)
+        inverse_root(28, 2)
+        gain(28)
+        hidden(27, 0)
+        dense_1(30, 0, "xt")
+        dense_1(30, 1, "r0")
+        scale_x(31)
+        hidden(27, 1)
+        quant_x(31)
+        dense_1(31, 0, "y")
+        dense_1(31, 1, "i0")
+        quant_h(26, 2)
+        square(30, 0)
+        square(30, 1)
+        add_squares(30, G)
+        stage_h(28, 2)
+        hidden(28, 0)
+        hidden(28, 1)
+        inverse_root(29, 2)
+        gain(29)
+        square(31, 0)
+        square(31, 1)
+        hidden(29, 0)
+        dense_2(25, "r2")
+        hidden(29, 1)
+        dense_2(26, "i2")
+        add_squares(31, V)
+        quant_h(28, 2)
+        inverse_root(30, 2)
+        gain(30)
+        inverse_root(31, 2)
+        gain(31)
+        emit_y(25)
+        emit_y(26)
+        hidden(30, 0)
+        dense_2(27, "xt")
+        hidden(30, 1)
+        dense_2(28, "r0")
+        dense_2(29, "r1")
+        emit_y(27)
+        store_y(24, 4)
+        emit_y(28)
+        emit_y(29)
+        store_y(28, 2)
+        hidden(31, 0)
+        quant_h(30)
+        hidden(31, 1)
+        dense_2(30, "i1")
+        quant_h(31, 1, 0, 1)
+        quant_h(31, 1, 1, 2)
+        emit_y(30)
+        store_y(30, 1)
+        last_y(31, ("r2", "i2"))

@@ -23,8 +23,8 @@ GROUPS = F // 4
 EPS = 1e-6
 SIGN_OF_ZERO = 1e-38
 PARTS = ("r", "i")
-SCALAR_COLS = 336
-GPSIMD_COLS = 640
+SCALAR_COLS = 344
+GPSIMD_COLS = 648
 
 
 def tile_complexdensemodrelupair_t_kernel(tc, x_bytes, x_scale, wr, wi, b, g, vr, vi, out_r, out_i):
@@ -35,9 +35,8 @@ def tile_complexdensemodrelupair_t_kernel(tc, x_bytes, x_scale, wr, wi, b, g, vr
 
     with ExitStack() as ctx:
         keep = ctx.enter_context(tc.tile_pool(name="keep", bufs=1))
-        stage = ctx.enter_context(tc.tile_pool(name="stage", bufs=3))
-        xq = ctx.enter_context(tc.tile_pool(name="xq", bufs=4))
-        hq = ctx.enter_context(tc.tile_pool(name="hq", bufs=8))
+        stage = ctx.enter_context(tc.tile_pool(name="stage", bufs=5))
+        qout = ctx.enter_context(tc.tile_pool(name="qout", bufs=8))
         mid = ctx.enter_context(tc.tile_pool(name="mid", bufs=3))
         gains = ctx.enter_context(tc.tile_pool(name="gains", bufs=4))
         outp = ctx.enter_context(tc.tile_pool(name="outp", bufs=3))
@@ -112,28 +111,62 @@ def tile_complexdensemodrelupair_t_kernel(tc, x_bytes, x_scale, wr, wi, b, g, vr
                     first = (i * D + kp * K_PASS) // 2
                     nc.tensor.transpose(xt[i][:, u, kp, :], words[:, first + u:first + K_PASS // 2:2], ident[:])
 
-        x_in = {}
+        place = {}
+        staged = {}
+        quantised = {}
+
+        def stage_for(*items):
+            values = stage.tile([P, len(items) * D], BF16, align_bytes=64, name="values")
+            staged[items[0]] = values
+            for n, item in enumerate(items):
+                place[item] = (items[0], n)
+
+        def staged_values(item):
+            if item not in place:
+                stage_for(item)
+            first, n = place[item]
+            return staged[first][:, n * D:(n + 1) * D]
 
         def scale_x(i):
-            x_scaled = stage.tile([P, D], BF16, align_bytes=64, name="x_scaled")
             V.tensor_tensor(
-                out=x_scaled[:].rearrange("p (q n u e) -> p q n u e", q=PASSES, u=2, e=2),
+                out=staged_values(("x", i)).rearrange("p (q n u e) -> p q n u e", q=PASSES, u=2, e=2),
                 in0=xt[i][:].rearrange("p u q n -> p (u q n)").bitcast(BF16).rearrange("p (u q n e) -> p q n u e", u=2, q=PASSES, e=2),
                 in1=xs[:].unsqueeze(2).to_broadcast([P, PASSES, P, 4]).rearrange("p q n (u e) -> p q n u e", u=2),
                 op=ALU.mult,
             )
-            x_in[i] = x_scaled
+
+        def turn_and_scale_pass(i, kp, tag):
+            words = xb[:].bitcast(F32)
+            pass_bank = banks.tile([P, 2, P], F32, tag=tag, name="pass_bank")
+            first = (i * D + kp * K_PASS) // 2
+            for u in range(2):
+                nc.tensor.transpose(pass_bank[:, u, :], words[:, first + u:first + K_PASS // 2:2], ident[:])
+            V.tensor_tensor(
+                out=staged_values(("x", i))[:, kp * K_PASS:(kp + 1) * K_PASS].rearrange("p (n u e) -> p n u e", u=2, e=2),
+                in0=pass_bank[:].rearrange("p u n -> p (u n)").bitcast(BF16).rearrange("p (u n e) -> p n u e", u=2, e=2),
+                in1=xs[:, kp, :].unsqueeze(1).to_broadcast([P, P, 4]).rearrange("p n (u e) -> p n u e", u=2),
+                op=ALU.mult,
+            )
 
         def quantise(codes, scales, values):
             V.quantize_mx(out=codes.bitcast(FP8X4), scales=scales, in_=values)
 
-        x_mx = {}
+        def quant(kind, i, count=1, halves=range(2)):
+            first, n = place[kind, i]
+            if first not in quantised:
+                width = staged[first].shape[1] // 4
+                codes = qout.tile([P, width], U32, align_bytes=64, name="codes")
+                scales = qout.tile([P, width], U8, align_bytes=64, name="scales")
+                quantised[first] = (codes, scales)
+            codes, scales = quantised[first]
+            lo, hi = 2 * n + halves.start, 2 * (n + count - 1) + halves.stop
+            quantise(codes[:, lo * P:hi * P], scales[:, lo * P:hi * P], staged[first][:, lo * K_PASS:hi * K_PASS])
 
-        def quant_x(i):
-            x_codes = xq.tile([P, PASSES * P], U32, align_bytes=64, name="x_codes")
-            x_sc = xq.tile([P, PASSES * P], U8, align_bytes=64, name="x_sc")
-            quantise(x_codes[:], x_sc[:], x_in[i][:])
-            x_mx[i] = (x_codes, x_sc)
+        def mx_half(kind, i, half):
+            first, n = place[kind, i]
+            codes, scales = quantised[first]
+            cols = slice((2 * n + half) * P, (2 * n + half + 1) * P)
+            return codes[:, cols].bitcast(FP8X4), scales[:, cols]
 
         w_grp = {}
         w_mx = {}
@@ -162,24 +195,24 @@ def tile_complexdensemodrelupair_t_kernel(tc, x_bytes, x_scale, wr, wi, b, g, vr
 
         z = {}
 
-        def dense_1(i, o, tag=None):
-            bank = banks.tile([P, 4, P], F32, tag=tag or PARTS[o] + str(i % 3), name="z_bank")
-            x_codes, x_sc = x_mx[i]
-            for kp in range(PASSES):
+        def dense_1(i, o, tag=None, passes=range(PASSES)):
+            if (i, o) not in z:
+                z_bank = banks.tile([P, 4, P], F32, tag=tag or PARTS[o] + str(i % 3), name="z_bank")
+                z[i, o] = z_bank
+            for kp in passes:
                 w_codes, w_sc = w_mx[PARTS[o], kp]
-                tokens = slice(kp * P, (kp + 1) * P)
+                x_codes, x_sc = mx_half("x", i, kp)
                 for t in range(4):
                     channels = slice(t * P, (t + 1) * P)
                     nc.tensor.matmul_mx(
-                        out=bank[:, t, :],
+                        out=z[i, o][:, t, :],
                         lhsT=w_codes[:, channels].bitcast(FP8X4),
                         lhsT_scale=w_sc[:, channels],
-                        rhs=x_codes[:, tokens].bitcast(FP8X4),
-                        rhs_scale=x_sc[:, tokens],
+                        rhs=x_codes,
+                        rhs_scale=x_sc,
                         start=(kp == 0 and t == 0),
                         stop=(kp == PASSES - 1 and t == 3),
                     )
-            z[i, o] = bank
 
         sq = {}
 
@@ -229,44 +262,20 @@ def tile_complexdensemodrelupair_t_kernel(tc, x_bytes, x_scale, wr, wi, b, g, vr
             flat = mg[i][:, slots.start:slots.stop, :].rearrange("p t n -> p (t n)")
             V.tensor_scalar(out=flat, in0=flat, scalar1=0.0, scalar2=None, op0=ALU.max)
 
-        h_in = {}
-        h_run = {}
-
-        def stage_h(first, count):
-            h_tile = stage.tile([P, count * 2 * F], BF16, align_bytes=64, name="h_tile")
-            h_run[first] = h_tile
-            for n in range(count):
-                h_in[first + n] = h_tile[:, n * 2 * F:(n + 1) * 2 * F]
-
         def hidden(i, o):
-            if i not in h_in:
-                stage_h(i, 1)
             V.tensor_tensor(
-                out=h_in[i][:, o * F:(o + 1) * F].rearrange("p (c k t) -> p c t k", k=2, t=4),
+                out=staged_values(("h", i))[:, o * F:(o + 1) * F].rearrange("p (c k t) -> p c t k", k=2, t=4),
                 in0=z[i, o][:].rearrange("p t (c k) -> p c t k", k=2),
                 in1=mg[i][:].rearrange("p t (c k) -> p c t k", k=2),
                 op=ALU.mult,
             )
 
-        h_mx = {}
-
-        def quant_h(first, count=1, lo=0, hi=None):
-            hi = 2 * count if hi is None else hi
-            if first not in h_mx:
-                h_codes = hq.tile([P, count * 2 * P], U32, align_bytes=64, name="h_codes")
-                h_sc = hq.tile([P, count * 2 * P], U8, align_bytes=64, name="h_sc")
-                for n in range(count):
-                    h_mx[first + n] = (h_codes, h_sc, 2 * n)
-            h_codes, h_sc, start = h_mx[first]
-            quantise(h_codes[:, lo * P:hi * P], h_sc[:, lo * P:hi * P], h_run[first][:, lo * F:hi * F])
-
         y = {}
 
         def product_2(out, i, o, cols):
-            h_codes, h_sc, start = h_mx[i]
-            tokens = slice((start + o) * P, (start + o + 1) * P)
+            h_codes, h_sc = mx_half("h", i, o)
             nc.tensor.matmul_mx(
-                out=out, lhsT=h_codes[:, tokens].bitcast(FP8X4), lhsT_scale=h_sc[:, tokens],
+                out=out, lhsT=h_codes, lhsT_scale=h_sc,
                 rhs=v_codes[:, cols].bitcast(FP8X4), rhs_scale=v_sc[:, cols], start=(o == 0), stop=(o == 1),
             )
 
@@ -337,34 +346,37 @@ def tile_complexdensemodrelupair_t_kernel(tc, x_bytes, x_scale, wr, wi, b, g, vr
             cols = slice(lo * E, hi * E)
             quantise(v_codes[:, cols], v_sc[:, cols], v_grp[:, lo:hi, :, :].rearrange("p o e j -> p (o e j)"))
 
+        widen_x(D // 4, S)
+        widen_x(D // 4, V)
+        widen_x(D // 4, S)
+        widen_x(D // 4, V)
         widen_x(D // 2, S)
         widen_x(D // 2, V)
-        turn_x(0, "xt")
-        widen_x(D // 2, S)
-        widen_x(D // 2, V)
-        turn_x(1, "y")
         widen_x(D, S)
         widen_x(D, V)
-        turn_x(2, "r2")
-        group_w("r", 0, 0, 64, S)
-        group_w("r", 0, 64, 128, G)
-        group_w("r", 1, 0, 112, S)
-        group_w("r", 1, 112, 128, G)
-        group_w("i", 0, 0, 96, S)
-        group_w("i", 1, 0, 24, S)
-        scale_x(0)
-        turn_x(3, "xt")
+        turn_and_scale_pass(0, 0, "xt")
+        turn_and_scale_pass(0, 1, "i2")
+        turn_x(1, "y")
+        group_w("r", 0, 0, 56, S)
+        group_w("r", 0, 56, 128, G)
+        group_w("r", 1, 0, 128, S)
+        group_w("i", 0, 0, 36, S)
+        group_w("i", 1, 0, 56, S)
         scale_x(1)
+        turn_x(2, "r2")
+        turn_x(3, "xt")
+        quant("x", 0)
         quant_w("r", 0)
-        quant_x(0)
-        quant_x(1)
-        group_w("i", 0, 96, 128, V)
+        quant("x", 1)
+        dense_1(0, 0, None, range(0, 1))
+        dense_1(1, 0, None, range(0, 1))
+        group_w("i", 0, 36, 128, V)
         quant_w("r", 1)
-        group_w("i", 1, 24, 128, V)
+        group_w("i", 1, 56, 128, V)
         quant_w("i", 0)
         quant_w("i", 1)
-        dense_1(0, 0)
-        dense_1(1, 0)
+        dense_1(0, 0, None, range(1, 2))
+        dense_1(1, 0, None, range(1, 2))
         dense_1(0, 1)
         dense_1(1, 1)
         prep_signs()
@@ -372,15 +384,15 @@ def tile_complexdensemodrelupair_t_kernel(tc, x_bytes, x_scale, wr, wi, b, g, vr
         sign_v(2, vi_raw, G, 0, 104)
         sign_v(2, vi_raw, V, 104, E)
         sign_v(1, vr_raw, V)
-        quant_x(2)
+        quant("x", 2)
         widen_x(D, S)
         square(0, 0)
         widen_x(384, S)
         square(1, 0)
         widen_x(384, S)
         square(0, 1)
-        add_squares(0, V)
         prep_beta()
+        add_squares(0, V)
         negate_v()
         dense_1(2, 0)
         turn_x(4, "y", range(0, 1))
@@ -396,23 +408,23 @@ def tile_complexdensemodrelupair_t_kernel(tc, x_bytes, x_scale, wr, wi, b, g, vr
         scale_x(3)
         turn_x(5)
         hidden(0, 0)
-        quant_x(3)
+        quant("x", 3)
         dense_1(3, 0)
         hidden(0, 1)
         dense_1(3, 1)
         square(2, 0)
         square(2, 1)
         add_squares(2, G)
-        widen_x(448, G)
+        widen_x(416, G)
         inverse_root(1, 2)
         gain(1)
-        widen_x(384, S)
+        widen_x(256, S)
         square(3, 0)
         widen_x(64, S)
         square(3, 1)
         add_squares(3, G)
         inverse_root(2)
-        widen_x(704, S)
+        widen_x(448, S)
         widen_x(GPSIMD_COLS, G)
         gain(2)
 
@@ -421,9 +433,9 @@ def tile_complexdensemodrelupair_t_kernel(tc, x_bytes, x_scale, wr, wi, b, g, vr
             if c > 4:
                 turn_x(c + 1)
             hidden(c - 3, 0)
-            quant_x(c)
+            quant("x", c)
             if c >= 4:
-                quant_h(c - 4)
+                quant("h", c - 4)
             dense_1(c, 0)
             hidden(c - 3, 1)
             dense_1(c, 1)
@@ -442,9 +454,9 @@ def tile_complexdensemodrelupair_t_kernel(tc, x_bytes, x_scale, wr, wi, b, g, vr
 
         scale_x(29)
         turn_x(30)
-        stage_h(26, 2)
+        stage_for(("h", 26), ("h", 27))
         hidden(26, 0)
-        quant_x(29)
+        quant("x", 29)
         dense_1(29, 0)
         hidden(26, 1)
         dense_1(29, 1)
@@ -453,8 +465,8 @@ def tile_complexdensemodrelupair_t_kernel(tc, x_bytes, x_scale, wr, wi, b, g, vr
         turn_x(31, "y")
         square(29, 1)
         scale_x(30)
-        quant_h(25)
-        quant_x(30)
+        quant("h", 25)
+        quant("x", 30)
         add_squares(29, G)
         inverse_root(28, 2)
         gain(28)
@@ -463,14 +475,14 @@ def tile_complexdensemodrelupair_t_kernel(tc, x_bytes, x_scale, wr, wi, b, g, vr
         dense_1(30, 1, "r0")
         scale_x(31)
         hidden(27, 1)
-        quant_x(31)
+        quant("x", 31)
         dense_1(31, 0, "y")
         dense_1(31, 1, "i0")
-        quant_h(26, 2)
+        quant("h", 26, 2)
         square(30, 0)
         square(30, 1)
         add_squares(30, G)
-        stage_h(28, 2)
+        stage_for(("h", 28), ("h", 29))
         hidden(28, 0)
         hidden(28, 1)
         inverse_root(29, 2)
@@ -482,7 +494,9 @@ def tile_complexdensemodrelupair_t_kernel(tc, x_bytes, x_scale, wr, wi, b, g, vr
         hidden(29, 1)
         dense_2(26, "i2")
         add_squares(31, V)
-        quant_h(28, 2)
+        quant("h", 28, 2)
+        dense_2(28, "r1")
+        dense_2(27, "i1")
         inverse_root(30, 2)
         gain(30)
         inverse_root(31, 2)
@@ -490,21 +504,19 @@ def tile_complexdensemodrelupair_t_kernel(tc, x_bytes, x_scale, wr, wi, b, g, vr
         emit_y(25)
         emit_y(26)
         hidden(30, 0)
-        dense_2(27, "xt")
         hidden(30, 1)
-        dense_2(28, "r0")
-        dense_2(29, "r1")
+        dense_2(29, "r0")
         emit_y(27)
         store_y(24, 4)
         emit_y(28)
         emit_y(29)
         store_y(28, 2)
         hidden(31, 0)
-        quant_h(30)
+        quant("h", 30)
         hidden(31, 1)
-        dense_2(30, "i1")
-        quant_h(31, 1, 0, 1)
-        quant_h(31, 1, 1, 2)
+        dense_2(30, "xt")
+        quant("h", 31, 1, range(0, 1))
+        quant("h", 31, 1, range(1, 2))
         emit_y(30)
         store_y(30, 1)
         last_y(31, ("r2", "i2"))

@@ -180,8 +180,8 @@ def tile_complexdensemodrelupair_t_kernel(tc, x_bytes, x_scale, wr, wi, b, g, vr
                 src = w_raw[part, kp][:].rearrange("p j (m t) -> p m t j", t=4)[:, lo:hi]
                 G.tensor_scalar(out=dst, in0=src, scalar1=1.0, scalar2=0.0, op0=ALU.mult, op1=ALU.add)
                 return
-            dst = w_grp[part, kp][:].rearrange("p (t m k j) -> p m t k j", t=4, k=2, j=4)[:, lo // 2:hi // 2]
-            src = w_raw[part, kp][:].rearrange("p j (m k t) -> p m t k j", k=2, t=4)[:, lo // 2:hi // 2]
+            dst = w_grp[part, kp][:].rearrange("p (a e m j) -> p m a j e", a=2, e=2, j=4)[:, lo:hi]
+            src = w_raw[part, kp][:].rearrange("p j (m a e) -> p m a j e", a=2, e=2)[:, lo:hi]
             if engine is V:
                 V.tensor_copy(out=dst, in_=src)
             else:

@@ -360,8 +360,8 @@ def tile_complexdensemodrelupair_t_kernel(tc, x_bytes, x_scale, wr, wi, b, g, vr
         group_w("r", 0, 0, 56, S)
         group_w("r", 0, 56, 128, G)
         group_w("r", 1, 0, 128, S)
-        group_w("i", 0, 0, 36, S)
-        group_w("i", 1, 0, 56, S)
+        group_w("i", 0, 0, 44, S)
+        group_w("i", 1, 0, 60, S)
         scale_x(1)
         turn_x(2, "r2")
         turn_x(3, "xt")
@@ -370,9 +370,9 @@ def tile_complexdensemodrelupair_t_kernel(tc, x_bytes, x_scale, wr, wi, b, g, vr
         quant("x", 1)
         dense_1(0, 0, None, range(0, 1))
         dense_1(1, 0, None, range(0, 1))
-        group_w("i", 0, 36, 128, V)
+        group_w("i", 0, 44, 128, V)
         quant_w("r", 1)
-        group_w("i", 1, 56, 128, V)
+        group_w("i", 1, 60, 128, V)
         quant_w("i", 0)
         quant_w("i", 1)
         dense_1(0, 0, None, range(1, 2))

@@ -45,9 +45,11 @@ def tile_complexdensemodrelupair_t_kernel(tc, x_bytes, x_scale, wr, wi, b, g, vr
 
         x8 = keep.tile([P, TILES * D], U8, name="x8")
 
+        def load_x_cols(lo, hi):
+            nc.sync.dma_start(out=x8[:, lo:hi], in_=x_rows[:, lo:hi])
+
         def load_x(first, count):
-            cols = slice(first * D, (first + count) * D)
-            nc.sync.dma_start(out=x8[:, cols], in_=x_rows[:, cols])
+            load_x_cols(first * D, (first + count) * D)
 
         w_raw = {}
 
@@ -56,7 +58,8 @@ def tile_complexdensemodrelupair_t_kernel(tc, x_bytes, x_scale, wr, wi, b, g, vr
             nc.sync.dma_start(out=w_rows[:], in_=src[kp * K_PASS:(kp + 1) * K_PASS, :].rearrange("(p j) c -> p j c", j=4))
             w_raw[part, kp] = w_rows
 
-        load_x(0, 1)
+        load_x_cols(0, K_PASS)
+        load_x_cols(K_PASS, D)
         load_x(1, 1)
         xs = keep.tile([P, PASSES, 4], F32)
         nc.sync.dma_start(out=xs[:], in_=x_scale.rearrange("o (q p t) -> p (o q) t", p=P, t=4))
@@ -65,12 +68,11 @@ def tile_complexdensemodrelupair_t_kernel(tc, x_bytes, x_scale, wr, wi, b, g, vr
         load_w("r", wr, 1)
         load_w("i", wi, 0)
         load_w("i", wi, 1)
-        load_x(4, 2)
+        load_x(4, 4)
         b_bf = keep.tile([P, 4], BF16)
         nc.sync.dma_start(out=b_bf[:], in_=b.rearrange("(p t) -> p t", t=4))
         g_bf = keep.tile([P, 4], BF16)
         nc.sync.dma_start(out=g_bf[:], in_=g.rearrange("(p t) -> p t", t=4))
-        load_x(6, 2)
         vr_raw = keep.tile([P, 4, E], BF16)
         nc.sync.dma_start(out=vr_raw[:], in_=vr.rearrange("(p j) e -> p j e", j=4))
         vi_raw = keep.tile([P, 4, E], BF16)
@@ -352,16 +354,15 @@ def tile_complexdensemodrelupair_t_kernel(tc, x_bytes, x_scale, wr, wi, b, g, vr
         widen_x(D // 4, V)
         widen_x(D // 2, S)
         widen_x(D // 2, V)
-        widen_x(D, S)
-        widen_x(D, V)
+        widen_x(3 * D // 2, S)
+        widen_x(D // 2, V)
         turn_and_scale_pass(0, 0, "xt")
         turn_and_scale_pass(0, 1, "i2")
         turn_x(1, "y")
-        group_w("r", 0, 0, 56, S)
-        group_w("r", 0, 56, 128, G)
+        group_w("r", 0, 0, 70, S)
+        group_w("r", 0, 70, 128, G)
         group_w("r", 1, 0, 128, S)
-        group_w("i", 0, 0, 44, S)
-        group_w("i", 1, 0, 60, S)
+        group_w("i", 1, 0, 88, S)
         scale_x(1)
         turn_x(2, "r2")
         turn_x(3, "xt")
@@ -370,9 +371,9 @@ def tile_complexdensemodrelupair_t_kernel(tc, x_bytes, x_scale, wr, wi, b, g, vr
         quant("x", 1)
         dense_1(0, 0, None, range(0, 1))
         dense_1(1, 0, None, range(0, 1))
-        group_w("i", 0, 44, 128, V)
+        group_w("i", 0, 0, 128, V)
         quant_w("r", 1)
-        group_w("i", 1, 60, 128, V)
+        group_w("i", 1, 88, 128, V)
         quant_w("i", 0)
         quant_w("i", 1)
         dense_1(0, 0, None, range(1, 2))
@@ -389,17 +390,16 @@ def tile_complexdensemodrelupair_t_kernel(tc, x_bytes, x_scale, wr, wi, b, g, vr
         square(0, 0)
         widen_x(384, S)
         square(1, 0)
-        widen_x(384, S)
+        widen_x(320, S)
         square(0, 1)
         prep_beta()
         add_squares(0, V)
         negate_v()
         dense_1(2, 0)
-        turn_x(4, "y", range(0, 1))
+        turn_x(4, "y")
         dense_1(2, 1)
-        turn_x(4, "y", range(1, 2))
         square(1, 1)
-        widen_x(896, S)
+        widen_x(960, S)
         quant_v(1, 3)
         quant_v(0, 1)
         add_squares(1, G, "v_grp_then_m2")
@@ -413,18 +413,18 @@ def tile_complexdensemodrelupair_t_kernel(tc, x_bytes, x_scale, wr, wi, b, g, vr
         hidden(0, 1)
         dense_1(3, 1)
         square(2, 0)
+        widen_x(320, S)
         square(2, 1)
         add_squares(2, G)
-        widen_x(416, G)
+        widen_x(320, G)
         inverse_root(1, 2)
         gain(1)
-        widen_x(256, S)
         square(3, 0)
         widen_x(64, S)
         square(3, 1)
         add_squares(3, G)
         inverse_root(2)
-        widen_x(448, S)
+        widen_x(480, S)
         widen_x(GPSIMD_COLS, G)
         gain(2)
 

@@ -23,6 +23,7 @@ GROUPS = F // 4
 EPS = 1e-6
 SIGN_OF_ZERO = 1e-38
 PARTS = ("r", "i")
+SHARED = "wi0_then_v_then_m2"
 SCALAR_COLS = 344
 GPSIMD_COLS = 648
 
@@ -175,7 +176,7 @@ def tile_complexdensemodrelupair_t_kernel(tc, x_bytes, x_scale, wr, wi, b, g, vr
 
         def group_w(part, kp, lo, hi, engine):
             if (part, kp) not in w_grp:
-                w_grouped = keep.tile([P, 4 * F], BF16, align_bytes=64, name="w_grouped_" + part + str(kp))
+                w_grouped = keep.tile([P, 4 * F], BF16, align_bytes=64, name=SHARED if (part, kp) == ("i", 0) else "w_grouped_" + part + str(kp))
                 w_grp[part, kp] = w_grouped
             if engine is G:
                 dst = w_grp[part, kp][:].rearrange("p (t m j) -> p m t j", t=4, j=4)[:, lo:hi]
@@ -322,7 +323,7 @@ def tile_complexdensemodrelupair_t_kernel(tc, x_bytes, x_scale, wr, wi, b, g, vr
         sgn = keep.tile([P, 4], BF16)
         absg = keep.tile([P, 4], F32)
         beta = keep.tile([P, 4], F32)
-        v_grp = keep.tile([P, 3, E, 4], BF16, align_bytes=64, name="v_grp_then_m2")
+        v_stage = []
         v_codes = keep.tile([P, 3 * E], U32, align_bytes=64)
         v_sc = keep.tile([P, 3 * E], U8, align_bytes=64)
 
@@ -334,19 +335,22 @@ def tile_complexdensemodrelupair_t_kernel(tc, x_bytes, x_scale, wr, wi, b, g, vr
             V.tensor_tensor(out=beta[:], in0=absg[:], in1=b_bf[:], op=ALU.mult)
 
         def sign_v(slot, raw, engine, lo=0, hi=E):
+            if not v_stage:
+                v_tile = keep.tile([P, 3, E, 4], BF16, align_bytes=64, name=SHARED)
+                v_stage.append(v_tile)
             walk = "p c j k" if engine is V else "p c k j"
             engine.tensor_tensor(
-                out=v_grp[:, slot, lo:hi, :].rearrange("p (c k) j -> " + walk, k=2),
+                out=v_stage[0][:, slot, lo:hi, :].rearrange("p (c k) j -> " + walk, k=2),
                 in0=raw[:, :, lo:hi].rearrange("p j (c k) -> " + walk, k=2),
                 in1=sgn[:].unsqueeze(1).to_broadcast([P, hi - lo, 4]).rearrange("p (c k) j -> " + walk, k=2), op=ALU.mult,
             )
 
         def negate_v():
-            V.tensor_scalar(out=v_grp[:, 0, :, :], in0=v_grp[:, 2, :, :], scalar1=-1.0, scalar2=None, op0=ALU.mult)
+            V.tensor_scalar(out=v_stage[0][:, 0, :, :], in0=v_stage[0][:, 2, :, :], scalar1=-1.0, scalar2=None, op0=ALU.mult)
 
         def quant_v(lo, hi):
             cols = slice(lo * E, hi * E)
-            quantise(v_codes[:, cols], v_sc[:, cols], v_grp[:, lo:hi, :, :].rearrange("p o e j -> p (o e j)"))
+            quantise(v_codes[:, cols], v_sc[:, cols], v_stage[0][:, lo:hi, :, :].rearrange("p o e j -> p (o e j)"))
 
         widen_x(D // 4, S)
         widen_x(D // 4, V)
@@ -402,7 +406,7 @@ def tile_complexdensemodrelupair_t_kernel(tc, x_bytes, x_scale, wr, wi, b, g, vr
         widen_x(960, S)
         quant_v(1, 3)
         quant_v(0, 1)
-        add_squares(1, G, "v_grp_then_m2")
+        add_squares(1, G, SHARED)
         inverse_root(0, 2)
         gain(0)
         scale_x(3)

from contextlib import ExitStack

import concourse.mybir as mybir
from concourse.masks import make_identity

N, D, F, E = 4096, 1024, 512, 128
FLOPS = 2 * N * D * F * 2 + 2 * N * F * E * 4

F32 = mybir.dt.float32
BF16 = mybir.dt.bfloat16
U32 = mybir.dt.uint32
U8 = mybir.dt.uint8
FP8 = mybir.dt.float8_e4m3fn
FP8X4 = mybir.dt.float8_e4m3fn_x4
ALU = mybir.AluOpType
ACT = mybir.ActivationFunctionType

P = 128
K_PASS = 4 * P
PASSES = D // K_PASS
TILES = N // P
GROUPS = F // 4
EPS = 1e-6
SIGN_OF_ZERO = 1e-38
PARTS = ("r", "i")
SHARED = "wi0_then_v_then_m2"
SCALAR_COLS = 344
GPSIMD_COLS = 648


def tile_complexdensemodrelupair_t_kernel(tc, x_bytes, x_scale, wr, wi, b, g, vr, vi, out_r, out_i):
    nc = tc.nc
    V, S, G = nc.vector, nc.scalar, nc.gpsimd
    x_rows = x_bytes.rearrange("(p i) k -> p (i k)", p=P)
    y_rows = [out_r.rearrange("(p i) e -> p i e", p=P), out_i.rearrange("(p i) e -> p i e", p=P)]

    with ExitStack() as ctx:
        keep = ctx.enter_context(tc.tile_pool(name="keep", bufs=1))
        stage = ctx.enter_context(tc.tile_pool(name="stage", bufs=5))
        qout = ctx.enter_context(tc.tile_pool(name="qout", bufs=8))
        mid = ctx.enter_context(tc.tile_pool(name="mid", bufs=3))
        gains = ctx.enter_context(tc.tile_pool(name="gains", bufs=4))
        outp = ctx.enter_context(tc.tile_pool(name="outp", bufs=3))
        banks = ctx.enter_context(tc.psum_pool(name="banks", bufs=1))
        ctx.enter_context(tc.manual_schedule())

        x8 = keep.tile([P, TILES * D], U8, name="x8")

        def load_x_cols(lo, hi):
            nc.sync.dma_start(out=x8[:, lo:hi], in_=x_rows[:, lo:hi])

        def load_x(first, count):
            load_x_cols(first * D, (first + count) * D)

        w_raw = {}

        def load_w(part, src, kp):
            w_rows = keep.tile([P, 4, F], BF16, name="w_raw_" + part + str(kp))
            nc.sync.dma_start(out=w_rows[:], in_=src[kp * K_PASS:(kp + 1) * K_PASS, :].rearrange("(p j) c -> p j c", j=4))
            w_raw[part, kp] = w_rows

        load_x_cols(0, K_PASS)
        load_x_cols(K_PASS, D)
        load_x(1, 1)
        xs = keep.tile([P, PASSES, 4], F32)
        nc.sync.dma_start(out=xs[:], in_=x_scale.rearrange("o (q p t) -> p (o q) t", p=P, t=4))
        load_x(2, 2)
        load_w("r", wr, 0)
        load_w("r", wr, 1)
        load_w("i", wi, 0)
        load_w("i", wi, 1)
        load_x(4, 4)
        b_bf = keep.tile([P, 4], BF16)
        nc.sync.dma_start(out=b_bf[:], in_=b.rearrange("(p t) -> p t", t=4))
        g_bf = keep.tile([P, 4], BF16)
        nc.sync.dma_start(out=g_bf[:], in_=g.rearrange("(p t) -> p t", t=4))
        vr_raw = keep.tile([P, 4, E], BF16)
        nc.sync.dma_start(out=vr_raw[:], in_=vr.rearrange("(p j) e -> p j e", j=4))
        vi_raw = keep.tile([P, 4, E], BF16)
        nc.sync.dma_start(out=vi_raw[:], in_=vi.rearrange("(p j) e -> p j e", j=4))
        for first in range(8, TILES, 4):
            load_x(first, 4)

        warm = keep.tile([P, 1], F32)
        V.memset(warm[:], 1.0)
        S.activation(out=warm[:], in_=warm[:], func=ACT.Abs_reciprocal_sqrt)
        ident = keep.tile([P, P], F32)
        make_identity(nc, ident[:])

        xb = keep.tile([P, TILES * D], BF16)
        widened = [0]

        def widen_x(count, engine):
            cols = slice(widened[0], min(widened[0] + count, TILES * D))
            widened.append(cols.stop)
            widened.remove(cols.start)
            if cols.start == cols.stop:
                return
            if engine is S:
                S.copy(out=xb[:, cols], in_=x8[:, cols].bitcast(FP8))
            else:
                engine.tensor_copy(out=xb[:, cols], in_=x8[:, cols].bitcast(FP8))

        xt = {}

        def turn_x(i, tag="xt", passes=range(PASSES)):
            assert widened[0] >= (i + 1) * D
            words = xb[:].bitcast(F32)
            if i not in xt:
                xt_bank = banks.tile([P, 2, PASSES, P], F32, tag=tag, name="xt_bank")
                xt[i] = xt_bank
            for kp in passes:
                for u in range(2):
                    first = (i * D + kp * K_PASS) // 2
                    nc.tensor.transpose(xt[i][:, u, kp, :], words[:, first + u:first + K_PASS // 2:2], ident[:])

        place = {}
        staged = {}
        quantised = {}

        def stage_for(*items):
            values = stage.tile([P, len(items) * D], BF16, align_bytes=64, name="values")
            staged[items[0]] = values
            for n, item in enumerate(items):
                place[item] = (items[0], n)

        def staged_values(item):
            if item not in place:
                stage_for(item)
            first, n = place[item]
            return staged[first][:, n * D:(n + 1) * D]

        def scale_x(i):
            V.tensor_tensor(
                out=staged_values(("x", i)).rearrange("p (q n u e) -> p q n u e", q=PASSES, u=2, e=2),
                in0=xt[i][:].rearrange("p u q n -> p (u q n)").bitcast(BF16).rearrange("p (u q n e) -> p q n u e", u=2, q=PASSES, e=2),
                in1=xs[:].unsqueeze(2).to_broadcast([P, PASSES, P, 4]).rearrange("p q n (u e) -> p q n u e", u=2),
                op=ALU.mult,
            )

        def turn_and_scale_pass(i, kp, tag):
            words = xb[:].bitcast(F32)
            pass_bank = banks.tile([P, 2, P], F32, tag=tag, name="pass_bank")
            first = (i * D + kp * K_PASS) // 2
            for u in range(2):
                nc.tensor.transpose(pass_bank[:, u, :], words[:, first + u:first + K_PASS // 2:2], ident[:])
            V.tensor_tensor(
                out=staged_values(("x", i))[:, kp * K_PASS:(kp + 1) * K_PASS].rearrange("p (n u e) -> p n u e", u=2, e=2),
                in0=pass_bank[:].rearrange("p u n -> p (u n)").bitcast(BF16).rearrange("p (u n e) -> p n u e", u=2, e=2),
                in1=xs[:, kp, :].unsqueeze(1).to_broadcast([P, P, 4]).rearrange("p n (u e) -> p n u e", u=2),
                op=ALU.mult,
            )

        def quantise(codes, scales, values):
            V.quantize_mx(out=codes.bitcast(FP8X4), scales=scales, in_=values)

        def quant(kind, i, count=1, halves=range(2)):
            first, n = place[kind, i]
            if first not in quantised:
                width = staged[first].shape[1] // 4
                codes = qout.tile([P, width], U32, align_bytes=64, name="codes")
                scales = qout.tile([P, width], U8, align_bytes=64, name="scales")
                quantised[first] = (codes, scales)
            codes, scales = quantised[first]
            lo, hi = 2 * n + halves.start, 2 * (n + count - 1) + halves.stop
            quantise(codes[:, lo * P:hi * P], scales[:, lo * P:hi * P], staged[first][:, lo * K_PASS:hi * K_PASS])

        def mx_half(kind, i, half):
            first, n = place[kind, i]
            codes, scales = quantised[first]
            cols = slice((2 * n + half) * P, (2 * n + half + 1) * P)
            return codes[:, cols].bitcast(FP8X4), scales[:, cols]

        w_grp = {}
        w_mx = {}

        def group_w(part, kp, lo, hi, engine):
            if (part, kp) not in w_grp:
                w_grouped = keep.tile([P, 4 * F], BF16, align_bytes=64, name=SHARED if (part, kp) == ("i", 0) else "w_grouped_" + part + str(kp))
                w_grp[part, kp] = w_grouped
            if engine is G:
                dst = w_grp[part, kp][:].rearrange("p (t m j) -> p m t j", t=4, j=4)[:, lo:hi]
                src = w_raw[part, kp][:].rearrange("p j (m t) -> p m t j", t=4)[:, lo:hi]
                G.tensor_scalar(out=dst, in0=src, scalar1=1.0, scalar2=0.0, op0=ALU.mult, op1=ALU.add)
                return
            dst = w_grp[part, kp][:].rearrange("p (a e m j) -> p m a j e", a=2, e=2, j=4)[:, lo:hi]
            src = w_raw[part, kp][:].rearrange("p j (m a e) -> p m a j e", a=2, e=2)[:, lo:hi]
            if engine is V:
                V.tensor_copy(out=dst, in_=src)
            else:
                S.copy(out=dst, in_=src)

        def quant_w(part, kp):
            w_codes = keep.tile([P, F], U32, align_bytes=64, name="w_codes_" + part + str(kp))
            w_sc = keep.tile([P, F], U8, align_bytes=64, name="w_sc_" + part + str(kp))
            quantise(w_codes[:], w_sc[:], w_grp[part, kp][:])
            w_mx[part, kp] = (w_codes, w_sc)

        z = {}

        def dense_1(i, o, tag=None, passes=range(PASSES)):
            if (i, o) not in z:
                z_bank = banks.tile([P, 4, P], F32, tag=tag or PARTS[o] + str(i % 3), name="z_bank")
                z[i, o] = z_bank
            for kp in passes:
                w_codes, w_sc = w_mx[PARTS[o], kp]
                x_codes, x_sc = mx_half("x", i, kp)
                for t in range(4):
                    channels = slice(t * P, (t + 1) * P)
                    nc.tensor.matmul_mx(
                        out=z[i, o][:, t, :],
                        lhsT=w_codes[:, channels].bitcast(FP8X4),
                        lhsT_scale=w_sc[:, channels],
                        rhs=x_codes,
                        rhs_scale=x_sc,
                        start=(kp == 0 and t == 0),
                        stop=(kp == PASSES - 1 and t == 3),
                    )

        sq = {}

        def square(i, o):
            if i not in sq:
                sq_pair = mid.tile([P, 2, F], F32, name="sq_pair")
                sq[i] = sq_pair
            S.activation(out=sq[i][:, o, :], in_=z[i, o][:].rearrange("p t n -> p (t n)"), func=ACT.Square)

        mg = {}

        def add_squares(i, engine, tag=None):
            if tag is None:
                m2_then_gain = gains.tile([P, 4, P], F32, align_bytes=64, name="m2_then_gain")
            else:
                m2_then_gain = keep.tile([P, 4, P], F32, align_bytes=64, name=tag)
            mg[i] = m2_then_gain
            engine.tensor_tensor(out=mg[i][:].rearrange("p t n -> p (t n)"), in0=sq[i][:, 0, :], in1=sq[i][:, 1, :], op=ALU.add)

        inv_m = {}

        def inverse_root(i, halves=1):
            r_tile = mid.tile([P, F], F32, name="r_tile")
            inv_m[i] = r_tile
            for half in range(halves):
                cols = slice(half * F // halves, (half + 1) * F // halves)
                S.activation(
                    out=r_tile[:, cols], in_=mg[i][:].rearrange("p t n -> p (t n)")[:, cols],
                    func=ACT.Abs_reciprocal_sqrt, bias=EPS,
                )

        def gain(i, slots=range(4)):
            for t in slots:
                S.activation(
                    out=mg[i][:, t, :], in_=inv_m[i][:, t * P:(t + 1) * P], func=ACT.Relu,
                    scale=beta[:, t:t + 1], bias=absg[:, t:t + 1],
                )

        def affine_on_vector(i, slots):
            for t in slots:
                V.tensor_scalar(
                    out=mg[i][:, t, :], in0=inv_m[i][:, t * P:(t + 1) * P], scalar1=beta[:, t:t + 1], scalar2=absg[:, t:t + 1],
                    op0=ALU.mult, op1=ALU.add,
                )

        def relu_on_vector(i, slots):
            flat = mg[i][:, slots.start:slots.stop, :].rearrange("p t n -> p (t n)")
            V.tensor_scalar(out=flat, in0=flat, scalar1=0.0, scalar2=None, op0=ALU.max)

        def hidden(i, o):
            V.tensor_tensor(
                out=staged_values(("h", i))[:, o * F:(o + 1) * F].rearrange("p (c k t) -> p c t k", k=2, t=4),
                in0=z[i, o][:].rearrange("p t (c k) -> p c t k", k=2),
                in1=mg[i][:].rearrange("p t (c k) -> p c t k", k=2),
                op=ALU.mult,
            )

        y = {}

        def product_2(out, i, o, cols):
            h_codes, h_sc = mx_half("h", i, o)
            nc.tensor.matmul_mx(
                out=out, lhsT=h_codes, lhsT_scale=h_sc,
                rhs=v_codes[:, cols].bitcast(FP8X4), rhs_scale=v_sc[:, cols], start=(o == 0), stop=(o == 1),
            )

        def dense_2(i, tag="y"):
            y_bank = banks.tile([P, 2, E], F32, tag=tag, name="y_bank")
            for o in range(2):
                product_2(y_bank[:].rearrange("p o e -> p (o e)"), i, o, slice((1 - o) * E, (3 - o) * E))
            y[i] = y_bank

        ysb = {}

        def y_tile(i):
            group, place = divmod(i, 4)
            if group not in ysb:
                y_group = outp.tile([P, 2, 4, E], F32, name="y_group")
                ysb[group] = y_group
            return ysb[group][:, :, place, :]

        def emit_y(i, engine=S):
            if engine is S:
                S.copy(out=y_tile(i), in_=y[i][:])
            else:
                V.tensor_copy(out=y_tile(i), in_=y[i][:])

        def store_y(first, count):
            group, place = divmod(first, 4)
            for o in range(2):
                nc.sync.dma_start(out=y_rows[o][:, first:first + count, :], in_=ysb[group][:, o, place:place + count, :])

        def last_y(i, tags):
            halves = []
            for tag in tags:
                y_half = banks.tile([P, E], F32, tag=tag, name="y_half")
                halves.append(y_half)
            for o in range(2):
                for part in range(2):
                    product_2(halves[part][:], i, o, slice((1 - o + part) * E, (2 - o + part) * E))
            V.tensor_copy(out=y_tile(i)[:, 0, :], in_=halves[0][:])
            S.copy(out=y_tile(i)[:, 1, :], in_=halves[1][:])
            store_y(i, 1)

        sgn = keep.tile([P, 4], BF16)
        absg = keep.tile([P, 4], F32)
        beta = keep.tile([P, 4], F32)
        v_stage = []
        v_codes = keep.tile([P, 3 * E], U32, align_bytes=64)
        v_sc = keep.tile([P, 3 * E], U8, align_bytes=64)

        def prep_signs():
            S.activation(out=sgn[:], in_=g_bf[:], func=ACT.Sign, bias=SIGN_OF_ZERO)
            S.activation(out=absg[:], in_=g_bf[:], func=ACT.Abs)

        def prep_beta():
            V.tensor_tensor(out=beta[:], in0=absg[:], in1=b_bf[:], op=ALU.mult)

        def sign_v(slot, raw, engine, lo=0, hi=E):
            if not v_stage:
                v_tile = keep.tile([P, 3, E, 4], BF16, align_bytes=64, name=SHARED)
                v_stage.append(v_tile)
            walk = "p c j k" if engine is V else "p c k j"
            engine.tensor_tensor(
                out=v_stage[0][:, slot, lo:hi, :].rearrange("p (c k) j -> " + walk, k=2),
                in0=raw[:, :, lo:hi].rearrange("p j (c k) -> " + walk, k=2),
                in1=sgn[:].unsqueeze(1).to_broadcast([P, hi - lo, 4]).rearrange("p (c k) j -> " + walk, k=2), op=ALU.mult,
            )

        def negate_v():
            V.tensor_scalar(out=v_stage[0][:, 0, :, :], in0=v_stage[0][:, 2, :, :], scalar1=-1.0, scalar2=None, op0=ALU.mult)

        def quant_v(lo, hi):
            cols = slice(lo * E, hi * E)
            quantise(v_codes[:, cols], v_sc[:, cols], v_stage[0][:, lo:hi, :, :].rearrange("p o e j -> p (o e j)"))

        widen_x(D // 4, S)
        widen_x(D // 4, V)
        widen_x(D // 4, S)
        widen_x(D // 4, V)
        widen_x(D // 2, S)
        widen_x(D // 2, V)
        widen_x(3 * D // 2, S)
        widen_x(D // 2, V)
        turn_and_scale_pass(0, 0, "xt")
        turn_and_scale_pass(0, 1, "i2")
        turn_x(1, "y")
        group_w("r", 0, 0, 70, S)
        group_w("r", 0, 70, 128, G)
        group_w("r", 1, 0, 128, S)
        group_w("i", 1, 0, 88, S)
        scale_x(1)
        turn_x(2, "r2")
        turn_x(3, "xt")
        quant("x", 0)
        quant_w("r", 0)
        quant("x", 1)
        dense_1(0, 0, None, range(0, 1))
        dense_1(1, 0, None, range(0, 1))
        group_w("i", 0, 0, 128, V)
        quant_w("r", 1)
        group_w("i", 1, 88, 128, V)
        quant_w("i", 0)
        quant_w("i", 1)
        dense_1(0, 0, None, range(1, 2))
        dense_1(1, 0, None, range(1, 2))
        dense_1(0, 1)
        dense_1(1, 1)
        prep_signs()
        scale_x(2)
        sign_v(2, vi_raw, G, 0, 104)
        sign_v(2, vi_raw, V, 104, E)
        sign_v(1, vr_raw, V)
        quant("x", 2)
        widen_x(D, S)
        square(0, 0)
        widen_x(384, S)
        square(1, 0)
        widen_x(320, S)
        square(0, 1)
        prep_beta()
        add_squares(0, V)
        negate_v()
        dense_1(2, 0)
        turn_x(4, "y")
        dense_1(2, 1)
        square(1, 1)
        widen_x(960, S)
        quant_v(1, 3)
        quant_v(0, 1)
        add_squares(1, G, SHARED)
        inverse_root(0, 2)
        gain(0)
        scale_x(3)
        turn_x(5)
        hidden(0, 0)
        quant("x", 3)
        dense_1(3, 0)
        hidden(0, 1)
        dense_1(3, 1)
        square(2, 0)
        widen_x(320, S)
        square(2, 1)
        add_squares(2, G)
        widen_x(320, G)
        inverse_root(1, 2)
        gain(1)
        square(3, 0)
        widen_x(64, S)
        square(3, 1)
        add_squares(3, G)
        inverse_root(2)
        widen_x(480, S)
        widen_x(GPSIMD_COLS, G)
        gain(2)

        for c in range(4, 29):
            scale_x(c)
            if c > 4:
                turn_x(c + 1)
            hidden(c - 3, 0)
            quant("x", c)
            if c >= 4:
                quant("h", c - 4)
            dense_1(c, 0)
            hidden(c - 3, 1)
            dense_1(c, 1)
            square(c, 0)
            widen_x(SCALAR_COLS, S)
            square(c, 1)
            add_squares(c, G)
            widen_x(GPSIMD_COLS, G)
            inverse_root(c - 1)
            if c >= 4:
                dense_2(c - 4)
                emit_y(c - 4)
                if c % 4 == 3:
                    store_y(c - 7, 4)
            gain(c - 1)

        scale_x(29)
        turn_x(30)
        stage_for(("h", 26), ("h", 27))
        hidden(26, 0)
        quant("x", 29)
        dense_1(29, 0)
        hidden(26, 1)
        dense_1(29, 1)
        square(29, 0)
        widen_x(D, S)
        turn_x(31, "y")
        square(29, 1)
        scale_x(30)
        quant("h", 25)
        quant("x", 30)
        add_squares(29, G)
        inverse_root(28, 2)
        gain(28)
        hidden(27, 0)
        dense_1(30, 0, "xt")
        dense_1(30, 1, "r0")
        scale_x(31)
        hidden(27, 1)
        quant("x", 31)
        dense_1(31, 0, "y")
        dense_1(31, 1, "i0")
        quant("h", 26, 2)
        square(30, 0)
        square(30, 1)
        add_squares(30, G)
        stage_for(("h", 28), ("h", 29))
        hidden(28, 0)
        hidden(28, 1)
        inverse_root(29, 2)
        gain(29)
        square(31, 0)
        square(31, 1)
        hidden(29, 0)
        dense_2(25, "r2")
        hidden(29, 1)
        dense_2(26, "i2")
        add_squares(31, V)
        quant("h", 28, 2)
        dense_2(28, "r1")
        dense_2(27, "i1")
        inverse_root(30, 2)
        gain(30)
        inverse_root(31, 2)
        gain(31)
        emit_y(25)
        emit_y(26)
        hidden(30, 0)
        hidden(30, 1)
        dense_2(29, "r0")
        emit_y(27)
        store_y(24, 4)
        emit_y(28)
        emit_y(29)
        store_y(28, 2)
        hidden(31, 0)
        quant("h", 30)
        hidden(31, 1)
        dense_2(30, "xt")
        quant("h", 31, 1, range(0, 1))
        quant("h", 31, 1, range(1, 2))
        emit_y(30)
        store_y(30, 1)
        last_y(31, ("r2", "i2"))
